import numpy as np
import ml_dtypes


def mxq(x, axis, fmt="e4m3"):
    dtype, down = {"e4m3": (ml_dtypes.float8_e4m3fn, 7), "e5m2": (ml_dtypes.float8_e5m2, 14)}[fmt]
    v = np.moveaxis(np.asarray(x, np.float32).astype(ml_dtypes.bfloat16).astype(np.float64), axis, -1)
    blocks = v.reshape(v.shape[:-1] + (-1, 32))
    amax = np.abs(blocks).max(-1, keepdims=True)
    byte = np.maximum(np.where(amax > 0, np.frexp(amax)[1] - 1 + 127, 0) - down, 1)
    scale = np.exp2(byte - 127.0)
    codes = (blocks / scale).astype(np.float32).astype(dtype).astype(np.float64)
    return np.moveaxis((codes * scale).reshape(v.shape), -1, axis)


WIDE = False


def mx_kscale(k):
    if not WIDE:
        return np.ones(k)
    levels = np.array([18, -18])
    if k % 512:
        return np.exp2(np.random.permutation(np.resize(levels, k // 32))).repeat(32)
    a = np.empty((k // 512, 16))
    for p in range(k // 512):
        a[p, :8] = np.random.permutation(np.resize(levels, 8))
        for g in range(8):
            far = levels[np.abs(levels - a[p, g]) >= 10]
            a[p, g + 8] = far[np.random.randint(len(far))]
    return np.exp2(a.ravel()).repeat(32)


def f64(x):
    return np.asarray(x).astype(np.float64)


def striped(idx):
    return np.tile(np.asarray(idx).reshape(-1, 16).T, (8, 1)).astype(np.uint16)


def unstriped(offs):
    return offs[:16].T.reshape(-1).astype(np.int64)


B, N, T, D, DV, R = 1, 512, 2048, 512, 512, 512
PAGE = 32


def setup_inputs():
    n = np.random.standard_normal
    pages = np.random.permutation(T // PAGE)[:B * N // PAGE]
    idx = (pages[:, None] * PAGE + np.arange(PAGE)[None, :]).reshape(-1)
    s = mx_kscale(D)[:, None]
    z = mx_kscale(R)[:, None]
    v = mx_kscale(DV)[:, None]
    q = n((B, D, R))
    do = n((B, DV, R))
    return {
        "qT": (q * s).astype(np.float32),
        "kT": (n((D, T)) * (1.00 / np.sqrt(D)) / s).astype(np.float32),
        "vT": (n((DV, T)) / np.sqrt(DV) / v).astype(np.float32),
        "doT": (do * v).astype(np.float32),
        "rw": (np.random.uniform(0.5, 1.5, (B, R, 1)) * 1.0 / np.sqrt(R) * z).astype(np.float32),
        "qm": (q.transpose(0, 2, 1) / z).astype(np.float32),
        "dom": (do.transpose(0, 2, 1) / z).astype(np.float32),
        "offs": striped(idx),
    }


def reference(qT, kT, vT, doT, rw, qm, dom, offs):
    idx = unstriped(offs)
    pick = lambda x: x[:, idx].reshape(x.shape[0], B, N).transpose(1, 0, 2)
    a = mxq(f64(qT), 1, "e4m3").transpose(0, 2, 1) @ mxq(pick(f64(kT)), 1, "e4m3")
    p = 1.0 / (1.0 + np.exp(-a))
    dp = mxq(f64(doT), 1, "e5m2").transpose(0, 2, 1) @ mxq(pick(f64(vT)), 1, "e4m3")
    ds = f64(rw) * dp * p * (1.0 - p)
    dk = mxq(f64(qm), 1, "e4m3").transpose(0, 2, 1) @ mxq(ds, 1, "e5m2")
    dv = mxq(f64(dom), 1, "e5m2").transpose(0, 2, 1) @ mxq(f64(rw) * p, 1, "e4m3")
    gk = np.zeros((D, T))
    gk[:, idx] = dk.transpose(1, 0, 2).reshape(D, B * N)
    gv = np.zeros((DV, T))
    gv[:, idx] = dv.transpose(1, 0, 2).reshape(DV, B * N)
    return gk, gv

@@ -1,0 +1,149 @@
+from contextlib import ExitStack
+
+import concourse.mybir as mybir
+
+N, T, D, DV, R = 512, 2048, 512, 512, 512
+FLOPS = 2 * R * N * (2 * D + 2 * DV)
+
+F32 = mybir.dt.float32
+BF16 = mybir.dt.bfloat16
+U32 = mybir.dt.uint32
+U16 = mybir.dt.uint16
+U8 = mybir.dt.uint8
+E4M3 = mybir.dt.float8_e4m3fn_x4
+E5M2 = mybir.dt.float8_e5m2_x4
+ACT = mybir.ActivationFunctionType
+MULT = mybir.AluOpType.mult
+
+P = 128
+PACK = 4
+WINDOWS = 6
+
+
+def tile_attend_gat_sig_kv_kernel(tc, qT, kT, vT, doT, rw, qm, dom, offs, out_0, out_1):
+    nc = tc.nc
+    with ExitStack() as ctx:
+        held = ctx.enter_context(tc.tile_pool(name="held", bufs=1))
+        woven_pool = ctx.enter_context(tc.tile_pool(name="woven", bufs=5))
+        staged_pool = ctx.enter_context(tc.tile_pool(name="staged", bufs=4))
+        psum = ctx.enter_context(tc.psum_pool(name="psum", bufs=4))
+
+        offsets = held.tile([P, N // 16], U16, name="offsets")
+        nc.sync.dma_start(offsets[:], offs)
+        gate = held.tile([P, PACK], F32, name="gate")
+        nc.sync.dma_start(gate[:], rw[0].rearrange("(p j) o -> p (j o)", j=PACK))
+
+        def load_rows(name, src):
+            raw = held.tile([P, PACK, 512], F32, name=name + "_raw")
+            nc.sync.dma_start(raw[:], src[0].rearrange("(p t) c -> p t c", t=PACK))
+            return raw
+
+        def load_plane(name, pool, t):
+            plane = held.tile([P, T], F32, name="%s_plane%d" % (name, t))
+            nc.sync.dma_start(plane[:], pool.rearrange("(p t) c -> t p c", t=PACK)[t])
+            return plane
+
+        q_raw = load_rows("q", qT)
+        dom_raw = load_rows("dom", dom)
+        k_planes = [load_plane("k", kT, t) for t in range(PACK)]
+        v_planes = [load_plane("v", vT, t) for t in range(PACK - 1)]
+        do_raw = load_rows("do", doT)
+        v_planes.append(load_plane("v", vT, PACK - 1))
+        qm_raw = load_rows("qm", qm)
+
+        warm = held.tile([P, 1], F32, name="warm")
+        warm_out = held.tile([P, 1], F32, name="warm_out")
+        nc.gpsimd.memset(warm[:], 0.0)
+        nc.scalar.activation(warm_out[:], warm[:], ACT.Sigmoid)
+
+        windows = []
+        for w in range(WINDOWS):
+            window = held.tile([P, T], F32, name="window%d" % w)
+            nc.vector.memset(window[:], 0.0)
+            windows.append(window)
+
+        def new_woven(name):
+            return woven_pool.tile([P, 512, PACK], BF16, name=name, tag="woven", align_bytes=64)
+
+        def quantise(name, woven, fmt):
+            codes = held.tile([P, 512], U32, name=name + "_codes", align_bytes=64)
+            scales = held.tile([P, 512], U8, name=name + "_scales", align_bytes=64)
+            nc.vector.quantize_mx(out=codes[:].bitcast(fmt), scales=scales[:], in_=woven[:].rearrange("p c t -> p (c t)"))
+            return codes, scales, fmt
+
+        def weave_dealt(name, raw):
+            woven = new_woven(name + "_woven")
+            nc.scalar.copy(
+                woven[:].rearrange("p (j s) t -> p s t j", j=PACK),
+                raw[:].rearrange("p t (s j) -> p s t j", j=PACK),
+            )
+            return woven
+
+        def weave(name, raw, copy):
+            woven = new_woven(name + "_woven")
+            copy(
+                woven[:].rearrange("p (c i) t -> p c t i", i=PACK),
+                raw[:].rearrange("p t (c i) -> p c t i", i=PACK),
+            )
+            return woven
+
+        def gather(name, planes):
+            woven = new_woven(name + "_woven")
+            for t in range(PACK):
+                nc.vector.tensor_copy(woven[:, :, t], planes[t][:].indirect(offsets[:]))
+            return woven
+
+        def product(name, tag, stationary, moving, m):
+            bank = psum.tile([P, N], F32, name="%s%d" % (name, m), tag=tag)
+            cols = slice(m * P, (m + 1) * P)
+            nc.tensor.matmul_mx(
+                out=bank[:],
+                lhsT=stationary[0][:, cols].bitcast(stationary[2]),
+                lhsT_scale=stationary[1][:, cols],
+                rhs=moving[0][:].bitcast(moving[2]),
+                rhs_scale=moving[1][:],
+                start=True,
+                stop=True,
+            )
+            return bank
+
+        def put(bank, window, rows):
+            staged = staged_pool.tile([P, N], F32, name="staged")
+            nc.scalar.copy(staged[:], bank[:])
+            nc.vector.tensor_copy(window[:].indirect(offsets[:]), staged[:])
+            nc.sync.dma_start(rows, window[:])
+
+        q_mx = quantise("q", weave_dealt("q", q_raw), E4M3)
+        dom_mx = quantise("dom", weave("dom", dom_raw, nc.scalar.copy), E5M2)
+        k_mx = quantise("k", gather("k", k_planes), E4M3)
+
+        scores = [product("score", "front", q_mx, k_mx, j) for j in range(PACK)]
+        prob = held.tile([P, PACK, N], F32, name="prob")
+        rest = held.tile([P, PACK, N], F32, name="rest")
+        pw_woven = new_woven("pw_woven")
+        for j in range(PACK):
+            nc.scalar.activation(prob[:, j, :], scores[j][:], ACT.Sigmoid)
+            nc.vector.tensor_scalar(pw_woven[:, :, j], prob[:, j, :], gate[:, j : j + 1], None, MULT)
+        pw_mx = quantise("pw", pw_woven, E4M3)
+        for j in range(PACK):
+            nc.scalar.activation(rest[:, j, :], scores[j][:], ACT.Sigmoid, scale=-1.0)
+
+        for m in range(DV // P):
+            put(product("dv", "back", dom_mx, pw_mx, m), windows[m], out_1[m * P : (m + 1) * P, :])
+
+        slope = held.tile([P, PACK, N], F32, name="slope")
+        for j in range(PACK):
+            nc.vector.scalar_tensor_tensor(slope[:, j, :], prob[:, j, :], gate[:, j : j + 1], rest[:, j, :], MULT, MULT)
+
+        do_mx = quantise("do", weave_dealt("do", do_raw), E5M2)
+        v_mx = quantise("v", gather("v", v_planes), E4M3)
+        ds_rows = held.tile([P, PACK, N], BF16, name="ds_rows")
+        for j in range(PACK):
+            dp = product("dp", "front", do_mx, v_mx, j)
+            nc.vector.tensor_tensor(ds_rows[:, j, :], dp[:], slope[:, j, :], MULT)
+        ds_mx = quantise("ds", weave("ds", ds_rows, nc.vector.tensor_copy), E5M2)
+        qm_mx = quantise("qm", weave("qm", qm_raw, nc.scalar.copy), E4M3)
+
+        for m in range(D // P):
+            window = windows[(DV // P + m) % WINDOWS]
+            put(product("dk", "back", qm_mx, ds_mx, m), window, out_0[m * P : (m + 1) * P, :])

@@ -7,6 +7,7 @@ FLOPS = 2 * R * N * (2 * D + 2 * DV)
 
 F32 = mybir.dt.float32
 BF16 = mybir.dt.bfloat16
+I32 = mybir.dt.int32
 U32 = mybir.dt.uint32
 U16 = mybir.dt.uint16
 U8 = mybir.dt.uint8
@@ -17,7 +18,7 @@ MULT = mybir.AluOpType.mult
 
 P = 128
 PACK = 4
-WINDOWS = 6
+WINDOWS = 4
 
 
 def tile_attend_gat_sig_kv_kernel(tc, qT, kT, vT, doT, rw, qm, dom, offs, out_0, out_1):
@@ -39,16 +40,16 @@ def tile_attend_gat_sig_kv_kernel(tc, qT, kT, vT, doT, rw, qm, dom, offs, out_0,
             return raw
 
         def load_plane(name, pool, t):
-            plane = held.tile([P, T], F32, name="%s_plane%d" % (name, t))
+            plane = held.tile([P, T], F32, name="%s_plane%d" % (name, t), tag="%s_plane%d" % (name, t))
             nc.sync.dma_start(plane[:], pool.rearrange("(p t) c -> t p c", t=PACK)[t])
             return plane
 
         q_raw = load_rows("q", qT)
-        dom_raw = load_rows("dom", dom)
         k_planes = [load_plane("k", kT, t) for t in range(PACK)]
-        v_planes = [load_plane("v", vT, t) for t in range(PACK - 1)]
+        dom_raw = load_rows("dom", dom)
+        v_planes = [load_plane("v", vT, t) for t in range(2)]
         do_raw = load_rows("do", doT)
-        v_planes.append(load_plane("v", vT, PACK - 1))
+        v_planes.extend([load_plane("v", vT, t) for t in range(2, PACK)])
         qm_raw = load_rows("qm", qm)
 
         warm = held.tile([P, 1], F32, name="warm")
@@ -59,7 +60,8 @@ def tile_attend_gat_sig_kv_kernel(tc, qT, kT, vT, doT, rw, qm, dom, offs, out_0,
         windows = []
         for w in range(WINDOWS):
             window = held.tile([P, T], F32, name="window%d" % w)
-            nc.vector.memset(window[:], 0.0)
+            engine = nc.vector if w % 2 == 0 else nc.gpsimd
+            engine.memset(window[:].bitcast(I32), 0)
             windows.append(window)
 
         def new_woven(name):
@@ -107,43 +109,56 @@ def tile_attend_gat_sig_kv_kernel(tc, qT, kT, vT, doT, rw, qm, dom, offs, out_0,
             )
             return bank
 
-        def put(bank, window, rows):
-            staged = staged_pool.tile([P, N], F32, name="staged")
+        def put(bank, window, rows, staged):
             nc.scalar.copy(staged[:], bank[:])
             nc.vector.tensor_copy(window[:].indirect(offsets[:]), staged[:])
             nc.sync.dma_start(rows, window[:])
 
+        def block(out, m):
+            return out[m * P : (m + 1) * P, :]
+
+        def new_staged(name):
+            return staged_pool.tile([P, N], F32, name=name, tag="staged")
+
         q_mx = quantise("q", weave_dealt("q", q_raw), E4M3)
-        dom_mx = quantise("dom", weave("dom", dom_raw, nc.scalar.copy), E5M2)
         k_mx = quantise("k", gather("k", k_planes), E4M3)
+        dom_mx = quantise("dom", weave("dom", dom_raw, nc.vector.tensor_copy), E5M2)
 
         scores = [product("score", "front", q_mx, k_mx, j) for j in range(PACK)]
         prob = held.tile([P, PACK, N], F32, name="prob")
         rest = held.tile([P, PACK, N], F32, name="rest")
-        pw_woven = new_woven("pw_woven")
+        pw_rows = held.tile([P, PACK, N], F32, name="pw_rows")
         for j in range(PACK):
             nc.scalar.activation(prob[:, j, :], scores[j][:], ACT.Sigmoid)
-            nc.vector.tensor_scalar(pw_woven[:, :, j], prob[:, j, :], gate[:, j : j + 1], None, MULT)
-        pw_mx = quantise("pw", pw_woven, E4M3)
+            nc.vector.tensor_scalar(pw_rows[:, j, :], prob[:, j, :], gate[:, j : j + 1], None, MULT)
+        pw_mx = quantise("pw", weave("pw", pw_rows, nc.vector.tensor_copy), E4M3)
+        dv = [product("dv", "back", dom_mx, pw_mx, m) for m in range(DV // P)]
+        put(dv[0], windows[0], block(out_1, 0), new_staged("dv0_staged"))
         for j in range(PACK):
             nc.scalar.activation(rest[:, j, :], scores[j][:], ACT.Sigmoid, scale=-1.0)
 
-        for m in range(DV // P):
-            put(product("dv", "back", dom_mx, pw_mx, m), windows[m], out_1[m * P : (m + 1) * P, :])
-
-        slope = held.tile([P, PACK, N], F32, name="slope")
+        slopes = []
         for j in range(PACK):
-            nc.vector.scalar_tensor_tensor(slope[:, j, :], prob[:, j, :], gate[:, j : j + 1], rest[:, j, :], MULT, MULT)
+            slope = held.tile([P, N], F32, name="slope%d" % j, tag="slope%d" % j)
+            nc.vector.tensor_tensor(slope[:], pw_rows[:, j, :], rest[:, j, :], MULT)
+            slopes.append(slope)
 
         do_mx = quantise("do", weave_dealt("do", do_raw), E5M2)
-        v_mx = quantise("v", gather("v", v_planes), E4M3)
-        ds_rows = held.tile([P, PACK, N], BF16, name="ds_rows")
+        v_rows = held.tile([P, PACK, N], BF16, name="v_rows")
+        for t in range(PACK):
+            nc.vector.tensor_copy(v_rows[:, t, :], v_planes[t][:].indirect(offsets[:]))
+        put(dv[1], windows[1], block(out_1, 1), held.tile([P, N], F32, name="dv1_staged", tag="v_plane3"))
+        v_mx = quantise("v", weave("v", v_rows, nc.scalar.copy), E4M3)
+        qm_woven = weave("qm", qm_raw, nc.scalar.copy)
+
+        ds_rows = held.tile([P, PACK, N], BF16, name="ds_rows", tag="ds_rows")
         for j in range(PACK):
             dp = product("dp", "front", do_mx, v_mx, j)
-            nc.vector.tensor_tensor(ds_rows[:, j, :], dp[:], slope[:, j, :], MULT)
-        ds_mx = quantise("ds", weave("ds", ds_rows, nc.vector.tensor_copy), E5M2)
-        qm_mx = quantise("qm", weave("qm", qm_raw, nc.scalar.copy), E4M3)
+            nc.vector.tensor_tensor(ds_rows[:, j, :], dp[:], slopes[j][:], MULT)
+        qm_mx = quantise("qm", qm_woven, E4M3)
+        put(dv[2], windows[2], block(out_1, 2), held.tile([P, N], F32, name="dv2_staged", tag="slope1"))
+        ds_mx = quantise("ds", weave("ds", ds_rows, nc.scalar.copy), E5M2)
+        put(dv[3], windows[3], block(out_1, 3), held.tile([P, N], F32, name="dv3_staged", tag="ds_rows"))
 
         for m in range(D // P):
-            window = windows[(DV // P + m) % WINDOWS]
-            put(product("dk", "back", qm_mx, ds_mx, m), window, out_0[m * P : (m + 1) * P, :])
+            put(product("dk", "front", qm_mx, ds_mx, m), windows[m], block(out_0, m), new_staged("dk%d_staged" % m))

@@ -15,47 +15,49 @@ E4M3 = mybir.dt.float8_e4m3fn_x4
 E5M2 = mybir.dt.float8_e5m2_x4
 ACT = mybir.ActivationFunctionType
 MULT = mybir.AluOpType.mult
+SUBTRACT = mybir.AluOpType.subtract
 
 P = 128
 PACK = 4
-WINDOWS = 4
+ALIGN = 64
+BLOCKS = DV // P
+WINDOWS = BLOCKS + 1
+VECTOR_SHARE = 320
+HALF = DV // 2
 
 
 def tile_attend_gat_sig_kv_kernel(tc, qT, kT, vT, doT, rw, qm, dom, offs, out_0, out_1):
     nc = tc.nc
     with ExitStack() as ctx:
         held = ctx.enter_context(tc.tile_pool(name="held", bufs=1))
-        woven_pool = ctx.enter_context(tc.tile_pool(name="woven", bufs=5))
-        staged_pool = ctx.enter_context(tc.tile_pool(name="staged", bufs=4))
-        psum = ctx.enter_context(tc.psum_pool(name="psum", bufs=4))
-
-        offsets = held.tile([P, N // 16], U16, name="offsets")
-        nc.sync.dma_start(offsets[:], offs)
-        gate = held.tile([P, PACK], F32, name="gate")
-        nc.sync.dma_start(gate[:], rw[0].rearrange("(p j) o -> p (j o)", j=PACK))
+        late = ctx.enter_context(tc.tile_pool(name="late", bufs=1))
+        psum = ctx.enter_context(tc.psum_pool(name="psum", bufs=PACK))
 
         def load_rows(name, src):
-            raw = held.tile([P, PACK, 512], F32, name=name + "_raw")
-            nc.sync.dma_start(raw[:], src[0].rearrange("(p t) c -> p t c", t=PACK))
-            return raw
+            rows = held.tile([P, PACK, src.shape[1]], F32, name=name + "_rows")
+            nc.sync.dma_start(rows[:], src.rearrange("(p t) c -> p t c", t=PACK))
+            return rows
 
-        def load_plane(name, pool, t):
-            plane = held.tile([P, T], F32, name="%s_plane%d" % (name, t), tag="%s_plane%d" % (name, t))
-            nc.sync.dma_start(plane[:], pool.rearrange("(p t) c -> t p c", t=PACK)[t])
+        def load_plane(plane, table, t):
+            nc.sync.dma_start(plane[:], table.rearrange("(p t) c -> t p c", t=PACK)[t])
             return plane
 
-        q_raw = load_rows("q", qT)
-        k_planes = [load_plane("k", kT, t) for t in range(PACK)]
-        dom_raw = load_rows("dom", dom)
-        v_planes = [load_plane("v", vT, t) for t in range(2)]
-        do_raw = load_rows("do", doT)
-        v_planes.extend([load_plane("v", vT, t) for t in range(2, PACK)])
-        qm_raw = load_rows("qm", qm)
+        def new_plane(name, t):
+            return held.tile([P, T], F32, name="%s_plane%d" % (name, t))
 
-        warm = held.tile([P, 1], F32, name="warm")
-        warm_out = held.tile([P, 1], F32, name="warm_out")
-        nc.gpsimd.memset(warm[:], 0.0)
-        nc.scalar.activation(warm_out[:], warm[:], ACT.Sigmoid)
+        q_rows = load_rows("q", qT[0])
+        offsets = held.tile([P, N // 16], U16, name="offsets")
+        nc.sync.dma_start(offsets[:], offs)
+        k_planes = [load_plane(new_plane("k", t), kT, t) for t in range(PACK)]
+        gate = held.tile([P, PACK], F32, name="gate")
+        nc.sync.dma_start(gate[:], rw[0].rearrange("(p j) o -> p (j o)", j=PACK))
+        dom_early_rows = load_rows("dom_early", dom[0][:, :HALF])
+        v_planes = [load_plane(new_plane("v", t), vT, t) for t in range(PACK - 1)]
+        do_rows = load_rows("do", doT[0])
+        v_last_plane = late.tile([P, T], F32, name="v_last_plane", offset=0, align_bytes=ALIGN)
+        v_planes.append(load_plane(v_last_plane, vT, PACK - 1))
+        dom_late_rows = load_rows("dom_late", dom[0][:, HALF:])
+        qm_rows = load_rows("qm", qm[0])
 
         windows = []
         for w in range(WINDOWS):
@@ -64,35 +66,40 @@ def tile_attend_gat_sig_kv_kernel(tc, qT, kT, vT, doT, rw, qm, dom, offs, out_0,
             engine.memset(window[:].bitcast(I32), 0)
             windows.append(window)
 
-        def new_woven(name):
-            return woven_pool.tile([P, 512, PACK], BF16, name=name, tag="woven", align_bytes=64)
+        def new_woven(name, width=N):
+            return held.tile([P, width, PACK], BF16, name=name + "_woven", align_bytes=ALIGN)
 
         def quantise(name, woven, fmt):
-            codes = held.tile([P, 512], U32, name=name + "_codes", align_bytes=64)
-            scales = held.tile([P, 512], U8, name=name + "_scales", align_bytes=64)
-            nc.vector.quantize_mx(out=codes[:].bitcast(fmt), scales=scales[:], in_=woven[:].rearrange("p c t -> p (c t)"))
-            return codes, scales, fmt
+            width = woven.shape[1]
+            words = held.tile([P, width], U32, name=name + "_words", align_bytes=ALIGN)
+            scales = held.tile([P, width], U8, name=name + "_scales", align_bytes=ALIGN)
+            nc.vector.quantize_mx(out=words[:].bitcast(fmt), scales=scales[:], in_=woven[:].rearrange("p c t -> p (c t)"))
+            return words, scales, fmt
 
-        def weave_dealt(name, raw):
-            woven = new_woven(name + "_woven")
+        def weave_dealt(name, rows):
+            woven = new_woven(name)
             nc.scalar.copy(
                 woven[:].rearrange("p (j s) t -> p s t j", j=PACK),
-                raw[:].rearrange("p t (s j) -> p s t j", j=PACK),
+                rows[:].rearrange("p t (s j) -> p s t j", j=PACK),
             )
             return woven
 
-        def weave(name, raw, copy):
-            woven = new_woven(name + "_woven")
+        def weave_columns(woven, rows, copy, cols):
             copy(
-                woven[:].rearrange("p (c i) t -> p c t i", i=PACK),
-                raw[:].rearrange("p t (c i) -> p c t i", i=PACK),
+                woven[:, cols, :].rearrange("p (c i) t -> p c t i", i=PACK),
+                rows[:, :, cols].rearrange("p t (c i) -> p c t i", i=PACK),
             )
+
+        def weave(name, rows, copy):
+            width = rows.shape[2]
+            woven = new_woven(name, width)
+            weave_columns(woven, rows, copy, slice(0, width))
             return woven
 
-        def gather(name, planes):
-            woven = new_woven(name + "_woven")
-            for t in range(PACK):
-                nc.vector.tensor_copy(woven[:, :, t], planes[t][:].indirect(offsets[:]))
+        def weave_shared(name, rows):
+            woven = new_woven(name)
+            weave_columns(woven, rows, nc.vector.tensor_copy, slice(0, VECTOR_SHARE))
+            weave_columns(woven, rows, nc.scalar.copy, slice(VECTOR_SHARE, N))
             return woven
 
         def product(name, tag, stationary, moving, m):
@@ -109,56 +116,59 @@ def tile_attend_gat_sig_kv_kernel(tc, qT, kT, vT, doT, rw, qm, dom, offs, out_0,
             )
             return bank
 
-        def put(bank, window, rows, staged):
+        def put(bank, staged, window, out, m):
             nc.scalar.copy(staged[:], bank[:])
             nc.vector.tensor_copy(window[:].indirect(offsets[:]), staged[:])
-            nc.sync.dma_start(rows, window[:])
+            nc.sync.dma_start(out[m * P : (m + 1) * P, :], window[:])
 
-        def block(out, m):
-            return out[m * P : (m + 1) * P, :]
-
-        def new_staged(name):
-            return staged_pool.tile([P, N], F32, name=name, tag="staged")
-
-        q_mx = quantise("q", weave_dealt("q", q_raw), E4M3)
-        k_mx = quantise("k", gather("k", k_planes), E4M3)
-        dom_mx = quantise("dom", weave("dom", dom_raw, nc.vector.tensor_copy), E5M2)
-
+        q_mx = quantise("q", weave_dealt("q", q_rows), E4M3)
+        k_woven = new_woven("k")
+        for t in range(PACK):
+            nc.vector.tensor_copy(k_woven[:, :, t], k_planes[t][:].indirect(offsets[:]))
+        k_mx = quantise("k", k_woven, E4M3)
+        dom_early_mx = quantise("dom_early", weave("dom_early", dom_early_rows, nc.vector.tensor_copy), E5M2)
         scores = [product("score", "front", q_mx, k_mx, j) for j in range(PACK)]
+
         prob = held.tile([P, PACK, N], F32, name="prob")
-        rest = held.tile([P, PACK, N], F32, name="rest")
         pw_rows = held.tile([P, PACK, N], F32, name="pw_rows")
         for j in range(PACK):
             nc.scalar.activation(prob[:, j, :], scores[j][:], ACT.Sigmoid)
-            nc.vector.tensor_scalar(pw_rows[:, j, :], prob[:, j, :], gate[:, j : j + 1], None, MULT)
-        pw_mx = quantise("pw", weave("pw", pw_rows, nc.vector.tensor_copy), E4M3)
-        dv = [product("dv", "back", dom_mx, pw_mx, m) for m in range(DV // P)]
-        put(dv[0], windows[0], block(out_1, 0), new_staged("dv0_staged"))
         for j in range(PACK):
-            nc.scalar.activation(rest[:, j, :], scores[j][:], ACT.Sigmoid, scale=-1.0)
+            nc.scalar.activation(pw_rows[:, j, :], prob[:, j, :], ACT.Copy, scale=gate[:, j : j + 1])
+        pw_mx = quantise("pw", weave_shared("pw", pw_rows), E4M3)
+        dv_early = [product("dv_early", "back", dom_early_mx, pw_mx, m) for m in range(HALF // P)]
 
-        slopes = []
+        minus_slopes = []
         for j in range(PACK):
-            slope = held.tile([P, N], F32, name="slope%d" % j, tag="slope%d" % j)
-            nc.vector.tensor_tensor(slope[:], pw_rows[:, j, :], rest[:, j, :], MULT)
-            slopes.append(slope)
+            minus_slope = held.tile([P, N], F32, name="minus_slope%d" % j, tag="minus_slope%d" % j)
+            nc.vector.scalar_tensor_tensor(minus_slope[:], prob[:, j, :], 1.0, pw_rows[:, j, :], SUBTRACT, MULT)
+            minus_slopes.append(minus_slope)
 
-        do_mx = quantise("do", weave_dealt("do", do_raw), E5M2)
+        do_mx = quantise("do", weave_dealt("do", do_rows), E5M2)
         v_rows = held.tile([P, PACK, N], BF16, name="v_rows")
         for t in range(PACK):
             nc.vector.tensor_copy(v_rows[:, t, :], v_planes[t][:].indirect(offsets[:]))
-        put(dv[1], windows[1], block(out_1, 1), held.tile([P, N], F32, name="dv1_staged", tag="v_plane3"))
-        v_mx = quantise("v", weave("v", v_rows, nc.scalar.copy), E4M3)
-        qm_woven = weave("qm", qm_raw, nc.scalar.copy)
+        v_mx = quantise("v", weave_shared("v", v_rows), E4M3)
+
+        for m in range(HALF // P):
+            staged = late.tile([P, N], F32, name="dv%d_staged" % m, offset=m * N * 4, align_bytes=ALIGN)
+            put(dv_early[m], staged, windows[m], out_1, m)
+        dom_late_mx = quantise("dom_late", weave("dom_late", dom_late_rows, nc.scalar.copy), E5M2)
+        dv_late = [product("dv_late", "back", dom_late_mx, pw_mx, m) for m in range(HALF // P)]
+        qm_woven = weave("qm", qm_rows, nc.scalar.copy)
 
         ds_rows = held.tile([P, PACK, N], BF16, name="ds_rows", tag="ds_rows")
         for j in range(PACK):
             dp = product("dp", "front", do_mx, v_mx, j)
-            nc.vector.tensor_tensor(ds_rows[:, j, :], dp[:], slopes[j][:], MULT)
+            nc.vector.scalar_tensor_tensor(ds_rows[:, j, :], dp[:], -1.0, minus_slopes[j][:], MULT, MULT)
+        staged = held.tile([P, N], F32, name="dv2_staged", tag="minus_slope0")
+        put(dv_late[0], staged, windows[2], out_1, 2)
         qm_mx = quantise("qm", qm_woven, E4M3)
-        put(dv[2], windows[2], block(out_1, 2), held.tile([P, N], F32, name="dv2_staged", tag="slope1"))
-        ds_mx = quantise("ds", weave("ds", ds_rows, nc.scalar.copy), E5M2)
-        put(dv[3], windows[3], block(out_1, 3), held.tile([P, N], F32, name="dv3_staged", tag="ds_rows"))
+        ds_mx = quantise("ds", weave_shared("ds", ds_rows), E5M2)
+        staged = held.tile([P, N], F32, name="dv3_staged", tag="ds_rows")
+        put(dv_late[1], staged, windows[3], out_1, 3)
 
-        for m in range(D // P):
-            put(product("dk", "front", qm_mx, ds_mx, m), windows[m], block(out_0, m), new_staged("dk%d_staged" % m))
+        for m in range(BLOCKS):
+            bank = product("dk", "front", qm_mx, ds_mx, m)
+            staged = held.tile([P, N], F32, name="dk%d_staged" % m)
+            put(bank, staged, windows[(BLOCKS + m) % WINDOWS], out_0, m)

@@ -22,8 +22,12 @@ PACK = 4
 ALIGN = 64
 BLOCKS = DV // P
 WINDOWS = BLOCKS + 1
-VECTOR_SHARE = 320
-HALF = DV // 2
+PW_SHARE = 128
+V_SHARE = 384
+DS_SHARE = 320
+PLANE_BYTES = T * 4
+ROWS_BYTES = PACK * N * 2
+STAGED_BYTES = N * 4
 
 
 def tile_attend_gat_sig_kv_kernel(tc, qT, kT, vT, doT, rw, qm, dom, offs, out_0, out_1):
@@ -33,30 +37,36 @@ def tile_attend_gat_sig_kv_kernel(tc, qT, kT, vT, doT, rw, qm, dom, offs, out_0,
         late = ctx.enter_context(tc.tile_pool(name="late", bufs=1))
         psum = ctx.enter_context(tc.psum_pool(name="psum", bufs=PACK))
 
+        at_v3 = 0
+        at_v = PLANE_BYTES
+        at_ds = at_v + ROWS_BYTES
+
+        def new_tile(name, shape, dtype, at=None):
+            if at is None:
+                return held.tile(shape, dtype, name=name, align_bytes=ALIGN)
+            return late.tile(shape, dtype, name=name, offset=at, align_bytes=ALIGN)
+
         def load_rows(name, src):
-            rows = held.tile([P, PACK, src.shape[1]], F32, name=name + "_rows")
+            rows = new_tile(name + "_rows", [P, PACK, src.shape[1]], F32)
             nc.sync.dma_start(rows[:], src.rearrange("(p t) c -> p t c", t=PACK))
             return rows
 
-        def load_plane(plane, table, t):
+        def load_plane(name, table, t, at=None):
+            plane = new_tile("%s_plane%d" % (name, t), [P, T], F32, at)
             nc.sync.dma_start(plane[:], table.rearrange("(p t) c -> t p c", t=PACK)[t])
             return plane
 
-        def new_plane(name, t):
-            return held.tile([P, T], F32, name="%s_plane%d" % (name, t))
-
-        q_rows = load_rows("q", qT[0])
+        k_planes = [load_plane("k", kT, 0)]
         offsets = held.tile([P, N // 16], U16, name="offsets")
         nc.sync.dma_start(offsets[:], offs)
-        k_planes = [load_plane(new_plane("k", t), kT, t) for t in range(PACK)]
         gate = held.tile([P, PACK], F32, name="gate")
         nc.sync.dma_start(gate[:], rw[0].rearrange("(p j) o -> p (j o)", j=PACK))
-        dom_early_rows = load_rows("dom_early", dom[0][:, :HALF])
-        v_planes = [load_plane(new_plane("v", t), vT, t) for t in range(PACK - 1)]
+        k_planes.extend(load_plane("k", kT, t) for t in range(1, PACK))
+        q_rows = load_rows("q", qT[0])
+        v_planes = [load_plane("v", vT, 0)]
+        dom_rows = load_rows("dom", dom[0])
+        v_planes.extend(load_plane("v", vT, t, at) for t, at in ((1, None), (2, None), (3, at_v3)))
         do_rows = load_rows("do", doT[0])
-        v_last_plane = late.tile([P, T], F32, name="v_last_plane", offset=0, align_bytes=ALIGN)
-        v_planes.append(load_plane(v_last_plane, vT, PACK - 1))
-        dom_late_rows = load_rows("dom_late", dom[0][:, HALF:])
         qm_rows = load_rows("qm", qm[0])
 
         windows = []
@@ -65,45 +75,46 @@ def tile_attend_gat_sig_kv_kernel(tc, qT, kT, vT, doT, rw, qm, dom, offs, out_0,
             engine = nc.vector if w % 2 == 0 else nc.gpsimd
             engine.memset(window[:].bitcast(I32), 0)
             windows.append(window)
+        minus_gate = held.tile([P, PACK], F32, name="minus_gate")
+        nc.scalar.activation(minus_gate[:], gate[:], ACT.Copy, scale=-1.0)
 
         def new_woven(name, width=N):
-            return held.tile([P, width, PACK], BF16, name=name + "_woven", align_bytes=ALIGN)
+            return new_tile(name + "_woven", [P, width, PACK], BF16)
 
-        def quantise(name, woven, fmt):
+        def quantise(name, woven, fmt, at=None):
             width = woven.shape[1]
-            words = held.tile([P, width], U32, name=name + "_words", align_bytes=ALIGN)
-            scales = held.tile([P, width], U8, name=name + "_scales", align_bytes=ALIGN)
+            words = new_tile(name + "_words", [P, width], U32, at)
+            scales = new_tile(name + "_scales", [P, width], U8, None if at is None else at + 4 * width)
             nc.vector.quantize_mx(out=words[:].bitcast(fmt), scales=scales[:], in_=woven[:].rearrange("p c t -> p (c t)"))
             return words, scales, fmt
 
-        def weave_dealt(name, rows):
-            woven = new_woven(name)
-            nc.scalar.copy(
-                woven[:].rearrange("p (j s) t -> p s t j", j=PACK),
-                rows[:].rearrange("p t (s j) -> p s t j", j=PACK),
-            )
-            return woven
-
-        def weave_columns(woven, rows, copy, cols):
+        def weave_dealt(name, rows, half, copy):
+            woven = new_woven(name, N // 2)
             copy(
-                woven[:, cols, :].rearrange("p (c i) t -> p c t i", i=PACK),
-                rows[:, :, cols].rearrange("p t (c i) -> p c t i", i=PACK),
+                woven[:].rearrange("p (j s) t -> p s t j", j=2),
+                rows[:].rearrange("p t (s j) -> p s t j", j=PACK)[:, :, :, 2 * half : 2 * half + 2],
+            )
+            return woven
+
+        def weave_columns(woven, rows, copy):
+            copy(
+                woven.rearrange("p (c i) t -> p c t i", i=PACK),
+                rows.rearrange("p t (c i) -> p c t i", i=PACK),
             )
 
-        def weave(name, rows, copy):
-            width = rows.shape[2]
+        def weave(name, rows, first, width):
             woven = new_woven(name, width)
-            weave_columns(woven, rows, copy, slice(0, width))
+            weave_columns(woven[:], rows[:, :, first : first + width], nc.scalar.copy)
             return woven
 
-        def weave_shared(name, rows):
+        def weave_shared(name, rows, share):
             woven = new_woven(name)
-            weave_columns(woven, rows, nc.vector.tensor_copy, slice(0, VECTOR_SHARE))
-            weave_columns(woven, rows, nc.scalar.copy, slice(VECTOR_SHARE, N))
+            weave_columns(woven[:, :share, :], rows[:, :, :share], nc.vector.tensor_copy)
+            weave_columns(woven[:, share:, :], rows[:, :, share:], nc.scalar.copy)
             return woven
 
-        def product(name, tag, stationary, moving, m):
-            bank = psum.tile([P, N], F32, name="%s%d" % (name, m), tag=tag)
+        def product(name, tag, stationary, m, moving):
+            bank = psum.tile([P, N], F32, name=name, tag=tag)
             cols = slice(m * P, (m + 1) * P)
             nc.tensor.matmul_mx(
                 out=bank[:],
@@ -116,59 +127,67 @@ def tile_attend_gat_sig_kv_kernel(tc, qT, kT, vT, doT, rw, qm, dom, offs, out_0,
             )
             return bank
 
-        def put(bank, staged, window, out, m):
+        def put(name, bank, window, out, m, at=None):
+            staged = new_tile(name + "_staged", [P, N], F32, at)
             nc.scalar.copy(staged[:], bank[:])
             nc.vector.tensor_copy(window[:].indirect(offsets[:]), staged[:])
             nc.sync.dma_start(out[m * P : (m + 1) * P, :], window[:])
 
-        q_mx = quantise("q", weave_dealt("q", q_rows), E4M3)
         k_woven = new_woven("k")
         for t in range(PACK):
             nc.vector.tensor_copy(k_woven[:, :, t], k_planes[t][:].indirect(offsets[:]))
         k_mx = quantise("k", k_woven, E4M3)
-        dom_early_mx = quantise("dom_early", weave("dom_early", dom_early_rows, nc.vector.tensor_copy), E5M2)
-        scores = [product("score", "front", q_mx, k_mx, j) for j in range(PACK)]
+        q_woven = [weave_dealt("q%d" % h, q_rows, h, copy) for h, copy in enumerate((nc.vector.tensor_copy, nc.scalar.copy))]
+        q_mx = [quantise("q%d" % h, q_woven[h], E4M3) for h in range(2)]
+        scores = [product("score%d" % j, "front", q_mx[j // 2], j % 2, k_mx) for j in range(PACK)]
 
+        v_rows = new_tile("v_rows", [P, PACK, N], BF16, at_v)
+
+        def gather_values(t):
+            nc.vector.tensor_copy(v_rows[:, t, :], v_planes[t][:].indirect(offsets[:]))
+
+        gather_values(0)
         prob = held.tile([P, PACK, N], F32, name="prob")
-        pw_rows = held.tile([P, PACK, N], F32, name="pw_rows")
+        pw_rows = new_tile("pw_rows", [P, PACK, N], BF16)
         for j in range(PACK):
             nc.scalar.activation(prob[:, j, :], scores[j][:], ACT.Sigmoid)
         for j in range(PACK):
-            nc.scalar.activation(pw_rows[:, j, :], prob[:, j, :], ACT.Copy, scale=gate[:, j : j + 1])
-        pw_mx = quantise("pw", weave_shared("pw", pw_rows), E4M3)
-        dv_early = [product("dv_early", "back", dom_early_mx, pw_mx, m) for m in range(HALF // P)]
+            nc.vector.tensor_scalar(pw_rows[:, j, :], prob[:, j, :], gate[:, j : j + 1], None, MULT)
+        dom_woven = [weave("dom0", dom_rows, 0, 2 * P)]
+        pw_woven = weave_shared("pw", pw_rows, PW_SHARE)
+        dom_woven.append(weave("dom1", dom_rows, 2 * P, 2 * P))
+        pw_mx = quantise("pw", pw_woven, E4M3)
+        dom_mx = [quantise("dom%d" % h, dom_woven[h], E5M2) for h in range(2)]
+        dv = [product("dv%d" % m, "back", dom_mx[m // 2], m % 2, pw_mx) for m in range(BLOCKS)]
+        for t in range(1, PACK):
+            gather_values(t)
 
         minus_slopes = []
         for j in range(PACK):
-            minus_slope = held.tile([P, N], F32, name="minus_slope%d" % j, tag="minus_slope%d" % j)
-            nc.vector.scalar_tensor_tensor(minus_slope[:], prob[:, j, :], 1.0, pw_rows[:, j, :], SUBTRACT, MULT)
+            minus_slope = new_tile("minus_slope%d" % j, [P, N], F32)
+            nc.vector.scalar_tensor_tensor(minus_slope[:], prob[:, j, :], 1.0, prob[:, j, :], SUBTRACT, MULT)
             minus_slopes.append(minus_slope)
 
-        do_mx = quantise("do", weave_dealt("do", do_rows), E5M2)
-        v_rows = held.tile([P, PACK, N], BF16, name="v_rows")
-        for t in range(PACK):
-            nc.vector.tensor_copy(v_rows[:, t, :], v_planes[t][:].indirect(offsets[:]))
-        v_mx = quantise("v", weave_shared("v", v_rows), E4M3)
+        put("dv0", dv[0], windows[0], out_1, 0, at_v3)
+        v_woven = weave_shared("v", v_rows, V_SHARE)
+        v_mx = quantise("v", v_woven, E4M3)
+        put("dv1", dv[1], windows[1], out_1, 1, at_v3 + STAGED_BYTES)
+        do_mx = [quantise("do0", weave_dealt("do0", do_rows, 0, nc.scalar.copy), E5M2)]
+        put("dv2", dv[2], windows[2], out_1, 2, at_v)
+        do_mx.append(quantise("do1", weave_dealt("do1", do_rows, 1, nc.scalar.copy), E5M2))
 
-        for m in range(HALF // P):
-            staged = late.tile([P, N], F32, name="dv%d_staged" % m, offset=m * N * 4, align_bytes=ALIGN)
-            put(dv_early[m], staged, windows[m], out_1, m)
-        dom_late_mx = quantise("dom_late", weave("dom_late", dom_late_rows, nc.scalar.copy), E5M2)
-        dv_late = [product("dv_late", "back", dom_late_mx, pw_mx, m) for m in range(HALF // P)]
-        qm_woven = weave("qm", qm_rows, nc.scalar.copy)
-
-        ds_rows = held.tile([P, PACK, N], BF16, name="ds_rows", tag="ds_rows")
+        ds_rows = new_tile("ds_rows", [P, PACK, N], BF16, at_ds)
         for j in range(PACK):
-            dp = product("dp", "front", do_mx, v_mx, j)
-            nc.vector.scalar_tensor_tensor(ds_rows[:, j, :], dp[:], -1.0, minus_slopes[j][:], MULT, MULT)
-        staged = held.tile([P, N], F32, name="dv2_staged", tag="minus_slope0")
-        put(dv_late[0], staged, windows[2], out_1, 2)
-        qm_mx = quantise("qm", qm_woven, E4M3)
-        ds_mx = quantise("ds", weave_shared("ds", ds_rows), E5M2)
-        staged = held.tile([P, N], F32, name="dv3_staged", tag="ds_rows")
-        put(dv_late[1], staged, windows[3], out_1, 3)
+            dp = product("dp%d" % j, "front", do_mx[j // 2], j % 2, v_mx)
+            nc.vector.scalar_tensor_tensor(
+                ds_rows[:, j, :], dp[:], minus_gate[:, j : j + 1], minus_slopes[j][:], MULT, MULT
+            )
+        ds_woven = weave_shared("ds", ds_rows, DS_SHARE)
+        qm_mx = [quantise("qm0", weave("qm0", qm_rows, 0, 2 * P), E4M3)]
+        ds_mx = quantise("ds", ds_woven, E5M2)
+        qm_mx.append(quantise("qm1", weave("qm1", qm_rows, 2 * P, 2 * P), E4M3, at_ds + STAGED_BYTES))
+        put("dv3", dv[3], windows[3], out_1, 3, at_ds)
 
         for m in range(BLOCKS):
-            bank = product("dk", "front", qm_mx, ds_mx, m)
-            staged = held.tile([P, N], F32, name="dk%d_staged" % m)
-            put(bank, staged, windows[(BLOCKS + m) % WINDOWS], out_0, m)
+            bank = product("dk%d" % m, "front", qm_mx[m // 2], m % 2, ds_mx)
+            put("dk%d" % m, bank, windows[(BLOCKS + m) % WINDOWS], out_0, m)

@@ -22,9 +22,9 @@ PACK = 4
 ALIGN = 64
 BLOCKS = DV // P
 WINDOWS = BLOCKS + 1
-PW_SHARE = 128
-V_SHARE = 384
+PW_SHARE = 352
 DS_SHARE = 320
+HALF = DV // 2
 PLANE_BYTES = T * 4
 ROWS_BYTES = PACK * N * 2
 STAGED_BYTES = N * 4
@@ -38,16 +38,16 @@ def tile_attend_gat_sig_kv_kernel(tc, qT, kT, vT, doT, rw, qm, dom, offs, out_0,
         psum = ctx.enter_context(tc.psum_pool(name="psum", bufs=PACK))
 
         at_v3 = 0
-        at_v = PLANE_BYTES
-        at_ds = at_v + ROWS_BYTES
+        at_slope = PLANE_BYTES
+        at_ds = at_slope + STAGED_BYTES
 
         def new_tile(name, shape, dtype, at=None):
             if at is None:
                 return held.tile(shape, dtype, name=name, align_bytes=ALIGN)
             return late.tile(shape, dtype, name=name, offset=at, align_bytes=ALIGN)
 
-        def load_rows(name, src):
-            rows = new_tile(name + "_rows", [P, PACK, src.shape[1]], F32)
+        def load_rows(name, src, at=None):
+            rows = new_tile(name + "_rows", [P, PACK, src.shape[1]], F32, at)
             nc.sync.dma_start(rows[:], src.rearrange("(p t) c -> p t c", t=PACK))
             return rows
 
@@ -63,10 +63,11 @@ def tile_attend_gat_sig_kv_kernel(tc, qT, kT, vT, doT, rw, qm, dom, offs, out_0,
         nc.sync.dma_start(gate[:], rw[0].rearrange("(p j) o -> p (j o)", j=PACK))
         k_planes.extend(load_plane("k", kT, t) for t in range(1, PACK))
         q_rows = load_rows("q", qT[0])
-        v_planes = [load_plane("v", vT, 0)]
-        dom_rows = load_rows("dom", dom[0])
-        v_planes.extend(load_plane("v", vT, t, at) for t, at in ((1, None), (2, None), (3, at_v3)))
+        dom_rows = [load_rows("dom0", dom[0][:, :HALF])]
+        v_planes = [load_plane("v", vT, t) for t in range(PACK - 1)]
         do_rows = load_rows("do", doT[0])
+        v_planes.append(load_plane("v", vT, PACK - 1, at_v3))
+        dom_rows.append(load_rows("dom1", dom[0][:, HALF:]))
         qm_rows = load_rows("qm", qm[0])
 
         windows = []
@@ -76,7 +77,7 @@ def tile_attend_gat_sig_kv_kernel(tc, qT, kT, vT, doT, rw, qm, dom, offs, out_0,
             engine.memset(window[:].bitcast(I32), 0)
             windows.append(window)
         minus_gate = held.tile([P, PACK], F32, name="minus_gate")
-        nc.scalar.activation(minus_gate[:], gate[:], ACT.Copy, scale=-1.0)
+        nc.vector.tensor_scalar(minus_gate[:], gate[:], -1.0, None, MULT)
 
         def new_woven(name, width=N):
             return new_tile(name + "_woven", [P, width, PACK], BF16)
@@ -88,11 +89,11 @@ def tile_attend_gat_sig_kv_kernel(tc, qT, kT, vT, doT, rw, qm, dom, offs, out_0,
             nc.vector.quantize_mx(out=words[:].bitcast(fmt), scales=scales[:], in_=woven[:].rearrange("p c t -> p (c t)"))
             return words, scales, fmt
 
-        def weave_dealt(name, rows, half, copy):
-            woven = new_woven(name, N // 2)
+        def weave_dealt(name, rows, first, count, copy):
+            woven = new_woven(name, count * P)
             copy(
-                woven[:].rearrange("p (j s) t -> p s t j", j=2),
-                rows[:].rearrange("p t (s j) -> p s t j", j=PACK)[:, :, :, 2 * half : 2 * half + 2],
+                woven[:].rearrange("p (j s) t -> p s t j", j=count),
+                rows[:].rearrange("p t (s j) -> p s t j", j=PACK)[:, :, :, first : first + count],
             )
             return woven
 
@@ -102,9 +103,9 @@ def tile_attend_gat_sig_kv_kernel(tc, qT, kT, vT, doT, rw, qm, dom, offs, out_0,
                 rows.rearrange("p t (c i) -> p c t i", i=PACK),
             )
 
-        def weave(name, rows, first, width):
+        def weave(name, rows, first, width, copy=nc.scalar.copy):
             woven = new_woven(name, width)
-            weave_columns(woven[:], rows[:, :, first : first + width], nc.scalar.copy)
+            weave_columns(woven[:], rows[:, :, first : first + width], copy)
             return woven
 
         def weave_shared(name, rows, share):
@@ -137,55 +138,53 @@ def tile_attend_gat_sig_kv_kernel(tc, qT, kT, vT, doT, rw, qm, dom, offs, out_0,
         for t in range(PACK):
             nc.vector.tensor_copy(k_woven[:, :, t], k_planes[t][:].indirect(offsets[:]))
         k_mx = quantise("k", k_woven, E4M3)
-        q_woven = [weave_dealt("q%d" % h, q_rows, h, copy) for h, copy in enumerate((nc.vector.tensor_copy, nc.scalar.copy))]
+        q_woven = [weave_dealt("q%d" % h, q_rows, 2 * h, 2, nc.vector.tensor_copy) for h in range(2)]
         q_mx = [quantise("q%d" % h, q_woven[h], E4M3) for h in range(2)]
         scores = [product("score%d" % j, "front", q_mx[j // 2], j % 2, k_mx) for j in range(PACK)]
 
-        v_rows = new_tile("v_rows", [P, PACK, N], BF16, at_v)
-
-        def gather_values(t):
-            nc.vector.tensor_copy(v_rows[:, t, :], v_planes[t][:].indirect(offsets[:]))
-
-        gather_values(0)
         prob = held.tile([P, PACK, N], F32, name="prob")
         pw_rows = new_tile("pw_rows", [P, PACK, N], BF16)
+        dom_mx = [quantise("dom0", weave("dom0", dom_rows[0], 0, HALF, nc.vector.tensor_copy), E5M2)]
         for j in range(PACK):
             nc.scalar.activation(prob[:, j, :], scores[j][:], ACT.Sigmoid)
         for j in range(PACK):
-            nc.vector.tensor_scalar(pw_rows[:, j, :], prob[:, j, :], gate[:, j : j + 1], None, MULT)
-        dom_woven = [weave("dom0", dom_rows, 0, 2 * P)]
-        pw_woven = weave_shared("pw", pw_rows, PW_SHARE)
-        dom_woven.append(weave("dom1", dom_rows, 2 * P, 2 * P))
-        pw_mx = quantise("pw", pw_woven, E4M3)
-        dom_mx = [quantise("dom%d" % h, dom_woven[h], E5M2) for h in range(2)]
-        dv = [product("dv%d" % m, "back", dom_mx[m // 2], m % 2, pw_mx) for m in range(BLOCKS)]
-        for t in range(1, PACK):
-            gather_values(t)
+            nc.scalar.activation(pw_rows[:, j, :], prob[:, j, :], ACT.Copy, scale=gate[:, j : j + 1])
+        pw_mx = quantise("pw", weave_shared("pw", pw_rows, PW_SHARE), E4M3)
+        dv = [product("dv%d" % m, "back", dom_mx[0], m, pw_mx) for m in range(2)]
+
+        v_rows = new_tile("v_rows", [P, PACK - 1, N], BF16)
+        for t in range(PACK - 1):
+            nc.vector.tensor_copy(v_rows[:, t, :], v_planes[t][:].indirect(offsets[:]))
+        v_woven = new_woven("v")
+        weave_columns(v_woven[:, :, : PACK - 1], v_rows[:], nc.vector.tensor_copy)
+        nc.vector.tensor_copy(v_woven[:, :, PACK - 1], v_planes[PACK - 1][:].indirect(offsets[:]))
 
         minus_slopes = []
         for j in range(PACK):
-            minus_slope = new_tile("minus_slope%d" % j, [P, N], F32)
+            minus_slope = new_tile("minus_slope%d" % j, [P, N], F32, at_slope if j == 0 else None)
             nc.vector.scalar_tensor_tensor(minus_slope[:], prob[:, j, :], 1.0, prob[:, j, :], SUBTRACT, MULT)
             minus_slopes.append(minus_slope)
 
-        put("dv0", dv[0], windows[0], out_1, 0, at_v3)
-        v_woven = weave_shared("v", v_rows, V_SHARE)
+        do_woven = weave_dealt("do", do_rows, 0, PACK, nc.scalar.copy)
         v_mx = quantise("v", v_woven, E4M3)
-        put("dv1", dv[1], windows[1], out_1, 1, at_v3 + STAGED_BYTES)
-        do_mx = [quantise("do0", weave_dealt("do0", do_rows, 0, nc.scalar.copy), E5M2)]
-        put("dv2", dv[2], windows[2], out_1, 2, at_v)
-        do_mx.append(quantise("do1", weave_dealt("do1", do_rows, 1, nc.scalar.copy), E5M2))
+        do_mx = quantise("do", do_woven, E5M2, at_v3 + 2 * STAGED_BYTES)
+        for m in range(2):
+            put("dv%d" % m, dv[m], windows[m], out_1, m, at_v3 + m * STAGED_BYTES)
+        dom_mx.append(quantise("dom1", weave("dom1", dom_rows[1], 0, HALF), E5M2))
+        dv.extend(product("dv%d" % m, "back", dom_mx[1], m - 2, pw_mx) for m in (2, 3))
+        qm_woven = [weave("qm%d" % h, qm_rows, h * HALF, HALF) for h in range(2)]
 
         ds_rows = new_tile("ds_rows", [P, PACK, N], BF16, at_ds)
         for j in range(PACK):
-            dp = product("dp%d" % j, "front", do_mx[j // 2], j % 2, v_mx)
+            dp = product("dp%d" % j, "front", do_mx, j, v_mx)
             nc.vector.scalar_tensor_tensor(
                 ds_rows[:, j, :], dp[:], minus_gate[:, j : j + 1], minus_slopes[j][:], MULT, MULT
             )
+        put("dv2", dv[2], windows[2], out_1, 2, at_slope)
         ds_woven = weave_shared("ds", ds_rows, DS_SHARE)
-        qm_mx = [quantise("qm0", weave("qm0", qm_rows, 0, 2 * P), E4M3)]
+        qm_mx = [quantise("qm0", qm_woven[0], E4M3)]
         ds_mx = quantise("ds", ds_woven, E5M2)
-        qm_mx.append(quantise("qm1", weave("qm1", qm_rows, 2 * P, 2 * P), E4M3, at_ds + STAGED_BYTES))
+        qm_mx.append(quantise("qm1", qm_woven[1], E4M3, at_ds + STAGED_BYTES))
         put("dv3", dv[3], windows[3], out_1, 3, at_ds)
 
         for m in range(BLOCKS):

@@ -22,7 +22,7 @@ PACK = 4
 ALIGN = 64
 BLOCKS = DV // P
 WINDOWS = BLOCKS + 1
-PW_SHARE = 352
+PW_SHARE = 288
 DS_SHARE = 320
 HALF = DV // 2
 PLANE_BYTES = T * 4
@@ -39,7 +39,7 @@ def tile_attend_gat_sig_kv_kernel(tc, qT, kT, vT, doT, rw, qm, dom, offs, out_0,
 
         at_v3 = 0
         at_slope = PLANE_BYTES
-        at_ds = at_slope + STAGED_BYTES
+        at_ds = at_slope + 2 * STAGED_BYTES
 
         def new_tile(name, shape, dtype, at=None):
             if at is None:
@@ -63,8 +63,9 @@ def tile_attend_gat_sig_kv_kernel(tc, qT, kT, vT, doT, rw, qm, dom, offs, out_0,
         nc.sync.dma_start(gate[:], rw[0].rearrange("(p j) o -> p (j o)", j=PACK))
         k_planes.extend(load_plane("k", kT, t) for t in range(1, PACK))
         q_rows = load_rows("q", qT[0])
+        v_planes = [load_plane("v", vT, 0)]
         dom_rows = [load_rows("dom0", dom[0][:, :HALF])]
-        v_planes = [load_plane("v", vT, t) for t in range(PACK - 1)]
+        v_planes.extend(load_plane("v", vT, t) for t in range(1, PACK - 1))
         do_rows = load_rows("do", doT[0])
         v_planes.append(load_plane("v", vT, PACK - 1, at_v3))
         dom_rows.append(load_rows("dom1", dom[0][:, HALF:]))
@@ -161,7 +162,7 @@ def tile_attend_gat_sig_kv_kernel(tc, qT, kT, vT, doT, rw, qm, dom, offs, out_0,
 
         minus_slopes = []
         for j in range(PACK):
-            minus_slope = new_tile("minus_slope%d" % j, [P, N], F32, at_slope if j == 0 else None)
+            minus_slope = new_tile("minus_slope%d" % j, [P, N], F32, {0: at_slope, 3: at_slope + STAGED_BYTES}.get(j))
             nc.vector.scalar_tensor_tensor(minus_slope[:], prob[:, j, :], 1.0, prob[:, j, :], SUBTRACT, MULT)
             minus_slopes.append(minus_slope)
 
@@ -171,7 +172,6 @@ def tile_attend_gat_sig_kv_kernel(tc, qT, kT, vT, doT, rw, qm, dom, offs, out_0,
         for m in range(2):
             put("dv%d" % m, dv[m], windows[m], out_1, m, at_v3 + m * STAGED_BYTES)
         dom_mx.append(quantise("dom1", weave("dom1", dom_rows[1], 0, HALF), E5M2))
-        dv.extend(product("dv%d" % m, "back", dom_mx[1], m - 2, pw_mx) for m in (2, 3))
         qm_woven = [weave("qm%d" % h, qm_rows, h * HALF, HALF) for h in range(2)]
 
         ds_rows = new_tile("ds_rows", [P, PACK, N], BF16, at_ds)
@@ -180,12 +180,13 @@ def tile_attend_gat_sig_kv_kernel(tc, qT, kT, vT, doT, rw, qm, dom, offs, out_0,
             nc.vector.scalar_tensor_tensor(
                 ds_rows[:, j, :], dp[:], minus_gate[:, j : j + 1], minus_slopes[j][:], MULT, MULT
             )
+        dv.extend(product("dv%d" % m, "back", dom_mx[1], m - 2, pw_mx) for m in (2, 3))
         put("dv2", dv[2], windows[2], out_1, 2, at_slope)
         ds_woven = weave_shared("ds", ds_rows, DS_SHARE)
         qm_mx = [quantise("qm0", qm_woven[0], E4M3)]
         ds_mx = quantise("ds", ds_woven, E5M2)
-        qm_mx.append(quantise("qm1", qm_woven[1], E4M3, at_ds + STAGED_BYTES))
-        put("dv3", dv[3], windows[3], out_1, 3, at_ds)
+        put("dv3", dv[3], windows[3], out_1, 3, at_slope + STAGED_BYTES)
+        qm_mx.append(quantise("qm1", qm_woven[1], E4M3, at_ds))
 
         for m in range(BLOCKS):
             bank = product("dk%d" % m, "front", qm_mx[m // 2], m % 2, ds_mx)

@@ -19,35 +19,39 @@ SUBTRACT = mybir.AluOpType.subtract
 
 P = 128
 PACK = 4
+LAST = PACK - 1
+BAND = 16
 ALIGN = 64
 BLOCKS = DV // P
 WINDOWS = BLOCKS + 1
 PW_SHARE = 288
 DS_SHARE = 320
 HALF = DV // 2
+HALF_BLOCKS = HALF // P
 PLANE_BYTES = T * 4
-ROWS_BYTES = PACK * N * 2
-STAGED_BYTES = N * 4
+BANK_BYTES = N * 4
+
+AT_LAST_PLANE = 0
+AT_DO_CODES = AT_LAST_PLANE + HALF_BLOCKS * BANK_BYTES
+AT_FIRST_SLOPE = PLANE_BYTES
+AT_LAST_SLOPE = AT_FIRST_SLOPE + BANK_BYTES
+AT_DK_STAGED = AT_LAST_SLOPE + BANK_BYTES
 
 
 def tile_attend_gat_sig_kv_kernel(tc, qT, kT, vT, doT, rw, qm, dom, offs, out_0, out_1):
     nc = tc.nc
     with ExitStack() as ctx:
         held = ctx.enter_context(tc.tile_pool(name="held", bufs=1))
-        late = ctx.enter_context(tc.tile_pool(name="late", bufs=1))
+        shared = ctx.enter_context(tc.tile_pool(name="shared", bufs=1))
         psum = ctx.enter_context(tc.psum_pool(name="psum", bufs=PACK))
-
-        at_v3 = 0
-        at_slope = PLANE_BYTES
-        at_ds = at_slope + 2 * STAGED_BYTES
 
         def new_tile(name, shape, dtype, at=None):
             if at is None:
                 return held.tile(shape, dtype, name=name, align_bytes=ALIGN)
-            return late.tile(shape, dtype, name=name, offset=at, align_bytes=ALIGN)
+            return shared.tile(shape, dtype, name=name, offset=at, align_bytes=ALIGN)
 
-        def load_rows(name, src, at=None):
-            rows = new_tile(name + "_rows", [P, PACK, src.shape[1]], F32, at)
+        def load_rows(name, src):
+            rows = new_tile(name + "_rows", [P, PACK, src.shape[1]], F32)
             nc.sync.dma_start(rows[:], src.rearrange("(p t) c -> p t c", t=PACK))
             return rows
 
@@ -57,18 +61,18 @@ def tile_attend_gat_sig_kv_kernel(tc, qT, kT, vT, doT, rw, qm, dom, offs, out_0,
             return plane
 
         k_planes = [load_plane("k", kT, 0)]
-        offsets = held.tile([P, N // 16], U16, name="offsets")
+        offsets = held.tile([P, N // BAND], U16, name="offsets")
         nc.sync.dma_start(offsets[:], offs)
         gate = held.tile([P, PACK], F32, name="gate")
         nc.sync.dma_start(gate[:], rw[0].rearrange("(p j) o -> p (j o)", j=PACK))
         k_planes.extend(load_plane("k", kT, t) for t in range(1, PACK))
         q_rows = load_rows("q", qT[0])
         v_planes = [load_plane("v", vT, 0)]
-        dom_rows = [load_rows("dom0", dom[0][:, :HALF])]
-        v_planes.extend(load_plane("v", vT, t) for t in range(1, PACK - 1))
+        dom_early_rows = load_rows("dom_early", dom[0][:, :HALF])
+        v_planes.extend(load_plane("v", vT, t) for t in range(1, LAST))
         do_rows = load_rows("do", doT[0])
-        v_planes.append(load_plane("v", vT, PACK - 1, at_v3))
-        dom_rows.append(load_rows("dom1", dom[0][:, HALF:]))
+        v_planes.append(load_plane("v", vT, LAST, AT_LAST_PLANE))
+        dom_late_rows = load_rows("dom_late", dom[0][:, HALF:])
         qm_rows = load_rows("qm", qm[0])
 
         windows = []
@@ -86,7 +90,7 @@ def tile_attend_gat_sig_kv_kernel(tc, qT, kT, vT, doT, rw, qm, dom, offs, out_0,
         def quantise(name, woven, fmt, at=None):
             width = woven.shape[1]
             words = new_tile(name + "_words", [P, width], U32, at)
-            scales = new_tile(name + "_scales", [P, width], U8, None if at is None else at + 4 * width)
+            scales = new_tile(name + "_scales", [P, width], U8, None if at is None else at + PACK * width)
             nc.vector.quantize_mx(out=words[:].bitcast(fmt), scales=scales[:], in_=woven[:].rearrange("p c t -> p (c t)"))
             return words, scales, fmt
 
@@ -98,21 +102,21 @@ def tile_attend_gat_sig_kv_kernel(tc, qT, kT, vT, doT, rw, qm, dom, offs, out_0,
             )
             return woven
 
-        def weave_columns(woven, rows, copy):
+        def weave_into(woven, rows, copy):
             copy(
                 woven.rearrange("p (c i) t -> p c t i", i=PACK),
                 rows.rearrange("p t (c i) -> p c t i", i=PACK),
             )
 
-        def weave(name, rows, first, width, copy=nc.scalar.copy):
-            woven = new_woven(name, width)
-            weave_columns(woven[:], rows[:, :, first : first + width], copy)
+        def weave_half(name, rows, first, copy):
+            woven = new_woven(name, HALF)
+            weave_into(woven[:], rows[:, :, first : first + HALF], copy)
             return woven
 
         def weave_shared(name, rows, share):
             woven = new_woven(name)
-            weave_columns(woven[:, :share, :], rows[:, :, :share], nc.vector.tensor_copy)
-            weave_columns(woven[:, share:, :], rows[:, :, share:], nc.scalar.copy)
+            weave_into(woven[:, :share, :], rows[:, :, :share], nc.vector.tensor_copy)
+            weave_into(woven[:, share:, :], rows[:, :, share:], nc.scalar.copy)
             return woven
 
         def product(name, tag, stationary, m, moving):
@@ -139,55 +143,59 @@ def tile_attend_gat_sig_kv_kernel(tc, qT, kT, vT, doT, rw, qm, dom, offs, out_0,
         for t in range(PACK):
             nc.vector.tensor_copy(k_woven[:, :, t], k_planes[t][:].indirect(offsets[:]))
         k_mx = quantise("k", k_woven, E4M3)
-        q_woven = [weave_dealt("q%d" % h, q_rows, 2 * h, 2, nc.vector.tensor_copy) for h in range(2)]
+        q_woven = [
+            weave_dealt("q%d" % h, q_rows, h * HALF_BLOCKS, HALF_BLOCKS, nc.vector.tensor_copy) for h in range(2)
+        ]
         q_mx = [quantise("q%d" % h, q_woven[h], E4M3) for h in range(2)]
-        scores = [product("score%d" % j, "front", q_mx[j // 2], j % 2, k_mx) for j in range(PACK)]
+        scores = [product("score%d" % j, "front", q_mx[j // HALF_BLOCKS], j % HALF_BLOCKS, k_mx) for j in range(PACK)]
 
         prob = held.tile([P, PACK, N], F32, name="prob")
         pw_rows = new_tile("pw_rows", [P, PACK, N], BF16)
-        dom_mx = [quantise("dom0", weave("dom0", dom_rows[0], 0, HALF, nc.vector.tensor_copy), E5M2)]
+        dom_early_mx = quantise("dom_early", weave_half("dom_early", dom_early_rows, 0, nc.vector.tensor_copy), E5M2)
         for j in range(PACK):
             nc.scalar.activation(prob[:, j, :], scores[j][:], ACT.Sigmoid)
         for j in range(PACK):
             nc.scalar.activation(pw_rows[:, j, :], prob[:, j, :], ACT.Copy, scale=gate[:, j : j + 1])
         pw_mx = quantise("pw", weave_shared("pw", pw_rows, PW_SHARE), E4M3)
-        dv = [product("dv%d" % m, "back", dom_mx[0], m, pw_mx) for m in range(2)]
+        dv = [product("dv%d" % m, "back", dom_early_mx, m, pw_mx) for m in range(HALF_BLOCKS)]
 
-        v_rows = new_tile("v_rows", [P, PACK - 1, N], BF16)
-        for t in range(PACK - 1):
+        v_rows = new_tile("v_rows", [P, LAST, N], BF16)
+        for t in range(LAST):
             nc.vector.tensor_copy(v_rows[:, t, :], v_planes[t][:].indirect(offsets[:]))
         v_woven = new_woven("v")
-        weave_columns(v_woven[:, :, : PACK - 1], v_rows[:], nc.vector.tensor_copy)
-        nc.vector.tensor_copy(v_woven[:, :, PACK - 1], v_planes[PACK - 1][:].indirect(offsets[:]))
+        weave_into(v_woven[:, :, :LAST], v_rows[:], nc.vector.tensor_copy)
+        nc.vector.tensor_copy(v_woven[:, :, LAST], v_planes[LAST][:].indirect(offsets[:]))
 
+        slope_at = {0: AT_FIRST_SLOPE, LAST: AT_LAST_SLOPE}
         minus_slopes = []
         for j in range(PACK):
-            minus_slope = new_tile("minus_slope%d" % j, [P, N], F32, {0: at_slope, 3: at_slope + STAGED_BYTES}.get(j))
+            minus_slope = new_tile("minus_slope%d" % j, [P, N], F32, slope_at.get(j))
             nc.vector.scalar_tensor_tensor(minus_slope[:], prob[:, j, :], 1.0, prob[:, j, :], SUBTRACT, MULT)
             minus_slopes.append(minus_slope)
 
         do_woven = weave_dealt("do", do_rows, 0, PACK, nc.scalar.copy)
         v_mx = quantise("v", v_woven, E4M3)
-        do_mx = quantise("do", do_woven, E5M2, at_v3 + 2 * STAGED_BYTES)
-        for m in range(2):
-            put("dv%d" % m, dv[m], windows[m], out_1, m, at_v3 + m * STAGED_BYTES)
-        dom_mx.append(quantise("dom1", weave("dom1", dom_rows[1], 0, HALF), E5M2))
-        qm_woven = [weave("qm%d" % h, qm_rows, h * HALF, HALF) for h in range(2)]
+        do_mx = quantise("do", do_woven, E5M2, AT_DO_CODES)
+        for m in range(HALF_BLOCKS):
+            put("dv%d" % m, dv[m], windows[m], out_1, m, AT_LAST_PLANE + m * BANK_BYTES)
+        dom_late_mx = quantise("dom_late", weave_half("dom_late", dom_late_rows, 0, nc.scalar.copy), E5M2)
+        qm_woven = [weave_half("qm%d" % h, qm_rows, h * HALF, nc.scalar.copy) for h in range(2)]
 
-        ds_rows = new_tile("ds_rows", [P, PACK, N], BF16, at_ds)
+        ds_rows = new_tile("ds_rows", [P, PACK, N], BF16)
         for j in range(PACK):
             dp = product("dp%d" % j, "front", do_mx, j, v_mx)
             nc.vector.scalar_tensor_tensor(
                 ds_rows[:, j, :], dp[:], minus_gate[:, j : j + 1], minus_slopes[j][:], MULT, MULT
             )
-        dv.extend(product("dv%d" % m, "back", dom_mx[1], m - 2, pw_mx) for m in (2, 3))
-        put("dv2", dv[2], windows[2], out_1, 2, at_slope)
+        dv.extend(product("dv%d" % (HALF_BLOCKS + m), "back", dom_late_mx, m, pw_mx) for m in range(HALF_BLOCKS))
+        put("dv2", dv[2], windows[2], out_1, 2, AT_FIRST_SLOPE)
         ds_woven = weave_shared("ds", ds_rows, DS_SHARE)
         qm_mx = [quantise("qm0", qm_woven[0], E4M3)]
         ds_mx = quantise("ds", ds_woven, E5M2)
-        put("dv3", dv[3], windows[3], out_1, 3, at_slope + STAGED_BYTES)
-        qm_mx.append(quantise("qm1", qm_woven[1], E4M3, at_ds))
+        put("dv3", dv[3], windows[3], out_1, 3, AT_LAST_SLOPE)
 
-        for m in range(BLOCKS):
-            bank = product("dk%d" % m, "front", qm_mx[m // 2], m % 2, ds_mx)
+        put("dk0", product("dk0", "front", qm_mx[0], 0, ds_mx), windows[BLOCKS], out_0, 0, AT_DK_STAGED)
+        qm_mx.append(quantise("qm1", qm_woven[1], E4M3, AT_DK_STAGED))
+        for m in range(1, BLOCKS):
+            bank = product("dk%d" % m, "front", qm_mx[m // HALF_BLOCKS], m % HALF_BLOCKS, ds_mx)
             put("dk%d" % m, bank, windows[(BLOCKS + m) % WINDOWS], out_0, m)

@@ -25,7 +25,7 @@ ALIGN = 64
 BLOCKS = DV // P
 WINDOWS = BLOCKS + 1
 PW_SHARE = 288
-DS_SHARE = 320
+DS_SHARE = 208
 HALF = DV // 2
 HALF_BLOCKS = HALF // P
 PLANE_BYTES = T * 4
@@ -33,9 +33,9 @@ BANK_BYTES = N * 4
 
 AT_LAST_PLANE = 0
 AT_DO_CODES = AT_LAST_PLANE + HALF_BLOCKS * BANK_BYTES
-AT_FIRST_SLOPE = PLANE_BYTES
-AT_LAST_SLOPE = AT_FIRST_SLOPE + BANK_BYTES
-AT_DK_STAGED = AT_LAST_SLOPE + BANK_BYTES
+AT_DOM_LATE = PLANE_BYTES
+AT_DS_ROWS = AT_DOM_LATE
+AT_QM_LATE = AT_DS_ROWS + BANK_BYTES
 
 
 def tile_attend_gat_sig_kv_kernel(tc, qT, kT, vT, doT, rw, qm, dom, offs, out_0, out_1):
@@ -84,8 +84,8 @@ def tile_attend_gat_sig_kv_kernel(tc, qT, kT, vT, doT, rw, qm, dom, offs, out_0,
         minus_gate = held.tile([P, PACK], F32, name="minus_gate")
         nc.vector.tensor_scalar(minus_gate[:], gate[:], -1.0, None, MULT)
 
-        def new_woven(name, width=N):
-            return new_tile(name + "_woven", [P, width, PACK], BF16)
+        def new_woven(name, width=N, at=None):
+            return new_tile(name + "_woven", [P, width, PACK], BF16, at)
 
         def quantise(name, woven, fmt, at=None):
             width = woven.shape[1]
@@ -108,8 +108,8 @@ def tile_attend_gat_sig_kv_kernel(tc, qT, kT, vT, doT, rw, qm, dom, offs, out_0,
                 rows.rearrange("p t (c i) -> p c t i", i=PACK),
             )
 
-        def weave_half(name, rows, first, copy):
-            woven = new_woven(name, HALF)
+        def weave_half(name, rows, first, copy, at=None):
+            woven = new_woven(name, HALF, at)
             weave_into(woven[:], rows[:, :, first : first + HALF], copy)
             return woven
 
@@ -166,36 +166,33 @@ def tile_attend_gat_sig_kv_kernel(tc, qT, kT, vT, doT, rw, qm, dom, offs, out_0,
         weave_into(v_woven[:, :, :LAST], v_rows[:], nc.vector.tensor_copy)
         nc.vector.tensor_copy(v_woven[:, :, LAST], v_planes[LAST][:].indirect(offsets[:]))
 
-        slope_at = {0: AT_FIRST_SLOPE, LAST: AT_LAST_SLOPE}
         minus_slopes = []
         for j in range(PACK):
-            minus_slope = new_tile("minus_slope%d" % j, [P, N], F32, slope_at.get(j))
+            minus_slope = new_tile("minus_slope%d" % j, [P, N], F32)
             nc.vector.scalar_tensor_tensor(minus_slope[:], prob[:, j, :], 1.0, prob[:, j, :], SUBTRACT, MULT)
             minus_slopes.append(minus_slope)
 
-        do_woven = weave_dealt("do", do_rows, 0, PACK, nc.scalar.copy)
+        do_woven = [weave_dealt("do%d" % h, do_rows, h * HALF_BLOCKS, HALF_BLOCKS, nc.scalar.copy) for h in range(2)]
+        do_mx = [quantise("do0", do_woven[0], E5M2), quantise("do1", do_woven[1], E5M2, AT_DO_CODES)]
         v_mx = quantise("v", v_woven, E4M3)
-        do_mx = quantise("do", do_woven, E5M2, AT_DO_CODES)
         for m in range(HALF_BLOCKS):
             put("dv%d" % m, dv[m], windows[m], out_1, m, AT_LAST_PLANE + m * BANK_BYTES)
-        dom_late_mx = quantise("dom_late", weave_half("dom_late", dom_late_rows, 0, nc.scalar.copy), E5M2)
-        qm_woven = [weave_half("qm%d" % h, qm_rows, h * HALF, nc.scalar.copy) for h in range(2)]
+        dom_late_mx = quantise("dom_late", weave_half("dom_late", dom_late_rows, 0, nc.scalar.copy, AT_DOM_LATE), E5M2)
+        qm_woven = weave_half("qm0", qm_rows, 0, nc.scalar.copy)
 
-        ds_rows = new_tile("ds_rows", [P, PACK, N], BF16)
+        ds_rows = new_tile("ds_rows", [P, PACK, N], BF16, AT_DS_ROWS)
         for j in range(PACK):
-            dp = product("dp%d" % j, "front", do_mx, j, v_mx)
+            dp = product("dp%d" % j, "front", do_mx[j // HALF_BLOCKS], j % HALF_BLOCKS, v_mx)
             nc.vector.scalar_tensor_tensor(
                 ds_rows[:, j, :], dp[:], minus_gate[:, j : j + 1], minus_slopes[j][:], MULT, MULT
             )
         dv.extend(product("dv%d" % (HALF_BLOCKS + m), "back", dom_late_mx, m, pw_mx) for m in range(HALF_BLOCKS))
-        put("dv2", dv[2], windows[2], out_1, 2, AT_FIRST_SLOPE)
+        put("dv2", dv[2], windows[2], out_1, 2)
         ds_woven = weave_shared("ds", ds_rows, DS_SHARE)
-        qm_mx = [quantise("qm0", qm_woven[0], E4M3)]
+        qm_mx = [quantise("qm0", qm_woven, E4M3)]
         ds_mx = quantise("ds", ds_woven, E5M2)
-        put("dv3", dv[3], windows[3], out_1, 3, AT_LAST_SLOPE)
-
-        put("dk0", product("dk0", "front", qm_mx[0], 0, ds_mx), windows[BLOCKS], out_0, 0, AT_DK_STAGED)
-        qm_mx.append(quantise("qm1", qm_woven[1], E4M3, AT_DK_STAGED))
-        for m in range(1, BLOCKS):
+        put("dv3", dv[3], windows[3], out_1, 3, AT_DS_ROWS)
+        qm_mx.append(quantise("qm1", weave_half("qm1", qm_rows, HALF, nc.scalar.copy, AT_QM_LATE), E4M3))
+        for m in range(BLOCKS):
             bank = product("dk%d" % m, "front", qm_mx[m // HALF_BLOCKS], m % HALF_BLOCKS, ds_mx)
             put("dk%d" % m, bank, windows[(BLOCKS + m) % WINDOWS], out_0, m)

@@ -24,7 +24,7 @@ BAND = 16
 ALIGN = 64
 BLOCKS = DV // P
 WINDOWS = BLOCKS + 1
-PW_SHARE = 288
+PW_SHARE = 384
 DS_SHARE = 208
 HALF = DV // 2
 HALF_BLOCKS = HALF // P
@@ -69,11 +69,12 @@ def tile_attend_gat_sig_kv_kernel(tc, qT, kT, vT, doT, rw, qm, dom, offs, out_0,
         q_rows = load_rows("q", qT[0])
         v_planes = [load_plane("v", vT, 0)]
         dom_early_rows = load_rows("dom_early", dom[0][:, :HALF])
-        v_planes.extend(load_plane("v", vT, t) for t in range(1, LAST))
+        v_planes.append(load_plane("v", vT, 1))
         do_rows = load_rows("do", doT[0])
+        v_planes.append(load_plane("v", vT, 2))
         v_planes.append(load_plane("v", vT, LAST, AT_LAST_PLANE))
         dom_late_rows = load_rows("dom_late", dom[0][:, HALF:])
-        qm_rows = load_rows("qm", qm[0])
+        qm_rows = [load_rows("qm%d" % h, qm[0][:, h * HALF : (h + 1) * HALF]) for h in range(2)]
 
         windows = []
         for w in range(WINDOWS):
@@ -83,6 +84,8 @@ def tile_attend_gat_sig_kv_kernel(tc, qT, kT, vT, doT, rw, qm, dom, offs, out_0,
             windows.append(window)
         minus_gate = held.tile([P, PACK], F32, name="minus_gate")
         nc.vector.tensor_scalar(minus_gate[:], gate[:], -1.0, None, MULT)
+
+        seen = {}
 
         def new_woven(name, width=N, at=None):
             return new_tile(name + "_woven", [P, width, PACK], BF16, at)
@@ -136,6 +139,7 @@ def tile_attend_gat_sig_kv_kernel(tc, qT, kT, vT, doT, rw, qm, dom, offs, out_0,
         def put(name, bank, window, out, m, at=None):
             staged = new_tile(name + "_staged", [P, N], F32, at)
             nc.scalar.copy(staged[:], bank[:])
+            seen[name] = staged
             nc.vector.tensor_copy(window[:].indirect(offsets[:]), staged[:])
             nc.sync.dma_start(out[m * P : (m + 1) * P, :], window[:])
 
@@ -156,15 +160,18 @@ def tile_attend_gat_sig_kv_kernel(tc, qT, kT, vT, doT, rw, qm, dom, offs, out_0,
             nc.scalar.activation(prob[:, j, :], scores[j][:], ACT.Sigmoid)
         for j in range(PACK):
             nc.scalar.activation(pw_rows[:, j, :], prob[:, j, :], ACT.Copy, scale=gate[:, j : j + 1])
-        pw_mx = quantise("pw", weave_shared("pw", pw_rows, PW_SHARE), E4M3)
+        pw_woven = weave_shared("pw", pw_rows, PW_SHARE)
+        pw_mx = quantise("pw", pw_woven, E4M3)
         dv = [product("dv%d" % m, "back", dom_early_mx, m, pw_mx) for m in range(HALF_BLOCKS)]
 
-        v_rows = new_tile("v_rows", [P, LAST, N], BF16)
-        for t in range(LAST):
-            nc.vector.tensor_copy(v_rows[:, t, :], v_planes[t][:].indirect(offsets[:]))
+        v_pairs = new_tile("v_pairs", [P, 2, N, 2], BF16)
+        for t in range(PACK):
+            nc.vector.tensor_copy(v_pairs[:, t // 2, :, t % 2], v_planes[t][:].indirect(offsets[:]))
         v_woven = new_woven("v")
-        weave_into(v_woven[:, :, :LAST], v_rows[:], nc.vector.tensor_copy)
-        nc.vector.tensor_copy(v_woven[:, :, LAST], v_planes[LAST][:].indirect(offsets[:]))
+        nc.vector.tensor_copy(
+            v_woven[:].rearrange("p c t -> p (c t)").bitcast(I32).rearrange("p (c u) -> p c u", u=2),
+            v_pairs[:].rearrange("p u c e -> p (u c e)").bitcast(I32).rearrange("p (u c) -> p c u", u=2),
+        )
 
         minus_slopes = []
         for j in range(PACK):
@@ -178,7 +185,7 @@ def tile_attend_gat_sig_kv_kernel(tc, qT, kT, vT, doT, rw, qm, dom, offs, out_0,
         for m in range(HALF_BLOCKS):
             put("dv%d" % m, dv[m], windows[m], out_1, m, AT_LAST_PLANE + m * BANK_BYTES)
         dom_late_mx = quantise("dom_late", weave_half("dom_late", dom_late_rows, 0, nc.scalar.copy, AT_DOM_LATE), E5M2)
-        qm_woven = weave_half("qm0", qm_rows, 0, nc.scalar.copy)
+        qm_woven = weave_half("qm0", qm_rows[0], 0, nc.scalar.copy)
 
         ds_rows = new_tile("ds_rows", [P, PACK, N], BF16, AT_DS_ROWS)
         for j in range(PACK):
@@ -192,7 +199,7 @@ def tile_attend_gat_sig_kv_kernel(tc, qT, kT, vT, doT, rw, qm, dom, offs, out_0,
         qm_mx = [quantise("qm0", qm_woven, E4M3)]
         ds_mx = quantise("ds", ds_woven, E5M2)
         put("dv3", dv[3], windows[3], out_1, 3, AT_DS_ROWS)
-        qm_mx.append(quantise("qm1", weave_half("qm1", qm_rows, HALF, nc.scalar.copy, AT_QM_LATE), E4M3))
+        qm_mx.append(quantise("qm1", weave_half("qm1", qm_rows[1], 0, nc.scalar.copy, AT_QM_LATE), E4M3))
         for m in range(BLOCKS):
             bank = product("dk%d" % m, "front", qm_mx[m // HALF_BLOCKS], m % HALF_BLOCKS, ds_mx)
             put("dk%d" % m, bank, windows[(BLOCKS + m) % WINDOWS], out_0, m)

@@ -25,7 +25,8 @@ ALIGN = 64
 BLOCKS = DV // P
 WINDOWS = BLOCKS + 1
 PW_SHARE = 384
-DS_SHARE = 208
+DS_SHARE = 224
+V_SHARE = 384
 HALF = DV // 2
 HALF_BLOCKS = HALF // P
 PLANE_BYTES = T * 4
@@ -33,9 +34,8 @@ BANK_BYTES = N * 4
 
 AT_LAST_PLANE = 0
 AT_DO_CODES = AT_LAST_PLANE + HALF_BLOCKS * BANK_BYTES
-AT_DOM_LATE = PLANE_BYTES
-AT_DS_ROWS = AT_DOM_LATE
-AT_QM_LATE = AT_DS_ROWS + BANK_BYTES
+AT_LATE_ROWS = PLANE_BYTES
+AT_LAST_SLOPE = AT_LATE_ROWS + 2 * BANK_BYTES
 
 
 def tile_attend_gat_sig_kv_kernel(tc, qT, kT, vT, doT, rw, qm, dom, offs, out_0, out_1):
@@ -50,8 +50,8 @@ def tile_attend_gat_sig_kv_kernel(tc, qT, kT, vT, doT, rw, qm, dom, offs, out_0,
                 return held.tile(shape, dtype, name=name, align_bytes=ALIGN)
             return shared.tile(shape, dtype, name=name, offset=at, align_bytes=ALIGN)
 
-        def load_rows(name, src):
-            rows = new_tile(name + "_rows", [P, PACK, src.shape[1]], F32)
+        def load_rows(name, src, at=None):
+            rows = new_tile(name + "_rows", [P, PACK, src.shape[1]], F32, at)
             nc.sync.dma_start(rows[:], src.rearrange("(p t) c -> p t c", t=PACK))
             return rows
 
@@ -73,7 +73,7 @@ def tile_attend_gat_sig_kv_kernel(tc, qT, kT, vT, doT, rw, qm, dom, offs, out_0,
         do_rows = load_rows("do", doT[0])
         v_planes.append(load_plane("v", vT, 2))
         v_planes.append(load_plane("v", vT, LAST, AT_LAST_PLANE))
-        dom_late_rows = load_rows("dom_late", dom[0][:, HALF:])
+        dom_late_rows = load_rows("dom_late", dom[0][:, HALF:], AT_LATE_ROWS)
         qm_rows = [load_rows("qm%d" % h, qm[0][:, h * HALF : (h + 1) * HALF]) for h in range(2)]
 
         windows = []
@@ -164,18 +164,14 @@ def tile_attend_gat_sig_kv_kernel(tc, qT, kT, vT, doT, rw, qm, dom, offs, out_0,
         pw_mx = quantise("pw", pw_woven, E4M3)
         dv = [product("dv%d" % m, "back", dom_early_mx, m, pw_mx) for m in range(HALF_BLOCKS)]
 
-        v_pairs = new_tile("v_pairs", [P, 2, N, 2], BF16)
+        v_rows = new_tile("v_rows", [P, PACK, N], BF16)
         for t in range(PACK):
-            nc.vector.tensor_copy(v_pairs[:, t // 2, :, t % 2], v_planes[t][:].indirect(offsets[:]))
-        v_woven = new_woven("v")
-        nc.vector.tensor_copy(
-            v_woven[:].rearrange("p c t -> p (c t)").bitcast(I32).rearrange("p (c u) -> p c u", u=2),
-            v_pairs[:].rearrange("p u c e -> p (u c e)").bitcast(I32).rearrange("p (u c) -> p c u", u=2),
-        )
+            nc.vector.tensor_copy(v_rows[:, t, :], v_planes[t][:].indirect(offsets[:]))
+        v_woven = weave_shared("v", v_rows, V_SHARE)
 
         minus_slopes = []
         for j in range(PACK):
-            minus_slope = new_tile("minus_slope%d" % j, [P, N], F32)
+            minus_slope = new_tile("minus_slope%d" % j, [P, N], F32, AT_LAST_SLOPE if j == LAST else None)
             nc.vector.scalar_tensor_tensor(minus_slope[:], prob[:, j, :], 1.0, prob[:, j, :], SUBTRACT, MULT)
             minus_slopes.append(minus_slope)
 
@@ -184,10 +180,10 @@ def tile_attend_gat_sig_kv_kernel(tc, qT, kT, vT, doT, rw, qm, dom, offs, out_0,
         v_mx = quantise("v", v_woven, E4M3)
         for m in range(HALF_BLOCKS):
             put("dv%d" % m, dv[m], windows[m], out_1, m, AT_LAST_PLANE + m * BANK_BYTES)
-        dom_late_mx = quantise("dom_late", weave_half("dom_late", dom_late_rows, 0, nc.scalar.copy, AT_DOM_LATE), E5M2)
+        dom_late_mx = quantise("dom_late", weave_half("dom_late", dom_late_rows, 0, nc.scalar.copy), E5M2)
         qm_woven = weave_half("qm0", qm_rows[0], 0, nc.scalar.copy)
 
-        ds_rows = new_tile("ds_rows", [P, PACK, N], BF16, AT_DS_ROWS)
+        ds_rows = new_tile("ds_rows", [P, PACK, N], BF16, AT_LATE_ROWS)
         for j in range(PACK):
             dp = product("dp%d" % j, "front", do_mx[j // HALF_BLOCKS], j % HALF_BLOCKS, v_mx)
             nc.vector.scalar_tensor_tensor(
@@ -198,8 +194,8 @@ def tile_attend_gat_sig_kv_kernel(tc, qT, kT, vT, doT, rw, qm, dom, offs, out_0,
         ds_woven = weave_shared("ds", ds_rows, DS_SHARE)
         qm_mx = [quantise("qm0", qm_woven, E4M3)]
         ds_mx = quantise("ds", ds_woven, E5M2)
-        put("dv3", dv[3], windows[3], out_1, 3, AT_DS_ROWS)
-        qm_mx.append(quantise("qm1", weave_half("qm1", qm_rows[1], 0, nc.scalar.copy, AT_QM_LATE), E4M3))
+        put("dv3", dv[3], windows[3], out_1, 3, AT_LAST_SLOPE)
+        qm_mx.append(quantise("qm1", weave_half("qm1", qm_rows[1], 0, nc.scalar.copy, AT_LATE_ROWS), E4M3))
         for m in range(BLOCKS):
             bank = product("dk%d" % m, "front", qm_mx[m // HALF_BLOCKS], m % HALF_BLOCKS, ds_mx)
             put("dk%d" % m, bank, windows[(BLOCKS + m) % WINDOWS], out_0, m)

@@ -165,8 +165,11 @@ def tile_attend_gat_sig_kv_kernel(tc, qT, kT, vT, doT, rw, qm, dom, offs, out_0,
         dv = [product("dv%d" % m, "back", dom_early_mx, m, pw_mx) for m in range(HALF_BLOCKS)]
 
         v_rows = new_tile("v_rows", [P, PACK, N], BF16)
-        for t in range(PACK):
+        for t in range(LAST):
             nc.vector.tensor_copy(v_rows[:, t, :], v_planes[t][:].indirect(offsets[:]))
+        for first, end in ((0, V_SHARE), (V_SHARE, N)):
+            part = offsets[:, first // BAND : end // BAND]
+            nc.vector.tensor_copy(v_rows[:, LAST, first:end], v_planes[LAST][:].indirect(part))
         v_woven = weave_shared("v", v_rows, V_SHARE)
 
         minus_slopes = []

@@ -36,6 +36,7 @@ AT_LAST_PLANE = 0
 AT_DO_CODES = AT_LAST_PLANE + HALF_BLOCKS * BANK_BYTES
 AT_LATE_ROWS = PLANE_BYTES
 AT_LAST_SLOPE = AT_LATE_ROWS + 2 * BANK_BYTES
+AT_DV_STAGED = AT_LAST_SLOPE + BANK_BYTES
 
 
 def tile_attend_gat_sig_kv_kernel(tc, qT, kT, vT, doT, rw, qm, dom, offs, out_0, out_1):
@@ -193,9 +194,9 @@ def tile_attend_gat_sig_kv_kernel(tc, qT, kT, vT, doT, rw, qm, dom, offs, out_0,
                 ds_rows[:, j, :], dp[:], minus_gate[:, j : j + 1], minus_slopes[j][:], MULT, MULT
             )
         dv.extend(product("dv%d" % (HALF_BLOCKS + m), "back", dom_late_mx, m, pw_mx) for m in range(HALF_BLOCKS))
-        put("dv2", dv[2], windows[2], out_1, 2)
+        put("dv2", dv[2], windows[2], out_1, 2, AT_DV_STAGED)
         ds_woven = weave_shared("ds", ds_rows, DS_SHARE)
-        qm_mx = [quantise("qm0", qm_woven, E4M3)]
+        qm_mx = [quantise("qm0", qm_woven, E4M3, AT_DV_STAGED)]
         ds_mx = quantise("ds", ds_woven, E5M2)
         put("dv3", dv[3], windows[3], out_1, 3, AT_LAST_SLOPE)
         qm_mx.append(quantise("qm1", weave_half("qm1", qm_rows[1], 0, nc.scalar.copy, AT_LATE_ROWS), E4M3))

@@ -24,8 +24,8 @@ BAND = 16
 ALIGN = 64
 BLOCKS = DV // P
 WINDOWS = BLOCKS + 1
-PW_SHARE = 384
-DS_SHARE = 224
+PW_SHARE = 352
+DS_SHARE = 272
 V_SHARE = 384
 HALF = DV // 2
 HALF_BLOCKS = HALF // P
@@ -159,7 +159,8 @@ def tile_attend_gat_sig_kv_kernel(tc, qT, kT, vT, doT, rw, qm, dom, offs, out_0,
         dom_early_mx = quantise("dom_early", weave_half("dom_early", dom_early_rows, 0, nc.vector.tensor_copy), E5M2)
         for j in range(PACK):
             nc.scalar.activation(prob[:, j, :], scores[j][:], ACT.Sigmoid)
-        for j in range(PACK):
+        nc.vector.tensor_scalar(pw_rows[:, 0, :], prob[:, 0, :], gate[:, 0:1], None, MULT)
+        for j in range(1, PACK):
             nc.scalar.activation(pw_rows[:, j, :], prob[:, j, :], ACT.Copy, scale=gate[:, j : j + 1])
         pw_woven = weave_shared("pw", pw_rows, PW_SHARE)
         pw_mx = quantise("pw", pw_woven, E4M3)

@@ -25,7 +25,6 @@ ALIGN = 64
 BLOCKS = DV // P
 WINDOWS = BLOCKS + 1
 PW_SHARE = 352
-DS_SHARE = 272
 V_SHARE = 384
 HALF = DV // 2
 HALF_BLOCKS = HALF // P
@@ -34,9 +33,10 @@ BANK_BYTES = N * 4
 
 AT_LAST_PLANE = 0
 AT_DO_CODES = AT_LAST_PLANE + HALF_BLOCKS * BANK_BYTES
-AT_LATE_ROWS = PLANE_BYTES
-AT_LAST_SLOPE = AT_LATE_ROWS + 2 * BANK_BYTES
-AT_DV_STAGED = AT_LAST_SLOPE + BANK_BYTES
+AT_LAST_SLOPE = PLANE_BYTES
+AT_DV_STAGED = AT_LAST_SLOPE + 2 * BANK_BYTES
+AT_QM_LATE = AT_DV_STAGED + (PACK + 1) * HALF
+AT_LATE_ROWS = AT_DV_STAGED + 2 * BANK_BYTES
 
 
 def tile_attend_gat_sig_kv_kernel(tc, qT, kT, vT, doT, rw, qm, dom, offs, out_0, out_1):
@@ -106,15 +106,18 @@ def tile_attend_gat_sig_kv_kernel(tc, qT, kT, vT, doT, rw, qm, dom, offs, out_0,
             )
             return woven
 
-        def weave_into(woven, rows, copy):
-            copy(
-                woven.rearrange("p (c i) t -> p c t i", i=PACK),
-                rows.rearrange("p t (c i) -> p c t i", i=PACK),
-            )
+        def walk_woven(woven, run):
+            return woven.rearrange("p (c i) t -> p c t i", i=run)
 
-        def weave_half(name, rows, first, copy, at=None):
+        def walk_rows(rows, run):
+            return rows.rearrange("p t (c i) -> p c t i", i=run)
+
+        def weave_into(woven, rows, copy, run=PACK):
+            copy(walk_woven(woven, run), walk_rows(rows, run))
+
+        def weave_half(name, rows, copy, at=None):
             woven = new_woven(name, HALF, at)
-            weave_into(woven[:], rows[:, :, first : first + HALF], copy)
+            weave_into(woven[:], rows[:], copy, 2)
             return woven
 
         def weave_shared(name, rows, share):
@@ -123,18 +126,21 @@ def tile_attend_gat_sig_kv_kernel(tc, qT, kT, vT, doT, rw, qm, dom, offs, out_0,
             weave_into(woven[:, share:, :], rows[:, :, share:], nc.scalar.copy)
             return woven
 
-        def product(name, tag, stationary, m, moving):
-            bank = psum.tile([P, N], F32, name=name, tag=tag)
+        def multiply(out, stationary, m, moving, slots):
             cols = slice(m * P, (m + 1) * P)
             nc.tensor.matmul_mx(
-                out=bank[:],
+                out=out,
                 lhsT=stationary[0][:, cols].bitcast(stationary[2]),
                 lhsT_scale=stationary[1][:, cols],
-                rhs=moving[0][:].bitcast(moving[2]),
-                rhs_scale=moving[1][:],
+                rhs=moving[0][:, slots].bitcast(moving[2]),
+                rhs_scale=moving[1][:, slots],
                 start=True,
                 stop=True,
             )
+
+        def product(name, tag, stationary, m, moving):
+            bank = psum.tile([P, N], F32, name=name, tag=tag)
+            multiply(bank[:], stationary, m, moving, slice(0, N))
             return bank
 
         def put(name, bank, window, out, m, at=None):
@@ -144,10 +150,29 @@ def tile_attend_gat_sig_kv_kernel(tc, qT, kT, vT, doT, rw, qm, dom, offs, out_0,
             nc.vector.tensor_copy(window[:].indirect(offsets[:]), staged[:])
             nc.sync.dma_start(out[m * P : (m + 1) * P, :], window[:])
 
-        k_woven = new_woven("k")
-        for t in range(PACK):
-            nc.vector.tensor_copy(k_woven[:, :, t], k_planes[t][:].indirect(offsets[:]))
-        k_mx = quantise("k", k_woven, E4M3)
+        k_rows = new_tile("k_rows", [P, PACK, N], BF16)
+        k_woven = [new_woven("k%d" % h, N // 2) for h in range(2)]
+        halves = [slice(0, N // 2), slice(N // 2, N)]
+
+        def weave_pair(places):
+            for h in range(2):
+                nc.vector.tensor_copy(k_woven[h][:, :, places], k_rows[:, places, halves[h]].rearrange("p t c -> p c t"))
+
+        for t in range(2):
+            nc.vector.tensor_copy(k_rows[:, t, :], k_planes[t][:].indirect(offsets[:]))
+        weave_pair(slice(0, 2))
+        nc.vector.tensor_copy(k_rows[:, 2, :], k_planes[2][:].indirect(offsets[:]))
+        for h in range(2):
+            part = offsets[:, h * N // 2 // BAND : (h + 1) * N // 2 // BAND]
+            nc.vector.tensor_copy(k_rows[:, LAST, halves[h]], k_planes[LAST][:].indirect(part))
+        weave_pair(slice(2, PACK))
+        k_mx = (new_tile("k_words", [P, N], U32), new_tile("k_scales", [P, N], U8), E4M3)
+        for h in range(2):
+            nc.vector.quantize_mx(
+                out=k_mx[0][:, halves[h]].bitcast(E4M3),
+                scales=k_mx[1][:, halves[h]],
+                in_=k_woven[h][:].rearrange("p c t -> p (c t)"),
+            )
         q_woven = [
             weave_dealt("q%d" % h, q_rows, h * HALF_BLOCKS, HALF_BLOCKS, nc.vector.tensor_copy) for h in range(2)
         ]
@@ -155,14 +180,30 @@ def tile_attend_gat_sig_kv_kernel(tc, qT, kT, vT, doT, rw, qm, dom, offs, out_0,
         scores = [product("score%d" % j, "front", q_mx[j // HALF_BLOCKS], j % HALF_BLOCKS, k_mx) for j in range(PACK)]
 
         prob = held.tile([P, PACK, N], F32, name="prob")
-        pw_rows = new_tile("pw_rows", [P, PACK, N], BF16)
-        dom_early_mx = quantise("dom_early", weave_half("dom_early", dom_early_rows, 0, nc.vector.tensor_copy), E5M2)
+        minus_pw = held.tile([P, PACK, N], F32, name="minus_pw")
+        slopes = [new_tile("slope%d" % h, [P, PACK, N // 2], F32, AT_LAST_SLOPE if h else None) for h in range(2)]
+
+        def slope(pair):
+            places = slice(2 * pair, 2 * pair + 2)
+            for h in range(2):
+                nc.vector.scalar_tensor_tensor(
+                    slopes[h][:, places, :], prob[:, places, halves[h]], 1.0, minus_pw[:, places, halves[h]], SUBTRACT, MULT
+                )
+
         for j in range(PACK):
             nc.scalar.activation(prob[:, j, :], scores[j][:], ACT.Sigmoid)
-        nc.vector.tensor_scalar(pw_rows[:, 0, :], prob[:, 0, :], gate[:, 0:1], None, MULT)
-        for j in range(1, PACK):
-            nc.scalar.activation(pw_rows[:, j, :], prob[:, j, :], ACT.Copy, scale=gate[:, j : j + 1])
-        pw_woven = weave_shared("pw", pw_rows, PW_SHARE)
+        for j in range(2):
+            nc.vector.tensor_scalar(minus_pw[:, j, :], prob[:, j, :], minus_gate[:, j : j + 1], None, MULT)
+        for j in range(2, PACK):
+            nc.scalar.activation(minus_pw[:, j, :], prob[:, j, :], ACT.Copy, scale=minus_gate[:, j : j + 1])
+        dom_early_mx = quantise("dom_early", weave_half("dom_early", dom_early_rows, nc.vector.tensor_copy), E5M2)
+        pw_woven = new_woven("pw")
+        nc.vector.tensor_scalar(
+            walk_woven(pw_woven[:, :PW_SHARE, :], 2), walk_rows(minus_pw[:, :, :PW_SHARE], 2), -1.0, None, MULT
+        )
+        nc.scalar.activation(
+            walk_woven(pw_woven[:, PW_SHARE:, :], 2), walk_rows(minus_pw[:, :, PW_SHARE:], 2), ACT.Copy, scale=-1.0
+        )
         pw_mx = quantise("pw", pw_woven, E4M3)
         dv = [product("dv%d" % m, "back", dom_early_mx, m, pw_mx) for m in range(HALF_BLOCKS)]
 
@@ -174,33 +215,33 @@ def tile_attend_gat_sig_kv_kernel(tc, qT, kT, vT, doT, rw, qm, dom, offs, out_0,
             nc.vector.tensor_copy(v_rows[:, LAST, first:end], v_planes[LAST][:].indirect(part))
         v_woven = weave_shared("v", v_rows, V_SHARE)
 
-        minus_slopes = []
-        for j in range(PACK):
-            minus_slope = new_tile("minus_slope%d" % j, [P, N], F32, AT_LAST_SLOPE if j == LAST else None)
-            nc.vector.scalar_tensor_tensor(minus_slope[:], prob[:, j, :], 1.0, prob[:, j, :], SUBTRACT, MULT)
-            minus_slopes.append(minus_slope)
+        for pair in range(2):
+            slope(pair)
 
         do_woven = [weave_dealt("do%d" % h, do_rows, h * HALF_BLOCKS, HALF_BLOCKS, nc.scalar.copy) for h in range(2)]
         do_mx = [quantise("do0", do_woven[0], E5M2), quantise("do1", do_woven[1], E5M2, AT_DO_CODES)]
         v_mx = quantise("v", v_woven, E4M3)
         for m in range(HALF_BLOCKS):
             put("dv%d" % m, dv[m], windows[m], out_1, m, AT_LAST_PLANE + m * BANK_BYTES)
-        dom_late_mx = quantise("dom_late", weave_half("dom_late", dom_late_rows, 0, nc.scalar.copy), E5M2)
-        qm_woven = weave_half("qm0", qm_rows[0], 0, nc.scalar.copy)
+        dom_late_mx = quantise("dom_late", weave_half("dom_late", dom_late_rows, nc.scalar.copy), E5M2)
+        qm_woven = weave_half("qm0", qm_rows[0], nc.scalar.copy)
 
-        ds_rows = new_tile("ds_rows", [P, PACK, N], BF16, AT_LATE_ROWS)
-        for j in range(PACK):
-            dp = product("dp%d" % j, "front", do_mx[j // HALF_BLOCKS], j % HALF_BLOCKS, v_mx)
-            nc.vector.scalar_tensor_tensor(
-                ds_rows[:, j, :], dp[:], minus_gate[:, j : j + 1], minus_slopes[j][:], MULT, MULT
+        ds_woven = new_woven("ds", N, AT_LATE_ROWS)
+        for b in range(PACK):
+            dp = psum.tile([P, PACK, P], F32, name="dp%d" % b, tag="front")
+            slots = slice(b * P, (b + 1) * P)
+            within = slice((b % 2) * P, (b % 2 + 1) * P)
+            for j in range(PACK):
+                multiply(dp[:, j, :], do_mx[j // HALF_BLOCKS], j % HALF_BLOCKS, v_mx, slots)
+            nc.vector.tensor_tensor(
+                walk_woven(ds_woven[:, slots, :], 2), walk_rows(dp[:], 2), walk_rows(slopes[b // 2][:, :, within], 2), MULT
             )
         dv.extend(product("dv%d" % (HALF_BLOCKS + m), "back", dom_late_mx, m, pw_mx) for m in range(HALF_BLOCKS))
         put("dv2", dv[2], windows[2], out_1, 2, AT_DV_STAGED)
-        ds_woven = weave_shared("ds", ds_rows, DS_SHARE)
-        qm_mx = [quantise("qm0", qm_woven, E4M3, AT_DV_STAGED)]
         ds_mx = quantise("ds", ds_woven, E5M2)
+        qm_mx = [quantise("qm0", qm_woven, E4M3, AT_DV_STAGED)]
         put("dv3", dv[3], windows[3], out_1, 3, AT_LAST_SLOPE)
-        qm_mx.append(quantise("qm1", weave_half("qm1", qm_rows[1], 0, nc.scalar.copy, AT_LATE_ROWS), E4M3))
+        qm_mx.append(quantise("qm1", weave_half("qm1", qm_rows[1], nc.scalar.copy, AT_QM_LATE), E4M3, AT_LAST_SLOPE))
         for m in range(BLOCKS):
             bank = product("dk%d" % m, "front", qm_mx[m // HALF_BLOCKS], m % HALF_BLOCKS, ds_mx)
             put("dk%d" % m, bank, windows[(BLOCKS + m) % WINDOWS], out_0, m)

@@ -25,9 +25,12 @@ ALIGN = 64
 BLOCKS = DV // P
 WINDOWS = BLOCKS + 1
 PW_SHARE = 352
-V_SHARE = 384
 HALF = DV // 2
 HALF_BLOCKS = HALF // P
+SLOT_HALVES = [slice(0, N // 2), slice(N // 2, N)]
+FIRST_PAIR, SECOND_PAIR = slice(0, 2), slice(2, PACK)
+VECTOR_GATES = 2
+RUN = 2
 PLANE_BYTES = T * 4
 BANK_BYTES = N * 4
 
@@ -37,6 +40,7 @@ AT_LAST_SLOPE = PLANE_BYTES
 AT_DV_STAGED = AT_LAST_SLOPE + 2 * BANK_BYTES
 AT_QM_LATE = AT_DV_STAGED + (PACK + 1) * HALF
 AT_LATE_ROWS = AT_DV_STAGED + 2 * BANK_BYTES
+AT_DO_ROWS = AT_LATE_ROWS + 2 * BANK_BYTES
 
 
 def tile_attend_gat_sig_kv_kernel(tc, qT, kT, vT, doT, rw, qm, dom, offs, out_0, out_1):
@@ -71,7 +75,7 @@ def tile_attend_gat_sig_kv_kernel(tc, qT, kT, vT, doT, rw, qm, dom, offs, out_0,
         v_planes = [load_plane("v", vT, 0)]
         dom_early_rows = load_rows("dom_early", dom[0][:, :HALF])
         v_planes.append(load_plane("v", vT, 1))
-        do_rows = load_rows("do", doT[0])
+        do_rows = load_rows("do", doT[0], AT_DO_ROWS)
         v_planes.append(load_plane("v", vT, 2))
         v_planes.append(load_plane("v", vT, LAST, AT_LAST_PLANE))
         dom_late_rows = load_rows("dom_late", dom[0][:, HALF:], AT_LATE_ROWS)
@@ -86,8 +90,6 @@ def tile_attend_gat_sig_kv_kernel(tc, qT, kT, vT, doT, rw, qm, dom, offs, out_0,
         minus_gate = held.tile([P, PACK], F32, name="minus_gate")
         nc.vector.tensor_scalar(minus_gate[:], gate[:], -1.0, None, MULT)
 
-        seen = {}
-
         def new_woven(name, width=N, at=None):
             return new_tile(name + "_woven", [P, width, PACK], BF16, at)
 
@@ -95,7 +97,8 @@ def tile_attend_gat_sig_kv_kernel(tc, qT, kT, vT, doT, rw, qm, dom, offs, out_0,
             width = woven.shape[1]
             words = new_tile(name + "_words", [P, width], U32, at)
             scales = new_tile(name + "_scales", [P, width], U8, None if at is None else at + PACK * width)
-            nc.vector.quantize_mx(out=words[:].bitcast(fmt), scales=scales[:], in_=woven[:].rearrange("p c t -> p (c t)"))
+            flat = woven[:].rearrange("p c t -> p (c t)")
+            nc.vector.quantize_mx(out=words[:].bitcast(fmt), scales=scales[:], in_=flat)
             return words, scales, fmt
 
         def weave_dealt(name, rows, first, count, copy):
@@ -106,24 +109,15 @@ def tile_attend_gat_sig_kv_kernel(tc, qT, kT, vT, doT, rw, qm, dom, offs, out_0,
             )
             return woven
 
-        def walk_woven(woven, run):
-            return woven.rearrange("p (c i) t -> p c t i", i=run)
+        def walk_woven(woven):
+            return woven.rearrange("p (c i) t -> p c t i", i=RUN)
 
-        def walk_rows(rows, run):
-            return rows.rearrange("p t (c i) -> p c t i", i=run)
-
-        def weave_into(woven, rows, copy, run=PACK):
-            copy(walk_woven(woven, run), walk_rows(rows, run))
+        def walk_rows(rows):
+            return rows.rearrange("p t (c i) -> p c t i", i=RUN)
 
         def weave_half(name, rows, copy, at=None):
             woven = new_woven(name, HALF, at)
-            weave_into(woven[:], rows[:], copy, 2)
-            return woven
-
-        def weave_shared(name, rows, share):
-            woven = new_woven(name)
-            weave_into(woven[:, :share, :], rows[:, :, :share], nc.vector.tensor_copy)
-            weave_into(woven[:, share:, :], rows[:, :, share:], nc.scalar.copy)
+            copy(walk_woven(woven[:]), walk_rows(rows[:]))
             return woven
 
         def multiply(out, stationary, m, moving, slots):
@@ -146,31 +140,34 @@ def tile_attend_gat_sig_kv_kernel(tc, qT, kT, vT, doT, rw, qm, dom, offs, out_0,
         def put(name, bank, window, out, m, at=None):
             staged = new_tile(name + "_staged", [P, N], F32, at)
             nc.scalar.copy(staged[:], bank[:])
-            seen[name] = staged
             nc.vector.tensor_copy(window[:].indirect(offsets[:]), staged[:])
             nc.sync.dma_start(out[m * P : (m + 1) * P, :], window[:])
 
+        def gather(rows, planes, t):
+            nc.vector.tensor_copy(rows[:, t, :], planes[t][:].indirect(offsets[:]))
+
+        def gather_last(rows, planes):
+            for slots in SLOT_HALVES:
+                part = offsets[:, slots.start // BAND : slots.stop // BAND]
+                nc.vector.tensor_copy(rows[:, LAST, slots], planes[LAST][:].indirect(part))
+
+        def weave_pair(woven, rows, pair, copy):
+            for h, slots in enumerate(SLOT_HALVES):
+                copy(woven[h][:, :, pair], rows[:, pair, slots].rearrange("p t c -> p c t"))
+
         k_rows = new_tile("k_rows", [P, PACK, N], BF16)
         k_woven = [new_woven("k%d" % h, N // 2) for h in range(2)]
-        halves = [slice(0, N // 2), slice(N // 2, N)]
-
-        def weave_pair(places):
-            for h in range(2):
-                nc.vector.tensor_copy(k_woven[h][:, :, places], k_rows[:, places, halves[h]].rearrange("p t c -> p c t"))
-
-        for t in range(2):
-            nc.vector.tensor_copy(k_rows[:, t, :], k_planes[t][:].indirect(offsets[:]))
-        weave_pair(slice(0, 2))
-        nc.vector.tensor_copy(k_rows[:, 2, :], k_planes[2][:].indirect(offsets[:]))
-        for h in range(2):
-            part = offsets[:, h * N // 2 // BAND : (h + 1) * N // 2 // BAND]
-            nc.vector.tensor_copy(k_rows[:, LAST, halves[h]], k_planes[LAST][:].indirect(part))
-        weave_pair(slice(2, PACK))
+        gather(k_rows, k_planes, 0)
+        gather(k_rows, k_planes, 1)
+        weave_pair(k_woven, k_rows, FIRST_PAIR, nc.vector.tensor_copy)
+        gather(k_rows, k_planes, 2)
+        gather_last(k_rows, k_planes)
+        weave_pair(k_woven, k_rows, SECOND_PAIR, nc.vector.tensor_copy)
         k_mx = (new_tile("k_words", [P, N], U32), new_tile("k_scales", [P, N], U8), E4M3)
-        for h in range(2):
+        for h, slots in enumerate(SLOT_HALVES):
             nc.vector.quantize_mx(
-                out=k_mx[0][:, halves[h]].bitcast(E4M3),
-                scales=k_mx[1][:, halves[h]],
+                out=k_mx[0][:, slots].bitcast(E4M3),
+                scales=k_mx[1][:, slots],
                 in_=k_woven[h][:].rearrange("p c t -> p (c t)"),
             )
         q_woven = [
@@ -183,44 +180,40 @@ def tile_attend_gat_sig_kv_kernel(tc, qT, kT, vT, doT, rw, qm, dom, offs, out_0,
         minus_pw = held.tile([P, PACK, N], F32, name="minus_pw")
         slopes = [new_tile("slope%d" % h, [P, PACK, N // 2], F32, AT_LAST_SLOPE if h else None) for h in range(2)]
 
-        def slope(pair):
-            places = slice(2 * pair, 2 * pair + 2)
-            for h in range(2):
-                nc.vector.scalar_tensor_tensor(
-                    slopes[h][:, places, :], prob[:, places, halves[h]], 1.0, minus_pw[:, places, halves[h]], SUBTRACT, MULT
-                )
-
         for j in range(PACK):
             nc.scalar.activation(prob[:, j, :], scores[j][:], ACT.Sigmoid)
-        for j in range(2):
+        for j in range(VECTOR_GATES):
             nc.vector.tensor_scalar(minus_pw[:, j, :], prob[:, j, :], minus_gate[:, j : j + 1], None, MULT)
-        for j in range(2, PACK):
+        for j in range(VECTOR_GATES, PACK):
             nc.scalar.activation(minus_pw[:, j, :], prob[:, j, :], ACT.Copy, scale=minus_gate[:, j : j + 1])
         dom_early_mx = quantise("dom_early", weave_half("dom_early", dom_early_rows, nc.vector.tensor_copy), E5M2)
         pw_woven = new_woven("pw")
         nc.vector.tensor_scalar(
-            walk_woven(pw_woven[:, :PW_SHARE, :], 2), walk_rows(minus_pw[:, :, :PW_SHARE], 2), -1.0, None, MULT
+            walk_woven(pw_woven[:, :PW_SHARE, :]), walk_rows(minus_pw[:, :, :PW_SHARE]), -1.0, None, MULT
         )
         nc.scalar.activation(
-            walk_woven(pw_woven[:, PW_SHARE:, :], 2), walk_rows(minus_pw[:, :, PW_SHARE:], 2), ACT.Copy, scale=-1.0
+            walk_woven(pw_woven[:, PW_SHARE:, :]), walk_rows(minus_pw[:, :, PW_SHARE:]), ACT.Copy, scale=-1.0
         )
         pw_mx = quantise("pw", pw_woven, E4M3)
         dv = [product("dv%d" % m, "back", dom_early_mx, m, pw_mx) for m in range(HALF_BLOCKS)]
 
         v_rows = new_tile("v_rows", [P, PACK, N], BF16)
         for t in range(LAST):
-            nc.vector.tensor_copy(v_rows[:, t, :], v_planes[t][:].indirect(offsets[:]))
-        for first, end in ((0, V_SHARE), (V_SHARE, N)):
-            part = offsets[:, first // BAND : end // BAND]
-            nc.vector.tensor_copy(v_rows[:, LAST, first:end], v_planes[LAST][:].indirect(part))
-        v_woven = weave_shared("v", v_rows, V_SHARE)
-
-        for pair in range(2):
-            slope(pair)
+            gather(v_rows, v_planes, t)
+        for pair in (FIRST_PAIR, SECOND_PAIR):
+            for h, slots in enumerate(SLOT_HALVES):
+                nc.vector.scalar_tensor_tensor(
+                    slopes[h][:, pair, :], prob[:, pair, slots], 1.0, minus_pw[:, pair, slots], SUBTRACT, MULT
+                )
 
         do_woven = [weave_dealt("do%d" % h, do_rows, h * HALF_BLOCKS, HALF_BLOCKS, nc.scalar.copy) for h in range(2)]
-        do_mx = [quantise("do0", do_woven[0], E5M2), quantise("do1", do_woven[1], E5M2, AT_DO_CODES)]
-        v_mx = quantise("v", v_woven, E4M3)
+        do_mx = [quantise("do0", do_woven[0], E5M2)]
+        v_woven = [new_woven("v%d" % h, N // 2, AT_DO_ROWS + h * BANK_BYTES) for h in range(2)]
+        weave_pair(v_woven, v_rows, FIRST_PAIR, nc.scalar.copy)
+        gather_last(v_rows, v_planes)
+        weave_pair(v_woven, v_rows, SECOND_PAIR, nc.vector.tensor_copy)
+        do_mx.append(quantise("do1", do_woven[1], E5M2, AT_DO_CODES))
+        v_mx = [quantise("v%d" % h, v_woven[h], E4M3) for h in range(2)]
         for m in range(HALF_BLOCKS):
             put("dv%d" % m, dv[m], windows[m], out_1, m, AT_LAST_PLANE + m * BANK_BYTES)
         dom_late_mx = quantise("dom_late", weave_half("dom_late", dom_late_rows, nc.scalar.copy), E5M2)
@@ -232,9 +225,9 @@ def tile_attend_gat_sig_kv_kernel(tc, qT, kT, vT, doT, rw, qm, dom, offs, out_0,
             slots = slice(b * P, (b + 1) * P)
             within = slice((b % 2) * P, (b % 2 + 1) * P)
             for j in range(PACK):
-                multiply(dp[:, j, :], do_mx[j // HALF_BLOCKS], j % HALF_BLOCKS, v_mx, slots)
+                multiply(dp[:, j, :], do_mx[j // HALF_BLOCKS], j % HALF_BLOCKS, v_mx[b // 2], within)
             nc.vector.tensor_tensor(
-                walk_woven(ds_woven[:, slots, :], 2), walk_rows(dp[:], 2), walk_rows(slopes[b // 2][:, :, within], 2), MULT
+                walk_woven(ds_woven[:, slots, :]), walk_rows(dp[:]), walk_rows(slopes[b // 2][:, :, within]), MULT
             )
         dv.extend(product("dv%d" % (HALF_BLOCKS + m), "back", dom_late_mx, m, pw_mx) for m in range(HALF_BLOCKS))
         put("dv2", dv[2], windows[2], out_1, 2, AT_DV_STAGED)

@@ -24,44 +24,29 @@ BAND = 16
 ALIGN = 64
 BLOCKS = DV // P
 WINDOWS = BLOCKS + 1
-PW_SHARE = 352
 HALF = DV // 2
 HALF_BLOCKS = HALF // P
 SLOT_HALVES = [slice(0, N // 2), slice(N // 2, N)]
 FIRST_PAIR, SECOND_PAIR = slice(0, 2), slice(2, PACK)
-VECTOR_GATES = 2
 RUN = 2
-PLANE_BYTES = T * 4
-BANK_BYTES = N * 4
-
-AT_LAST_PLANE = 0
-AT_DO_CODES = AT_LAST_PLANE + HALF_BLOCKS * BANK_BYTES
-AT_LAST_SLOPE = PLANE_BYTES
-AT_DV_STAGED = AT_LAST_SLOPE + 2 * BANK_BYTES
-AT_QM_LATE = AT_DV_STAGED + (PACK + 1) * HALF
-AT_LATE_ROWS = AT_DV_STAGED + 2 * BANK_BYTES
-AT_DO_ROWS = AT_LATE_ROWS + 2 * BANK_BYTES
 
 
 def tile_attend_gat_sig_kv_kernel(tc, qT, kT, vT, doT, rw, qm, dom, offs, out_0, out_1):
     nc = tc.nc
     with ExitStack() as ctx:
         held = ctx.enter_context(tc.tile_pool(name="held", bufs=1))
-        shared = ctx.enter_context(tc.tile_pool(name="shared", bufs=1))
         psum = ctx.enter_context(tc.psum_pool(name="psum", bufs=PACK))
 
-        def new_tile(name, shape, dtype, at=None):
-            if at is None:
-                return held.tile(shape, dtype, name=name, align_bytes=ALIGN)
-            return shared.tile(shape, dtype, name=name, offset=at, align_bytes=ALIGN)
+        def new_tile(name, shape, dtype):
+            return held.tile(shape, dtype, name=name, align_bytes=ALIGN)
 
-        def load_rows(name, src, at=None):
-            rows = new_tile(name + "_rows", [P, PACK, src.shape[1]], F32, at)
+        def load_rows(name, src):
+            rows = new_tile(name + "_rows", [P, PACK, src.shape[1]], F32)
             nc.sync.dma_start(rows[:], src.rearrange("(p t) c -> p t c", t=PACK))
             return rows
 
-        def load_plane(name, table, t, at=None):
-            plane = new_tile("%s_plane%d" % (name, t), [P, T], F32, at)
+        def load_plane(name, table, t):
+            plane = new_tile("%s_plane%d" % (name, t), [P, T], F32)
             nc.sync.dma_start(plane[:], table.rearrange("(p t) c -> t p c", t=PACK)[t])
             return plane
 
@@ -72,14 +57,11 @@ def tile_attend_gat_sig_kv_kernel(tc, qT, kT, vT, doT, rw, qm, dom, offs, out_0,
         nc.sync.dma_start(gate[:], rw[0].rearrange("(p j) o -> p (j o)", j=PACK))
         k_planes.extend(load_plane("k", kT, t) for t in range(1, PACK))
         q_rows = load_rows("q", qT[0])
-        v_planes = [load_plane("v", vT, 0)]
-        dom_early_rows = load_rows("dom_early", dom[0][:, :HALF])
-        v_planes.append(load_plane("v", vT, 1))
-        do_rows = load_rows("do", doT[0], AT_DO_ROWS)
-        v_planes.append(load_plane("v", vT, 2))
-        v_planes.append(load_plane("v", vT, LAST, AT_LAST_PLANE))
-        dom_late_rows = load_rows("dom_late", dom[0][:, HALF:], AT_LATE_ROWS)
-        qm_rows = [load_rows("qm%d" % h, qm[0][:, h * HALF : (h + 1) * HALF]) for h in range(2)]
+        dom_rows = load_rows("dom", dom[0])
+        v_planes = [load_plane("v", vT, t) for t in range(2)]
+        do_rows = load_rows("do", doT[0])
+        v_planes.extend(load_plane("v", vT, t) for t in range(2, PACK))
+        qm_rows = load_rows("qm", qm[0])
 
         windows = []
         for w in range(WINDOWS):
@@ -90,22 +72,23 @@ def tile_attend_gat_sig_kv_kernel(tc, qT, kT, vT, doT, rw, qm, dom, offs, out_0,
         minus_gate = held.tile([P, PACK], F32, name="minus_gate")
         nc.vector.tensor_scalar(minus_gate[:], gate[:], -1.0, None, MULT)
 
-        def new_woven(name, width=N, at=None):
-            return new_tile(name + "_woven", [P, width, PACK], BF16, at)
+        def new_woven(name, width=N):
+            return new_tile(name + "_woven", [P, width, PACK], BF16)
 
-        def quantise(name, woven, fmt, at=None):
+        def quantise(name, woven, fmt):
             width = woven.shape[1]
-            words = new_tile(name + "_words", [P, width], U32, at)
-            scales = new_tile(name + "_scales", [P, width], U8, None if at is None else at + PACK * width)
+            words = new_tile(name + "_words", [P, width], U32)
+            scales = new_tile(name + "_scales", [P, width], U8)
             flat = woven[:].rearrange("p c t -> p (c t)")
             nc.vector.quantize_mx(out=words[:].bitcast(fmt), scales=scales[:], in_=flat)
             return words, scales, fmt
 
-        def weave_dealt(name, rows, first, count, copy):
-            woven = new_woven(name, count * P)
+        def weave_dealt(name, rows, h, copy):
+            woven = new_woven(name, HALF)
+            first = h * HALF_BLOCKS
             copy(
-                woven[:].rearrange("p (j s) t -> p s t j", j=count),
-                rows[:].rearrange("p t (s j) -> p s t j", j=PACK)[:, :, :, first : first + count],
+                woven[:].rearrange("p (j s) t -> p s t j", j=HALF_BLOCKS),
+                rows[:].rearrange("p t (s j) -> p s t j", j=PACK)[:, :, :, first : first + HALF_BLOCKS],
             )
             return woven
 
@@ -115,9 +98,9 @@ def tile_attend_gat_sig_kv_kernel(tc, qT, kT, vT, doT, rw, qm, dom, offs, out_0,
         def walk_rows(rows):
             return rows.rearrange("p t (c i) -> p c t i", i=RUN)
 
-        def weave_half(name, rows, copy, at=None):
-            woven = new_woven(name, HALF, at)
-            copy(walk_woven(woven[:]), walk_rows(rows[:]))
+        def weave_half(name, rows, h, copy):
+            woven = new_woven(name, HALF)
+            copy(walk_woven(woven[:]), walk_rows(rows[:, :, h * HALF : (h + 1) * HALF]))
             return woven
 
         def multiply(out, stationary, m, moving, slots):
@@ -132,37 +115,38 @@ def tile_attend_gat_sig_kv_kernel(tc, qT, kT, vT, doT, rw, qm, dom, offs, out_0,
                 stop=True,
             )
 
-        def product(name, tag, stationary, m, moving):
+        def product(name, tag, halves, m, moving):
             bank = psum.tile([P, N], F32, name=name, tag=tag)
-            multiply(bank[:], stationary, m, moving, slice(0, N))
+            multiply(bank[:], halves[m // HALF_BLOCKS], m % HALF_BLOCKS, moving, slice(0, N))
             return bank
 
-        def put(name, bank, window, out, m, at=None):
-            staged = new_tile(name + "_staged", [P, N], F32, at)
+        def listed(slots):
+            return offsets[:, slots.start // BAND : slots.stop // BAND]
+
+        def stage(name, bank):
+            staged = new_tile(name + "_staged", [P, N], F32)
             nc.scalar.copy(staged[:], bank[:])
-            nc.vector.tensor_copy(window[:].indirect(offsets[:]), staged[:])
-            nc.sync.dma_start(out[m * P : (m + 1) * P, :], window[:])
+            return staged
 
         def gather(rows, planes, t):
             nc.vector.tensor_copy(rows[:, t, :], planes[t][:].indirect(offsets[:]))
 
         def gather_last(rows, planes):
             for slots in SLOT_HALVES:
-                part = offsets[:, slots.start // BAND : slots.stop // BAND]
-                nc.vector.tensor_copy(rows[:, LAST, slots], planes[LAST][:].indirect(part))
+                nc.vector.tensor_copy(rows[:, LAST, slots], planes[LAST][:].indirect(listed(slots)))
 
-        def weave_pair(woven, rows, pair, copy):
+        def weave_pair(woven, rows, pair):
             for h, slots in enumerate(SLOT_HALVES):
-                copy(woven[h][:, :, pair], rows[:, pair, slots].rearrange("p t c -> p c t"))
+                nc.vector.tensor_copy(woven[h][:, :, pair], rows[:, pair, slots].rearrange("p t c -> p c t"))
 
         k_rows = new_tile("k_rows", [P, PACK, N], BF16)
         k_woven = [new_woven("k%d" % h, N // 2) for h in range(2)]
         gather(k_rows, k_planes, 0)
         gather(k_rows, k_planes, 1)
-        weave_pair(k_woven, k_rows, FIRST_PAIR, nc.vector.tensor_copy)
+        weave_pair(k_woven, k_rows, FIRST_PAIR)
         gather(k_rows, k_planes, 2)
         gather_last(k_rows, k_planes)
-        weave_pair(k_woven, k_rows, SECOND_PAIR, nc.vector.tensor_copy)
+        weave_pair(k_woven, k_rows, SECOND_PAIR)
         k_mx = (new_tile("k_words", [P, N], U32), new_tile("k_scales", [P, N], U8), E4M3)
         for h, slots in enumerate(SLOT_HALVES):
             nc.vector.quantize_mx(
@@ -170,56 +154,48 @@ def tile_attend_gat_sig_kv_kernel(tc, qT, kT, vT, doT, rw, qm, dom, offs, out_0,
                 scales=k_mx[1][:, slots],
                 in_=k_woven[h][:].rearrange("p c t -> p (c t)"),
             )
-        q_woven = [
-            weave_dealt("q%d" % h, q_rows, h * HALF_BLOCKS, HALF_BLOCKS, nc.vector.tensor_copy) for h in range(2)
-        ]
+        q_woven = [weave_dealt("q%d" % h, q_rows, h, nc.vector.tensor_copy) for h in range(2)]
         q_mx = [quantise("q%d" % h, q_woven[h], E4M3) for h in range(2)]
-        scores = [product("score%d" % j, "front", q_mx[j // HALF_BLOCKS], j % HALF_BLOCKS, k_mx) for j in range(PACK)]
+        scores = [product("score%d" % j, "front", q_mx, j, k_mx) for j in range(PACK)]
 
         prob = held.tile([P, PACK, N], F32, name="prob")
         minus_pw = held.tile([P, PACK, N], F32, name="minus_pw")
-        slopes = [new_tile("slope%d" % h, [P, PACK, N // 2], F32, AT_LAST_SLOPE if h else None) for h in range(2)]
-
         for j in range(PACK):
             nc.scalar.activation(prob[:, j, :], scores[j][:], ACT.Sigmoid)
-        for j in range(VECTOR_GATES):
-            nc.vector.tensor_scalar(minus_pw[:, j, :], prob[:, j, :], minus_gate[:, j : j + 1], None, MULT)
-        for j in range(VECTOR_GATES, PACK):
+        for j in range(PACK):
             nc.scalar.activation(minus_pw[:, j, :], prob[:, j, :], ACT.Copy, scale=minus_gate[:, j : j + 1])
-        dom_early_mx = quantise("dom_early", weave_half("dom_early", dom_early_rows, nc.vector.tensor_copy), E5M2)
         pw_woven = new_woven("pw")
-        nc.vector.tensor_scalar(
-            walk_woven(pw_woven[:, :PW_SHARE, :]), walk_rows(minus_pw[:, :, :PW_SHARE]), -1.0, None, MULT
-        )
-        nc.scalar.activation(
-            walk_woven(pw_woven[:, PW_SHARE:, :]), walk_rows(minus_pw[:, :, PW_SHARE:]), ACT.Copy, scale=-1.0
-        )
+        nc.scalar.activation(walk_woven(pw_woven[:]), walk_rows(minus_pw[:]), ACT.Copy, scale=-1.0)
+        dom_woven = [weave_half("dom%d" % h, dom_rows, h, nc.vector.tensor_copy) for h in range(2)]
+        dom_mx = [quantise("dom%d" % h, dom_woven[h], E5M2) for h in range(2)]
         pw_mx = quantise("pw", pw_woven, E4M3)
-        dv = [product("dv%d" % m, "back", dom_early_mx, m, pw_mx) for m in range(HALF_BLOCKS)]
+        dv = [product("dv%d" % m, "back", dom_mx, m, pw_mx) for m in range(BLOCKS)]
+        for m in range(BLOCKS):
+            staged = stage("dv%d" % m, dv[m])
+            for slots in SLOT_HALVES:
+                nc.scalar.activation(windows[m][:].indirect(listed(slots)), staged[:, slots], ACT.Copy)
+            nc.sync.dma_start(out_1[m * P : (m + 1) * P, :], windows[m][:])
 
         v_rows = new_tile("v_rows", [P, PACK, N], BF16)
-        for t in range(LAST):
-            gather(v_rows, v_planes, t)
+        v_woven = [new_woven("v%d" % h, N // 2) for h in range(2)]
+        gather(v_rows, v_planes, 0)
+        gather(v_rows, v_planes, 1)
+        weave_pair(v_woven, v_rows, FIRST_PAIR)
+        do_woven = [weave_dealt("do%d" % h, do_rows, h, nc.vector.tensor_copy) for h in range(2)]
+        do_mx = [quantise("do%d" % h, do_woven[h], E5M2) for h in range(2)]
+        gather(v_rows, v_planes, 2)
+        slopes = [new_tile("slope%d" % h, [P, PACK, N // 2], F32) for h in range(2)]
         for pair in (FIRST_PAIR, SECOND_PAIR):
             for h, slots in enumerate(SLOT_HALVES):
                 nc.vector.scalar_tensor_tensor(
                     slopes[h][:, pair, :], prob[:, pair, slots], 1.0, minus_pw[:, pair, slots], SUBTRACT, MULT
                 )
-
-        do_woven = [weave_dealt("do%d" % h, do_rows, h * HALF_BLOCKS, HALF_BLOCKS, nc.scalar.copy) for h in range(2)]
-        do_mx = [quantise("do0", do_woven[0], E5M2)]
-        v_woven = [new_woven("v%d" % h, N // 2, AT_DO_ROWS + h * BANK_BYTES) for h in range(2)]
-        weave_pair(v_woven, v_rows, FIRST_PAIR, nc.scalar.copy)
         gather_last(v_rows, v_planes)
-        weave_pair(v_woven, v_rows, SECOND_PAIR, nc.vector.tensor_copy)
-        do_mx.append(quantise("do1", do_woven[1], E5M2, AT_DO_CODES))
+        weave_pair(v_woven, v_rows, SECOND_PAIR)
         v_mx = [quantise("v%d" % h, v_woven[h], E4M3) for h in range(2)]
-        for m in range(HALF_BLOCKS):
-            put("dv%d" % m, dv[m], windows[m], out_1, m, AT_LAST_PLANE + m * BANK_BYTES)
-        dom_late_mx = quantise("dom_late", weave_half("dom_late", dom_late_rows, nc.scalar.copy), E5M2)
-        qm_woven = weave_half("qm0", qm_rows[0], nc.scalar.copy)
+        qm_woven = [weave_half("qm%d" % h, qm_rows, h, nc.scalar.copy) for h in range(2)]
 
-        ds_woven = new_woven("ds", N, AT_LATE_ROWS)
+        ds_woven = new_woven("ds")
         for b in range(PACK):
             dp = psum.tile([P, PACK, P], F32, name="dp%d" % b, tag="front")
             slots = slice(b * P, (b + 1) * P)
@@ -229,12 +205,11 @@ def tile_attend_gat_sig_kv_kernel(tc, qT, kT, vT, doT, rw, qm, dom, offs, out_0,
             nc.vector.tensor_tensor(
                 walk_woven(ds_woven[:, slots, :]), walk_rows(dp[:]), walk_rows(slopes[b // 2][:, :, within]), MULT
             )
-        dv.extend(product("dv%d" % (HALF_BLOCKS + m), "back", dom_late_mx, m, pw_mx) for m in range(HALF_BLOCKS))
-        put("dv2", dv[2], windows[2], out_1, 2, AT_DV_STAGED)
+        qm_mx = [quantise("qm0", qm_woven[0], E4M3)]
         ds_mx = quantise("ds", ds_woven, E5M2)
-        qm_mx = [quantise("qm0", qm_woven, E4M3, AT_DV_STAGED)]
-        put("dv3", dv[3], windows[3], out_1, 3, AT_LAST_SLOPE)
-        qm_mx.append(quantise("qm1", weave_half("qm1", qm_rows[1], nc.scalar.copy, AT_QM_LATE), E4M3, AT_LAST_SLOPE))
+        qm_mx.append(quantise("qm1", qm_woven[1], E4M3))
         for m in range(BLOCKS):
-            bank = product("dk%d" % m, "front", qm_mx[m // HALF_BLOCKS], m % HALF_BLOCKS, ds_mx)
-            put("dk%d" % m, bank, windows[(BLOCKS + m) % WINDOWS], out_0, m)
+            staged = stage("dk%d" % m, product("dk%d" % m, "front", qm_mx, m, ds_mx))
+            window = windows[(BLOCKS + m) % WINDOWS]
+            nc.vector.tensor_copy(window[:].indirect(offsets[:]), staged[:])
+            nc.sync.dma_start(out_0[m * P : (m + 1) * P, :], window[:])

@@ -171,9 +171,11 @@ def tile_attend_gat_sig_kv_kernel(tc, qT, kT, vT, doT, rw, qm, dom, offs, out_0,
         pw_mx = quantise("pw", pw_woven, E4M3)
         dv = [product("dv%d" % m, "back", dom_mx, m, pw_mx) for m in range(BLOCKS)]
         for m in range(BLOCKS):
-            staged = stage("dv%d" % m, dv[m])
-            for slots in SLOT_HALVES:
-                nc.scalar.activation(windows[m][:].indirect(listed(slots)), staged[:, slots], ACT.Copy)
+            halves = [new_tile("dv%d_staged%d" % (m, h), [P, N // 2], F32) for h in range(2)]
+            for h, slots in enumerate(SLOT_HALVES):
+                nc.scalar.copy(halves[h][:], dv[m][:, slots])
+            for h, slots in enumerate(SLOT_HALVES):
+                nc.scalar.activation(windows[m][:].indirect(listed(slots)), halves[h][:], ACT.Copy)
             nc.sync.dma_start(out_1[m * P : (m + 1) * P, :], windows[m][:])
 
         v_rows = new_tile("v_rows", [P, PACK, N], BF16)
@@ -193,7 +195,8 @@ def tile_attend_gat_sig_kv_kernel(tc, qT, kT, vT, doT, rw, qm, dom, offs, out_0,
         gather_last(v_rows, v_planes)
         weave_pair(v_woven, v_rows, SECOND_PAIR)
         v_mx = [quantise("v%d" % h, v_woven[h], E4M3) for h in range(2)]
-        qm_woven = [weave_half("qm%d" % h, qm_rows, h, nc.scalar.copy) for h in range(2)]
+        qm_first = new_woven("qm_first", P)
+        nc.vector.tensor_copy(walk_woven(qm_first[:]), walk_rows(qm_rows[:, :, :P]))
 
         ds_woven = new_woven("ds")
         for b in range(PACK):
@@ -205,11 +208,23 @@ def tile_attend_gat_sig_kv_kernel(tc, qT, kT, vT, doT, rw, qm, dom, offs, out_0,
             nc.vector.tensor_tensor(
                 walk_woven(ds_woven[:, slots, :]), walk_rows(dp[:]), walk_rows(slopes[b // 2][:, :, within]), MULT
             )
-        qm_mx = [quantise("qm0", qm_woven[0], E4M3)]
+        qm_first_mx = quantise("qm_first", qm_first, E4M3)
         ds_mx = quantise("ds", ds_woven, E5M2)
-        qm_mx.append(quantise("qm1", qm_woven[1], E4M3))
-        for m in range(BLOCKS):
-            staged = stage("dk%d" % m, product("dk%d" % m, "front", qm_mx, m, ds_mx))
+
+        def put_dk(m, staged):
             window = windows[(BLOCKS + m) % WINDOWS]
             nc.vector.tensor_copy(window[:].indirect(offsets[:]), staged[:])
             nc.sync.dma_start(out_0[m * P : (m + 1) * P, :], window[:])
+
+        bank = product("dk0", "front", [qm_first_mx], 0, ds_mx)
+        qm_second = new_woven("qm_second", P)
+        nc.vector.tensor_copy(walk_woven(qm_second[:]), walk_rows(qm_rows[:, :, P:HALF]))
+        qm_late = weave_half("qm_late", qm_rows, 1, nc.vector.tensor_copy)
+        staged = new_tile("dk0_staged", [P, N], F32)
+        nc.vector.tensor_copy(staged[:], bank[:])
+        qm_second_mx = quantise("qm_second", qm_second, E4M3)
+        put_dk(0, staged)
+        qm_late_mx = quantise("qm_late", qm_late, E4M3)
+        put_dk(1, stage("dk1", product("dk1", "front", [qm_second_mx], 0, ds_mx)))
+        for m in range(HALF_BLOCKS, BLOCKS):
+            put_dk(m, stage("dk%d" % m, product("dk%d" % m, "front", [None, qm_late_mx], m, ds_mx)))

@@ -159,21 +159,30 @@ def tile_attend_gat_sig_kv_kernel(tc, qT, kT, vT, doT, rw, qm, dom, offs, out_0,
         scores = [product("score%d" % j, "front", q_mx, j, k_mx) for j in range(PACK)]
 
         prob = held.tile([P, PACK, N], F32, name="prob")
-        minus_pw = held.tile([P, PACK, N], F32, name="minus_pw")
+        minus_pw = [new_tile("minus_pw%d" % h, [P, PACK, N // 2], F32) for h in range(2)]
         for j in range(PACK):
             nc.scalar.activation(prob[:, j, :], scores[j][:], ACT.Sigmoid)
-        for j in range(PACK):
-            nc.scalar.activation(minus_pw[:, j, :], prob[:, j, :], ACT.Copy, scale=minus_gate[:, j : j + 1])
-        pw_woven = new_woven("pw")
-        nc.scalar.activation(walk_woven(pw_woven[:]), walk_rows(minus_pw[:]), ACT.Copy, scale=-1.0)
+        pw_woven = [new_woven("pw%d" % h, N // 2) for h in range(2)]
+        for h, slots in enumerate(SLOT_HALVES):
+            for j in range(PACK):
+                nc.scalar.activation(
+                    minus_pw[h][:, j, :], prob[:, j, slots], ACT.Copy, scale=minus_gate[:, j : j + 1]
+                )
+            nc.scalar.activation(walk_woven(pw_woven[h][:]), walk_rows(minus_pw[h][:]), ACT.Copy, scale=-1.0)
         dom_woven = [weave_half("dom%d" % h, dom_rows, h, nc.vector.tensor_copy) for h in range(2)]
         dom_mx = [quantise("dom%d" % h, dom_woven[h], E5M2) for h in range(2)]
-        pw_mx = quantise("pw", pw_woven, E4M3)
-        dv = [product("dv%d" % m, "back", dom_mx, m, pw_mx) for m in range(BLOCKS)]
+        dv = []
+        for h in range(2):
+            pw_mx = quantise("pw%d" % h, pw_woven[h], E4M3)
+            banks = [psum.tile([P, HALF_BLOCKS, N // 2], F32, name="dv%d%d" % (h, g), tag="back") for g in range(2)]
+            for m in range(BLOCKS):
+                g, within = divmod(m, HALF_BLOCKS)
+                multiply(banks[g][:, within, :], dom_mx[g], within, pw_mx, slice(0, N // 2))
+            dv.append(banks)
         for m in range(BLOCKS):
             halves = [new_tile("dv%d_staged%d" % (m, h), [P, N // 2], F32) for h in range(2)]
-            for h, slots in enumerate(SLOT_HALVES):
-                nc.scalar.copy(halves[h][:], dv[m][:, slots])
+            for h in range(2):
+                nc.scalar.copy(halves[h][:], dv[h][m // HALF_BLOCKS][:, m % HALF_BLOCKS, :])
             for h, slots in enumerate(SLOT_HALVES):
                 nc.scalar.activation(windows[m][:].indirect(listed(slots)), halves[h][:], ACT.Copy)
             nc.sync.dma_start(out_1[m * P : (m + 1) * P, :], windows[m][:])
@@ -187,10 +196,10 @@ def tile_attend_gat_sig_kv_kernel(tc, qT, kT, vT, doT, rw, qm, dom, offs, out_0,
         do_mx = [quantise("do%d" % h, do_woven[h], E5M2) for h in range(2)]
         gather(v_rows, v_planes, 2)
         slopes = [new_tile("slope%d" % h, [P, PACK, N // 2], F32) for h in range(2)]
-        for pair in (FIRST_PAIR, SECOND_PAIR):
-            for h, slots in enumerate(SLOT_HALVES):
+        for h, slots in enumerate(SLOT_HALVES):
+            for pair in (FIRST_PAIR, SECOND_PAIR):
                 nc.vector.scalar_tensor_tensor(
-                    slopes[h][:, pair, :], prob[:, pair, slots], 1.0, minus_pw[:, pair, slots], SUBTRACT, MULT
+                    slopes[h][:, pair, :], prob[:, pair, slots], 1.0, minus_pw[h][:, pair, :], SUBTRACT, MULT
                 )
         gather_last(v_rows, v_planes)
         weave_pair(v_woven, v_rows, SECOND_PAIR)

@@ -58,9 +58,8 @@ def tile_attend_gat_sig_kv_kernel(tc, qT, kT, vT, doT, rw, qm, dom, offs, out_0,
         k_planes.extend(load_plane("k", kT, t) for t in range(1, PACK))
         q_rows = load_rows("q", qT[0])
         dom_rows = load_rows("dom", dom[0])
-        v_planes = [load_plane("v", vT, t) for t in range(2)]
         do_rows = load_rows("do", doT[0])
-        v_planes.extend(load_plane("v", vT, t) for t in range(2, PACK))
+        v_planes = [load_plane("v", vT, t) for t in range(PACK)]
         qm_rows = load_rows("qm", qm[0])
 
         windows = []
@@ -189,11 +188,11 @@ def tile_attend_gat_sig_kv_kernel(tc, qT, kT, vT, doT, rw, qm, dom, offs, out_0,
 
         v_rows = new_tile("v_rows", [P, PACK, N], BF16)
         v_woven = [new_woven("v%d" % h, N // 2) for h in range(2)]
+        do_woven = [weave_dealt("do%d" % h, do_rows, h, nc.vector.tensor_copy) for h in range(2)]
+        do_mx = [quantise("do%d" % h, do_woven[h], E5M2) for h in range(2)]
         gather(v_rows, v_planes, 0)
         gather(v_rows, v_planes, 1)
         weave_pair(v_woven, v_rows, FIRST_PAIR)
-        do_woven = [weave_dealt("do%d" % h, do_rows, h, nc.vector.tensor_copy) for h in range(2)]
-        do_mx = [quantise("do%d" % h, do_woven[h], E5M2) for h in range(2)]
         gather(v_rows, v_planes, 2)
         slopes = [new_tile("slope%d" % h, [P, PACK, N // 2], F32) for h in range(2)]
         for h, slots in enumerate(SLOT_HALVES):
@@ -204,36 +203,53 @@ def tile_attend_gat_sig_kv_kernel(tc, qT, kT, vT, doT, rw, qm, dom, offs, out_0,
         gather_last(v_rows, v_planes)
         weave_pair(v_woven, v_rows, SECOND_PAIR)
         v_mx = [quantise("v%d" % h, v_woven[h], E4M3) for h in range(2)]
-        qm_first = new_woven("qm_first", P)
-        nc.vector.tensor_copy(walk_woven(qm_first[:]), walk_rows(qm_rows[:, :, :P]))
 
-        ds_woven = new_woven("ds")
-        for b in range(PACK):
+        def weave_qm(m):
+            woven = new_woven("qm%d" % m, P)
+            nc.vector.tensor_copy(walk_woven(woven[:]), walk_rows(qm_rows[:, :, m * P : (m + 1) * P]))
+            return woven
+
+        ds_woven = [new_woven("ds%d" % h, N // 2) for h in range(2)]
+        ds_mx = (new_tile("ds_words", [P, N], U32), new_tile("ds_scales", [P, N], U8), E5M2)
+
+        def form_ds(b):
+            h, within = b // 2, slice((b % 2) * P, (b % 2 + 1) * P)
             dp = psum.tile([P, PACK, P], F32, name="dp%d" % b, tag="front")
-            slots = slice(b * P, (b + 1) * P)
-            within = slice((b % 2) * P, (b % 2 + 1) * P)
             for j in range(PACK):
-                multiply(dp[:, j, :], do_mx[j // HALF_BLOCKS], j % HALF_BLOCKS, v_mx[b // 2], within)
+                multiply(dp[:, j, :], do_mx[j // HALF_BLOCKS], j % HALF_BLOCKS, v_mx[h], within)
             nc.vector.tensor_tensor(
-                walk_woven(ds_woven[:, slots, :]), walk_rows(dp[:]), walk_rows(slopes[b // 2][:, :, within]), MULT
+                walk_woven(ds_woven[h][:, within, :]), walk_rows(dp[:]), walk_rows(slopes[h][:, :, within]), MULT
             )
-        qm_first_mx = quantise("qm_first", qm_first, E4M3)
-        ds_mx = quantise("ds", ds_woven, E5M2)
+
+        def quantise_ds(h):
+            nc.vector.quantize_mx(
+                out=ds_mx[0][:, SLOT_HALVES[h]].bitcast(E5M2),
+                scales=ds_mx[1][:, SLOT_HALVES[h]],
+                in_=ds_woven[h][:].rearrange("p c t -> p (c t)"),
+            )
 
         def put_dk(m, staged):
             window = windows[(BLOCKS + m) % WINDOWS]
             nc.vector.tensor_copy(window[:].indirect(offsets[:]), staged[:])
             nc.sync.dma_start(out_0[m * P : (m + 1) * P, :], window[:])
 
-        bank = product("dk0", "front", [qm_first_mx], 0, ds_mx)
-        qm_second = new_woven("qm_second", P)
-        nc.vector.tensor_copy(walk_woven(qm_second[:]), walk_rows(qm_rows[:, :, P:HALF]))
-        qm_late = weave_half("qm_late", qm_rows, 1, nc.vector.tensor_copy)
+        qm_woven = weave_qm(0)
+        form_ds(0)
+        qm_mx = quantise("qm0", qm_woven, E4M3)
+        form_ds(1)
+        form_ds(2)
+        quantise_ds(0)
+        form_ds(LAST)
+        qm_woven = weave_qm(1)
+        quantise_ds(1)
         staged = new_tile("dk0_staged", [P, N], F32)
-        nc.vector.tensor_copy(staged[:], bank[:])
-        qm_second_mx = quantise("qm_second", qm_second, E4M3)
+        for h, slots in enumerate(SLOT_HALVES):
+            bank = psum.tile([P, N // 2], F32, name="dk0_%d" % h, tag="front")
+            multiply(bank[:], qm_mx, 0, ds_mx, slots)
+            nc.vector.tensor_copy(staged[:, slots], bank[:])
+        qm_mx = quantise("qm1", qm_woven, E4M3)
         put_dk(0, staged)
-        qm_late_mx = quantise("qm_late", qm_late, E4M3)
-        put_dk(1, stage("dk1", product("dk1", "front", [qm_second_mx], 0, ds_mx)))
+        qm_late_mx = quantise("qm_late", weave_half("qm_late", qm_rows, 1, nc.vector.tensor_copy), E4M3)
+        put_dk(1, stage("dk1", product("dk1", "front", [qm_mx], 0, ds_mx)))
         for m in range(HALF_BLOCKS, BLOCKS):
             put_dk(m, stage("dk%d" % m, product("dk%d" % m, "front", [None, qm_late_mx], m, ds_mx)))

@@ -45,21 +45,24 @@ def tile_attend_gat_sig_kv_kernel(tc, qT, kT, vT, doT, rw, qm, dom, offs, out_0,
             nc.sync.dma_start(rows[:], src.rearrange("(p t) c -> p t c", t=PACK))
             return rows
 
-        def load_plane(name, table, t):
-            plane = new_tile("%s_plane%d" % (name, t), [P, T], F32)
-            nc.sync.dma_start(plane[:], table.rearrange("(p t) c -> t p c", t=PACK)[t])
-            return plane
+        def load_planes(name, table, places):
+            count = places.stop - places.start
+            planes = new_tile("%s_planes%d" % (name, places.start), [P, count, T], F32)
+            nc.sync.dma_start(planes[:], table.rearrange("(p t) c -> p t c", t=PACK)[:, places, :])
+            return [planes[:, t, :] for t in range(count)]
 
-        k_planes = [load_plane("k", kT, 0)]
+        k_planes = load_planes("k", kT, FIRST_PAIR)
         offsets = held.tile([P, N // BAND], U16, name="offsets")
         nc.sync.dma_start(offsets[:], offs)
         gate = held.tile([P, PACK], F32, name="gate")
         nc.sync.dma_start(gate[:], rw[0].rearrange("(p j) o -> p (j o)", j=PACK))
-        k_planes.extend(load_plane("k", kT, t) for t in range(1, PACK))
+        k_planes.extend(load_planes("k", kT, SECOND_PAIR))
         q_rows = load_rows("q", qT[0])
         dom_rows = load_rows("dom", dom[0])
         do_rows = load_rows("do", doT[0])
-        v_planes = [load_plane("v", vT, t) for t in range(PACK)]
+        v_planes = load_planes("v", vT, FIRST_PAIR)
+        for t in range(SECOND_PAIR.start, PACK):
+            v_planes.extend(load_planes("v", vT, slice(t, t + 1)))
         qm_rows = load_rows("qm", qm[0])
 
         windows = []
@@ -69,7 +72,7 @@ def tile_attend_gat_sig_kv_kernel(tc, qT, kT, vT, doT, rw, qm, dom, offs, out_0,
             engine.memset(window[:].bitcast(I32), 0)
             windows.append(window)
         minus_gate = held.tile([P, PACK], F32, name="minus_gate")
-        nc.vector.tensor_scalar(minus_gate[:], gate[:], -1.0, None, MULT)
+        nc.scalar.activation(minus_gate[:], gate[:], ACT.Copy, scale=-1.0)
 
         def new_woven(name, width=N):
             return new_tile(name + "_woven", [P, width, PACK], BF16)
@@ -128,23 +131,23 @@ def tile_attend_gat_sig_kv_kernel(tc, qT, kT, vT, doT, rw, qm, dom, offs, out_0,
             return staged
 
         def gather(rows, planes, t):
-            nc.vector.tensor_copy(rows[:, t, :], planes[t][:].indirect(offsets[:]))
+            nc.vector.tensor_copy(rows[:, t, :], planes[t].indirect(offsets[:]))
 
         def gather_last(rows, planes):
             for slots in SLOT_HALVES:
-                nc.vector.tensor_copy(rows[:, LAST, slots], planes[LAST][:].indirect(listed(slots)))
+                nc.vector.tensor_copy(rows[:, LAST, slots], planes[LAST].indirect(listed(slots)))
 
         def weave_pair(woven, rows, pair):
             for h, slots in enumerate(SLOT_HALVES):
-                nc.vector.tensor_copy(woven[h][:, :, pair], rows[:, pair, slots].rearrange("p t c -> p c t"))
+                nc.vector.tensor_copy(walk_woven(woven[h][:, :, pair]), walk_rows(rows[:, pair, slots]))
 
-        k_rows = new_tile("k_rows", [P, PACK, N], BF16)
+        k_rows = held.tile([P, PACK, N], F32, name="k_rows", tag="gathered")
         k_woven = [new_woven("k%d" % h, N // 2) for h in range(2)]
         gather(k_rows, k_planes, 0)
         gather(k_rows, k_planes, 1)
         weave_pair(k_woven, k_rows, FIRST_PAIR)
         gather(k_rows, k_planes, 2)
-        gather_last(k_rows, k_planes)
+        nc.scalar.activation(k_rows[:, LAST, :], k_planes[LAST].indirect(offsets[:]), ACT.Copy)
         weave_pair(k_woven, k_rows, SECOND_PAIR)
         k_mx = (new_tile("k_words", [P, N], U32), new_tile("k_scales", [P, N], U8), E4M3)
         for h, slots in enumerate(SLOT_HALVES):
@@ -186,7 +189,7 @@ def tile_attend_gat_sig_kv_kernel(tc, qT, kT, vT, doT, rw, qm, dom, offs, out_0,
                 nc.scalar.activation(windows[m][:].indirect(listed(slots)), halves[h][:], ACT.Copy)
             nc.sync.dma_start(out_1[m * P : (m + 1) * P, :], windows[m][:])
 
-        v_rows = new_tile("v_rows", [P, PACK, N], BF16)
+        v_rows = held.tile([P, PACK, N], F32, name="v_rows", tag="gathered")
         v_woven = [new_woven("v%d" % h, N // 2) for h in range(2)]
         do_woven = [weave_dealt("do%d" % h, do_rows, h, nc.vector.tensor_copy) for h in range(2)]
         do_mx = [quantise("do%d" % h, do_woven[h], E5M2) for h in range(2)]

@@ -29,16 +29,20 @@ HALF_BLOCKS = HALF // P
 SLOT_HALVES = [slice(0, N // 2), slice(N // 2, N)]
 FIRST_PAIR, SECOND_PAIR = slice(0, 2), slice(2, PACK)
 RUN = 2
+AT_DK_STAGED = 0
 
 
 def tile_attend_gat_sig_kv_kernel(tc, qT, kT, vT, doT, rw, qm, dom, offs, out_0, out_1):
     nc = tc.nc
     with ExitStack() as ctx:
         held = ctx.enter_context(tc.tile_pool(name="held", bufs=1))
+        shared = ctx.enter_context(tc.tile_pool(name="shared", bufs=1))
         psum = ctx.enter_context(tc.psum_pool(name="psum", bufs=PACK))
 
-        def new_tile(name, shape, dtype):
-            return held.tile(shape, dtype, name=name, align_bytes=ALIGN)
+        def new_tile(name, shape, dtype, at=None):
+            if at is None:
+                return held.tile(shape, dtype, name=name, align_bytes=ALIGN)
+            return shared.tile(shape, dtype, name=name, offset=at, align_bytes=ALIGN)
 
         def load_rows(name, src):
             rows = new_tile(name + "_rows", [P, PACK, src.shape[1]], F32)
@@ -60,8 +64,8 @@ def tile_attend_gat_sig_kv_kernel(tc, qT, kT, vT, doT, rw, qm, dom, offs, out_0,
         q_rows = load_rows("q", qT[0])
         dom_rows = load_rows("dom", dom[0])
         do_rows = load_rows("do", doT[0])
-        v_planes = load_planes("v", vT, FIRST_PAIR)
-        for t in range(SECOND_PAIR.start, PACK):
+        v_planes = []
+        for t in range(PACK):
             v_planes.extend(load_planes("v", vT, slice(t, t + 1)))
         qm_rows = load_rows("qm", qm[0])
 
@@ -74,13 +78,13 @@ def tile_attend_gat_sig_kv_kernel(tc, qT, kT, vT, doT, rw, qm, dom, offs, out_0,
         minus_gate = held.tile([P, PACK], F32, name="minus_gate")
         nc.scalar.activation(minus_gate[:], gate[:], ACT.Copy, scale=-1.0)
 
-        def new_woven(name, width=N):
-            return new_tile(name + "_woven", [P, width, PACK], BF16)
+        def new_woven(name, width=N, at=None):
+            return new_tile(name + "_woven", [P, width, PACK], BF16, at)
 
-        def quantise(name, woven, fmt):
+        def quantise(name, woven, fmt, at=None):
             width = woven.shape[1]
-            words = new_tile(name + "_words", [P, width], U32)
-            scales = new_tile(name + "_scales", [P, width], U8)
+            words = new_tile(name + "_words", [P, width], U32, at)
+            scales = new_tile(name + "_scales", [P, width], U8, None if at is None else at + PACK * width)
             flat = woven[:].rearrange("p c t -> p (c t)")
             nc.vector.quantize_mx(out=words[:].bitcast(fmt), scales=scales[:], in_=flat)
             return words, scales, fmt
@@ -207,9 +211,9 @@ def tile_attend_gat_sig_kv_kernel(tc, qT, kT, vT, doT, rw, qm, dom, offs, out_0,
         weave_pair(v_woven, v_rows, SECOND_PAIR)
         v_mx = [quantise("v%d" % h, v_woven[h], E4M3) for h in range(2)]
 
-        def weave_qm(m):
+        def weave_qm(m, copy):
             woven = new_woven("qm%d" % m, P)
-            nc.vector.tensor_copy(walk_woven(woven[:]), walk_rows(qm_rows[:, :, m * P : (m + 1) * P]))
+            copy(walk_woven(woven[:]), walk_rows(qm_rows[:, :, m * P : (m + 1) * P]))
             return woven
 
         ds_woven = [new_woven("ds%d" % h, N // 2) for h in range(2)]
@@ -236,23 +240,24 @@ def tile_attend_gat_sig_kv_kernel(tc, qT, kT, vT, doT, rw, qm, dom, offs, out_0,
             nc.vector.tensor_copy(window[:].indirect(offsets[:]), staged[:])
             nc.sync.dma_start(out_0[m * P : (m + 1) * P, :], window[:])
 
-        qm_woven = weave_qm(0)
+        qm_woven = weave_qm(0, nc.vector.tensor_copy)
         form_ds(0)
         qm_mx = quantise("qm0", qm_woven, E4M3)
         form_ds(1)
         form_ds(2)
         quantise_ds(0)
         form_ds(LAST)
-        qm_woven = weave_qm(1)
+        qm_woven = weave_qm(1, nc.vector.tensor_copy)
+        qm_late = weave_half("qm_late", qm_rows, 1, nc.scalar.copy)
         quantise_ds(1)
-        staged = new_tile("dk0_staged", [P, N], F32)
+        staged = new_tile("dk0_staged", [P, N], F32, AT_DK_STAGED)
         for h, slots in enumerate(SLOT_HALVES):
             bank = psum.tile([P, N // 2], F32, name="dk0_%d" % h, tag="front")
             multiply(bank[:], qm_mx, 0, ds_mx, slots)
             nc.vector.tensor_copy(staged[:, slots], bank[:])
         qm_mx = quantise("qm1", qm_woven, E4M3)
         put_dk(0, staged)
-        qm_late_mx = quantise("qm_late", weave_half("qm_late", qm_rows, 1, nc.vector.tensor_copy), E4M3)
+        qm_late_mx = quantise("qm_late", qm_late, E4M3, AT_DK_STAGED)
         put_dk(1, stage("dk1", product("dk1", "front", [qm_mx], 0, ds_mx)))
         for m in range(HALF_BLOCKS, BLOCKS):
             put_dk(m, stage("dk%d" % m, product("dk%d" % m, "front", [None, qm_late_mx], m, ds_mx)))

@@ -29,7 +29,8 @@ HALF_BLOCKS = HALF // P
 SLOT_HALVES = [slice(0, N // 2), slice(N // 2, N)]
 FIRST_PAIR, SECOND_PAIR = slice(0, 2), slice(2, PACK)
 RUN = 2
-AT_DK_STAGED = 0
+AT_DK_FIRST = 0
+AT_DK_SECOND = N * 2
 
 
 def tile_attend_gat_sig_kv_kernel(tc, qT, kT, vT, doT, rw, qm, dom, offs, out_0, out_1):
@@ -49,24 +50,21 @@ def tile_attend_gat_sig_kv_kernel(tc, qT, kT, vT, doT, rw, qm, dom, offs, out_0,
             nc.sync.dma_start(rows[:], src.rearrange("(p t) c -> p t c", t=PACK))
             return rows
 
-        def load_planes(name, table, places):
-            count = places.stop - places.start
-            planes = new_tile("%s_planes%d" % (name, places.start), [P, count, T], F32)
-            nc.sync.dma_start(planes[:], table.rearrange("(p t) c -> p t c", t=PACK)[:, places, :])
-            return [planes[:, t, :] for t in range(count)]
+        def load_plane(name, table, t):
+            plane = new_tile("%s_plane%d" % (name, t), [P, T], F32)
+            nc.sync.dma_start(plane[:], table.rearrange("(p t) c -> t p c", t=PACK)[t])
+            return plane
 
-        k_planes = load_planes("k", kT, FIRST_PAIR)
+        k_planes = [load_plane("k", kT, 0)]
         offsets = held.tile([P, N // BAND], U16, name="offsets")
         nc.sync.dma_start(offsets[:], offs)
         gate = held.tile([P, PACK], F32, name="gate")
         nc.sync.dma_start(gate[:], rw[0].rearrange("(p j) o -> p (j o)", j=PACK))
-        k_planes.extend(load_planes("k", kT, SECOND_PAIR))
+        k_planes.extend(load_plane("k", kT, t) for t in range(1, PACK))
         q_rows = load_rows("q", qT[0])
         dom_rows = load_rows("dom", dom[0])
         do_rows = load_rows("do", doT[0])
-        v_planes = []
-        for t in range(PACK):
-            v_planes.extend(load_planes("v", vT, slice(t, t + 1)))
+        v_planes = [load_plane("v", vT, t) for t in range(PACK)]
         qm_rows = load_rows("qm", qm[0])
 
         windows = []
@@ -76,7 +74,7 @@ def tile_attend_gat_sig_kv_kernel(tc, qT, kT, vT, doT, rw, qm, dom, offs, out_0,
             engine.memset(window[:].bitcast(I32), 0)
             windows.append(window)
         minus_gate = held.tile([P, PACK], F32, name="minus_gate")
-        nc.scalar.activation(minus_gate[:], gate[:], ACT.Copy, scale=-1.0)
+        nc.vector.tensor_scalar(minus_gate[:], gate[:], -1.0, None, MULT)
 
         def new_woven(name, width=N, at=None):
             return new_tile(name + "_woven", [P, width, PACK], BF16, at)
@@ -104,8 +102,8 @@ def tile_attend_gat_sig_kv_kernel(tc, qT, kT, vT, doT, rw, qm, dom, offs, out_0,
         def walk_rows(rows):
             return rows.rearrange("p t (c i) -> p c t i", i=RUN)
 
-        def weave_half(name, rows, h, copy):
-            woven = new_woven(name, HALF)
+        def weave_half(name, rows, h, copy, at=None):
+            woven = new_woven(name, HALF, at)
             copy(walk_woven(woven[:]), walk_rows(rows[:, :, h * HALF : (h + 1) * HALF]))
             return woven
 
@@ -135,23 +133,23 @@ def tile_attend_gat_sig_kv_kernel(tc, qT, kT, vT, doT, rw, qm, dom, offs, out_0,
             return staged
 
         def gather(rows, planes, t):
-            nc.vector.tensor_copy(rows[:, t, :], planes[t].indirect(offsets[:]))
+            nc.vector.tensor_copy(rows[:, t, :], planes[t][:].indirect(offsets[:]))
 
         def gather_last(rows, planes):
             for slots in SLOT_HALVES:
-                nc.vector.tensor_copy(rows[:, LAST, slots], planes[LAST].indirect(listed(slots)))
+                nc.vector.tensor_copy(rows[:, LAST, slots], planes[LAST][:].indirect(listed(slots)))
 
         def weave_pair(woven, rows, pair):
             for h, slots in enumerate(SLOT_HALVES):
-                nc.vector.tensor_copy(walk_woven(woven[h][:, :, pair]), walk_rows(rows[:, pair, slots]))
+                nc.vector.tensor_copy(woven[h][:, :, pair], rows[:, pair, slots].rearrange("p t c -> p c t"))
 
-        k_rows = held.tile([P, PACK, N], F32, name="k_rows", tag="gathered")
+        k_rows = new_tile("k_rows", [P, PACK, N], BF16)
         k_woven = [new_woven("k%d" % h, N // 2) for h in range(2)]
         gather(k_rows, k_planes, 0)
         gather(k_rows, k_planes, 1)
         weave_pair(k_woven, k_rows, FIRST_PAIR)
         gather(k_rows, k_planes, 2)
-        nc.scalar.activation(k_rows[:, LAST, :], k_planes[LAST].indirect(offsets[:]), ACT.Copy)
+        gather_last(k_rows, k_planes)
         weave_pair(k_woven, k_rows, SECOND_PAIR)
         k_mx = (new_tile("k_words", [P, N], U32), new_tile("k_scales", [P, N], U8), E4M3)
         for h, slots in enumerate(SLOT_HALVES):
@@ -193,7 +191,7 @@ def tile_attend_gat_sig_kv_kernel(tc, qT, kT, vT, doT, rw, qm, dom, offs, out_0,
                 nc.scalar.activation(windows[m][:].indirect(listed(slots)), halves[h][:], ACT.Copy)
             nc.sync.dma_start(out_1[m * P : (m + 1) * P, :], windows[m][:])
 
-        v_rows = held.tile([P, PACK, N], F32, name="v_rows", tag="gathered")
+        v_rows = new_tile("v_rows", [P, PACK, N], BF16)
         v_woven = [new_woven("v%d" % h, N // 2) for h in range(2)]
         do_woven = [weave_dealt("do%d" % h, do_rows, h, nc.vector.tensor_copy) for h in range(2)]
         do_mx = [quantise("do%d" % h, do_woven[h], E5M2) for h in range(2)]
@@ -216,24 +214,31 @@ def tile_attend_gat_sig_kv_kernel(tc, qT, kT, vT, doT, rw, qm, dom, offs, out_0,
             copy(walk_woven(woven[:]), walk_rows(qm_rows[:, :, m * P : (m + 1) * P]))
             return woven
 
-        ds_woven = [new_woven("ds%d" % h, N // 2) for h in range(2)]
+        ds_parts = [slice(0, 2 * P), slice(2 * P, 3 * P), slice(3 * P, N)]
+        ds_woven = [new_woven("ds%d" % g, part.stop - part.start) for g, part in enumerate(ds_parts)]
         ds_mx = (new_tile("ds_words", [P, N], U32), new_tile("ds_scales", [P, N], U8), E5M2)
 
         def form_ds(b):
             h, within = b // 2, slice((b % 2) * P, (b % 2 + 1) * P)
+            woven = ds_woven[0][:, within, :] if h == 0 else ds_woven[b - 1][:]
             dp = psum.tile([P, PACK, P], F32, name="dp%d" % b, tag="front")
             for j in range(PACK):
                 multiply(dp[:, j, :], do_mx[j // HALF_BLOCKS], j % HALF_BLOCKS, v_mx[h], within)
-            nc.vector.tensor_tensor(
-                walk_woven(ds_woven[h][:, within, :]), walk_rows(dp[:]), walk_rows(slopes[h][:, :, within]), MULT
-            )
+            nc.vector.tensor_tensor(walk_woven(woven), walk_rows(dp[:]), walk_rows(slopes[h][:, :, within]), MULT)
 
-        def quantise_ds(h):
+        staged = [new_tile("dk0_staged%d" % h, [P, N // 2], F32, at) for h, at in enumerate((AT_DK_FIRST, AT_DK_SECOND))]
+
+        def finish_part(g, stationary):
+            part = ds_parts[g]
             nc.vector.quantize_mx(
-                out=ds_mx[0][:, SLOT_HALVES[h]].bitcast(E5M2),
-                scales=ds_mx[1][:, SLOT_HALVES[h]],
-                in_=ds_woven[h][:].rearrange("p c t -> p (c t)"),
+                out=ds_mx[0][:, part].bitcast(E5M2),
+                scales=ds_mx[1][:, part],
+                in_=ds_woven[g][:].rearrange("p c t -> p (c t)"),
             )
+            bank = psum.tile([P, part.stop - part.start], F32, name="dk0_%d" % g, tag="back")
+            multiply(bank[:], stationary, 0, ds_mx, part)
+            h, start = divmod(part.start, N // 2)
+            nc.scalar.copy(staged[h][:, start : start + part.stop - part.start], bank[:])
 
         def put_dk(m, staged):
             window = windows[(BLOCKS + m) % WINDOWS]
@@ -243,21 +248,21 @@ def tile_attend_gat_sig_kv_kernel(tc, qT, kT, vT, doT, rw, qm, dom, offs, out_0,
         qm_woven = weave_qm(0, nc.vector.tensor_copy)
         form_ds(0)
         qm_mx = quantise("qm0", qm_woven, E4M3)
+        qm_woven = weave_qm(1, nc.scalar.copy)
         form_ds(1)
         form_ds(2)
-        quantise_ds(0)
+        finish_part(0, qm_mx)
         form_ds(LAST)
-        qm_woven = weave_qm(1, nc.vector.tensor_copy)
-        qm_late = weave_half("qm_late", qm_rows, 1, nc.scalar.copy)
-        quantise_ds(1)
-        staged = new_tile("dk0_staged", [P, N], F32, AT_DK_STAGED)
-        for h, slots in enumerate(SLOT_HALVES):
-            bank = psum.tile([P, N // 2], F32, name="dk0_%d" % h, tag="front")
-            multiply(bank[:], qm_mx, 0, ds_mx, slots)
-            nc.vector.tensor_copy(staged[:, slots], bank[:])
-        qm_mx = quantise("qm1", qm_woven, E4M3)
-        put_dk(0, staged)
-        qm_late_mx = quantise("qm_late", qm_late, E4M3, AT_DK_STAGED)
-        put_dk(1, stage("dk1", product("dk1", "front", [qm_mx], 0, ds_mx)))
+        finish_part(1, qm_mx)
+        finish_part(2, qm_mx)
+        window = windows[BLOCKS]
+        nc.vector.tensor_copy(window[:].indirect(listed(SLOT_HALVES[0])), staged[0][:])
+        qm_mx = quantise("qm1", qm_woven, E4M3, AT_DK_FIRST)
+        nc.vector.tensor_copy(window[:].indirect(listed(SLOT_HALVES[1])), staged[1][:])
+        nc.sync.dma_start(out_0[:P, :], window[:])
+        qm_late = weave_half("qm_late", qm_rows, 1, nc.vector.tensor_copy, AT_DK_SECOND)
+        dk1 = stage("dk1", product("dk1", "front", [qm_mx], 0, ds_mx))
+        qm_late_mx = quantise("qm_late", qm_late, E4M3)
+        put_dk(1, dk1)
         for m in range(HALF_BLOCKS, BLOCKS):
             put_dk(m, stage("dk%d" % m, product("dk%d" % m, "front", [None, qm_late_mx], m, ds_mx)))

@@ -50,21 +50,22 @@ def tile_attend_gat_sig_kv_kernel(tc, qT, kT, vT, doT, rw, qm, dom, offs, out_0,
             nc.sync.dma_start(rows[:], src.rearrange("(p t) c -> p t c", t=PACK))
             return rows
 
-        def load_plane(name, table, t):
-            plane = new_tile("%s_plane%d" % (name, t), [P, T], F32)
-            nc.sync.dma_start(plane[:], table.rearrange("(p t) c -> t p c", t=PACK)[t])
-            return plane
+        def load_planes(name, table, places):
+            count = places.stop - places.start
+            planes = new_tile("%s_planes%d" % (name, places.start), [P, count, T], F32)
+            nc.sync.dma_start(planes[:], table.rearrange("(p t) c -> p t c", t=PACK)[:, places, :])
+            return [planes[:, t, :] for t in range(count)]
 
-        k_planes = [load_plane("k", kT, 0)]
+        k_planes = load_planes("k", kT, FIRST_PAIR)
         offsets = held.tile([P, N // BAND], U16, name="offsets")
         nc.sync.dma_start(offsets[:], offs)
         gate = held.tile([P, PACK], F32, name="gate")
         nc.sync.dma_start(gate[:], rw[0].rearrange("(p j) o -> p (j o)", j=PACK))
-        k_planes.extend(load_plane("k", kT, t) for t in range(1, PACK))
+        k_planes.extend(load_planes("k", kT, SECOND_PAIR))
         q_rows = load_rows("q", qT[0])
         dom_rows = load_rows("dom", dom[0])
         do_rows = load_rows("do", doT[0])
-        v_planes = [load_plane("v", vT, t) for t in range(PACK)]
+        v_planes = load_planes("v", vT, FIRST_PAIR) + load_planes("v", vT, SECOND_PAIR)
         qm_rows = load_rows("qm", qm[0])
 
         windows = []
@@ -133,17 +134,17 @@ def tile_attend_gat_sig_kv_kernel(tc, qT, kT, vT, doT, rw, qm, dom, offs, out_0,
             return staged
 
         def gather(rows, planes, t):
-            nc.vector.tensor_copy(rows[:, t, :], planes[t][:].indirect(offsets[:]))
+            nc.vector.tensor_copy(rows[:, t, :], planes[t].indirect(offsets[:]))
 
         def gather_last(rows, planes):
             for slots in SLOT_HALVES:
-                nc.vector.tensor_copy(rows[:, LAST, slots], planes[LAST][:].indirect(listed(slots)))
+                nc.vector.tensor_copy(rows[:, LAST, slots], planes[LAST].indirect(listed(slots)))
 
         def weave_pair(woven, rows, pair):
             for h, slots in enumerate(SLOT_HALVES):
-                nc.vector.tensor_copy(woven[h][:, :, pair], rows[:, pair, slots].rearrange("p t c -> p c t"))
+                nc.vector.tensor_copy(walk_woven(woven[h][:, :, pair]), walk_rows(rows[:, pair, slots]))
 
-        k_rows = new_tile("k_rows", [P, PACK, N], BF16)
+        k_rows = held.tile([P, PACK, N], F32, name="k_rows", tag="gathered")
         k_woven = [new_woven("k%d" % h, N // 2) for h in range(2)]
         gather(k_rows, k_planes, 0)
         gather(k_rows, k_planes, 1)
@@ -191,7 +192,7 @@ def tile_attend_gat_sig_kv_kernel(tc, qT, kT, vT, doT, rw, qm, dom, offs, out_0,
                 nc.scalar.activation(windows[m][:].indirect(listed(slots)), halves[h][:], ACT.Copy)
             nc.sync.dma_start(out_1[m * P : (m + 1) * P, :], windows[m][:])
 
-        v_rows = new_tile("v_rows", [P, PACK, N], BF16)
+        v_rows = held.tile([P, PACK, N], F32, name="v_rows", tag="gathered")
         v_woven = [new_woven("v%d" % h, N // 2) for h in range(2)]
         do_woven = [weave_dealt("do%d" % h, do_rows, h, nc.vector.tensor_copy) for h in range(2)]
         do_mx = [quantise("do%d" % h, do_woven[h], E5M2) for h in range(2)]

@@ -22,6 +22,9 @@ PACK = 4
 LAST = PACK - 1
 BAND = 16
 ALIGN = 64
+DMA_ALIGN = 4096
+CELL = T * 4
+K_CELL, V_CELL, Q_CELL, DOM_CELL, DO_CELL, QM_CELL, WINDOW_CELL = 0, 4, 8, 9, 10, 11, 12
 BLOCKS = DV // P
 WINDOWS = BLOCKS + 1
 HALF = DV // 2
@@ -36,6 +39,7 @@ AT_DK_SECOND = N * 2
 def tile_attend_gat_sig_kv_kernel(tc, qT, kT, vT, doT, rw, qm, dom, offs, out_0, out_1):
     nc = tc.nc
     with ExitStack() as ctx:
+        moved = ctx.enter_context(tc.tile_pool(name="moved", bufs=1))
         held = ctx.enter_context(tc.tile_pool(name="held", bufs=1))
         shared = ctx.enter_context(tc.tile_pool(name="shared", bufs=1))
         psum = ctx.enter_context(tc.psum_pool(name="psum", bufs=PACK))
@@ -45,32 +49,35 @@ def tile_attend_gat_sig_kv_kernel(tc, qT, kT, vT, doT, rw, qm, dom, offs, out_0,
                 return held.tile(shape, dtype, name=name, align_bytes=ALIGN)
             return shared.tile(shape, dtype, name=name, offset=at, align_bytes=ALIGN)
 
-        def load_rows(name, src):
-            rows = new_tile(name + "_rows", [P, PACK, src.shape[1]], F32)
+        def moved_tile(name, shape, cell):
+            return moved.tile(shape, F32, name=name, offset=cell * CELL, align_bytes=DMA_ALIGN)
+
+        def load_rows(name, src, cell):
+            rows = moved_tile(name + "_rows", [P, PACK, src.shape[1]], cell)
             nc.sync.dma_start(rows[:], src.rearrange("(p t) c -> p t c", t=PACK))
             return rows
 
-        def load_planes(name, table, places):
+        def load_planes(name, table, places, cell):
             count = places.stop - places.start
-            planes = new_tile("%s_planes%d" % (name, places.start), [P, count, T], F32)
+            planes = moved_tile("%s_planes%d" % (name, places.start), [P, count, T], cell + places.start)
             nc.sync.dma_start(planes[:], table.rearrange("(p t) c -> p t c", t=PACK)[:, places, :])
             return [planes[:, t, :] for t in range(count)]
 
-        k_planes = load_planes("k", kT, FIRST_PAIR)
+        k_planes = load_planes("k", kT, FIRST_PAIR, K_CELL)
         offsets = held.tile([P, N // BAND], U16, name="offsets")
         nc.sync.dma_start(offsets[:], offs)
         gate = held.tile([P, PACK], F32, name="gate")
         nc.sync.dma_start(gate[:], rw[0].rearrange("(p j) o -> p (j o)", j=PACK))
-        k_planes.extend(load_planes("k", kT, SECOND_PAIR))
-        q_rows = load_rows("q", qT[0])
-        dom_rows = load_rows("dom", dom[0])
-        do_rows = load_rows("do", doT[0])
-        v_planes = load_planes("v", vT, FIRST_PAIR) + load_planes("v", vT, SECOND_PAIR)
-        qm_rows = load_rows("qm", qm[0])
+        k_planes.extend(load_planes("k", kT, SECOND_PAIR, K_CELL))
+        q_rows = load_rows("q", qT[0], Q_CELL)
+        dom_rows = load_rows("dom", dom[0], DOM_CELL)
+        do_rows = load_rows("do", doT[0], DO_CELL)
+        v_planes = load_planes("v", vT, FIRST_PAIR, V_CELL) + load_planes("v", vT, SECOND_PAIR, V_CELL)
+        qm_rows = load_rows("qm", qm[0], QM_CELL)
 
         windows = []
         for w in range(WINDOWS):
-            window = held.tile([P, T], F32, name="window%d" % w)
+            window = moved_tile("window%d" % w, [P, T], WINDOW_CELL + w)
             engine = nc.vector if w % 2 == 0 else nc.gpsimd
             engine.memset(window[:].bitcast(I32), 0)
             windows.append(window)
@@ -79,6 +86,10 @@ def tile_attend_gat_sig_kv_kernel(tc, qT, kT, vT, doT, rw, qm, dom, offs, out_0,
 
         def new_woven(name, width=N, at=None):
             return new_tile(name + "_woven", [P, width, PACK], BF16, at)
+
+        def table_woven(name, h):
+            shape = [P, N // 2, PACK]
+            return held.tile(shape, BF16, name="%s%d_woven" % (name, h), tag="table%d" % h, align_bytes=ALIGN)
 
         def quantise(name, woven, fmt, at=None):
             width = woven.shape[1]
@@ -145,7 +156,7 @@ def tile_attend_gat_sig_kv_kernel(tc, qT, kT, vT, doT, rw, qm, dom, offs, out_0,
                 nc.vector.tensor_copy(walk_woven(woven[h][:, :, pair]), walk_rows(rows[:, pair, slots]))
 
         k_rows = held.tile([P, PACK, N], F32, name="k_rows", tag="gathered")
-        k_woven = [new_woven("k%d" % h, N // 2) for h in range(2)]
+        k_woven = [table_woven("k", h) for h in range(2)]
         gather(k_rows, k_planes, 0)
         gather(k_rows, k_planes, 1)
         weave_pair(k_woven, k_rows, FIRST_PAIR)
@@ -193,7 +204,7 @@ def tile_attend_gat_sig_kv_kernel(tc, qT, kT, vT, doT, rw, qm, dom, offs, out_0,
             nc.sync.dma_start(out_1[m * P : (m + 1) * P, :], windows[m][:])
 
         v_rows = held.tile([P, PACK, N], F32, name="v_rows", tag="gathered")
-        v_woven = [new_woven("v%d" % h, N // 2) for h in range(2)]
+        v_woven = [table_woven("v", h) for h in range(2)]
         do_woven = [weave_dealt("do%d" % h, do_rows, h, nc.vector.tensor_copy) for h in range(2)]
         do_mx = [quantise("do%d" % h, do_woven[h], E5M2) for h in range(2)]
         gather(v_rows, v_planes, 0)

@@ -26,11 +26,11 @@ DMA_ALIGN = 4096
 CELL = T * 4
 K_CELL, V_CELL, Q_CELL, DOM_CELL, DO_CELL, QM_CELL, WINDOW_CELL = 0, 4, 8, 9, 10, 11, 12
 BLOCKS = DV // P
-WINDOWS = BLOCKS + 1
 HALF = DV // 2
 HALF_BLOCKS = HALF // P
 SLOT_HALVES = [slice(0, N // 2), slice(N // 2, N)]
 FIRST_PAIR, SECOND_PAIR = slice(0, 2), slice(2, PACK)
+TABLE_LOADS = (FIRST_PAIR, slice(2, LAST), slice(LAST, PACK))
 RUN = 2
 AT_DK_FIRST = 0
 AT_DK_SECOND = N * 2
@@ -63,23 +63,24 @@ def tile_attend_gat_sig_kv_kernel(tc, qT, kT, vT, doT, rw, qm, dom, offs, out_0,
             nc.sync.dma_start(planes[:], table.rearrange("(p t) c -> p t c", t=PACK)[:, places, :])
             return [planes[:, t, :] for t in range(count)]
 
-        k_planes = load_planes("k", kT, FIRST_PAIR, K_CELL)
+        def load_table(name, table, cell):
+            return [plane for places in TABLE_LOADS for plane in load_planes(name, table, places, cell)]
+
+        q_rows = load_rows("q", qT[0], Q_CELL)
         offsets = held.tile([P, N // BAND], U16, name="offsets")
         nc.sync.dma_start(offsets[:], offs)
         gate = held.tile([P, PACK], F32, name="gate")
         nc.sync.dma_start(gate[:], rw[0].rearrange("(p j) o -> p (j o)", j=PACK))
-        k_planes.extend(load_planes("k", kT, SECOND_PAIR, K_CELL))
-        q_rows = load_rows("q", qT[0], Q_CELL)
+        k_planes = load_table("k", kT, K_CELL)
         dom_rows = load_rows("dom", dom[0], DOM_CELL)
         do_rows = load_rows("do", doT[0], DO_CELL)
-        v_planes = load_planes("v", vT, FIRST_PAIR, V_CELL) + load_planes("v", vT, SECOND_PAIR, V_CELL)
+        v_planes = load_table("v", vT, V_CELL)
         qm_rows = load_rows("qm", qm[0], QM_CELL)
 
         windows = []
-        for w in range(WINDOWS):
+        for w in range(BLOCKS):
             window = moved_tile("window%d" % w, [P, T], WINDOW_CELL + w)
-            engine = nc.vector if w % 2 == 0 else nc.gpsimd
-            engine.memset(window[:].bitcast(I32), 0)
+            nc.vector.memset(window[:].bitcast(I32), 0)
             windows.append(window)
         minus_gate = held.tile([P, PACK], F32, name="minus_gate")
         nc.vector.tensor_scalar(minus_gate[:], gate[:], -1.0, None, MULT)
@@ -155,6 +156,8 @@ def tile_attend_gat_sig_kv_kernel(tc, qT, kT, vT, doT, rw, qm, dom, offs, out_0,
             for h, slots in enumerate(SLOT_HALVES):
                 nc.vector.tensor_copy(walk_woven(woven[h][:, :, pair]), walk_rows(rows[:, pair, slots]))
 
+        q_woven = [weave_dealt("q%d" % h, q_rows, h, nc.vector.tensor_copy) for h in range(2)]
+        q_mx = [quantise("q%d" % h, q_woven[h], E4M3) for h in range(2)]
         k_rows = held.tile([P, PACK, N], F32, name="k_rows", tag="gathered")
         k_woven = [table_woven("k", h) for h in range(2)]
         gather(k_rows, k_planes, 0)
@@ -163,63 +166,64 @@ def tile_attend_gat_sig_kv_kernel(tc, qT, kT, vT, doT, rw, qm, dom, offs, out_0,
         gather(k_rows, k_planes, 2)
         gather_last(k_rows, k_planes)
         weave_pair(k_woven, k_rows, SECOND_PAIR)
-        k_mx = (new_tile("k_words", [P, N], U32), new_tile("k_scales", [P, N], U8), E4M3)
-        for h, slots in enumerate(SLOT_HALVES):
-            nc.vector.quantize_mx(
-                out=k_mx[0][:, slots].bitcast(E4M3),
-                scales=k_mx[1][:, slots],
-                in_=k_woven[h][:].rearrange("p c t -> p (c t)"),
-            )
-        q_woven = [weave_dealt("q%d" % h, q_rows, h, nc.vector.tensor_copy) for h in range(2)]
-        q_mx = [quantise("q%d" % h, q_woven[h], E4M3) for h in range(2)]
-        scores = [product("score%d" % j, "front", q_mx, j, k_mx) for j in range(PACK)]
+        k_mx = [quantise("k%d" % h, k_woven[h], E4M3) for h in range(2)]
 
-        prob = held.tile([P, PACK, N], F32, name="prob")
+        def paired_product(name, tag, stationary, moving):
+            bank = psum.tile([P, HALF_BLOCKS, N // 2], F32, name=name, tag=tag)
+            for within in range(HALF_BLOCKS):
+                multiply(bank[:, within, :], stationary, within, moving, slice(0, N // 2))
+            return bank
+
+        prob = [new_tile("prob%d" % h, [P, PACK, N // 2], F32) for h in range(2)]
         minus_pw = [new_tile("minus_pw%d" % h, [P, PACK, N // 2], F32) for h in range(2)]
-        for j in range(PACK):
-            nc.scalar.activation(prob[:, j, :], scores[j][:], ACT.Sigmoid)
-        pw_woven = [new_woven("pw%d" % h, N // 2) for h in range(2)]
-        for h, slots in enumerate(SLOT_HALVES):
-            for j in range(PACK):
-                nc.scalar.activation(
-                    minus_pw[h][:, j, :], prob[:, j, slots], ACT.Copy, scale=minus_gate[:, j : j + 1]
-                )
-            nc.scalar.activation(walk_woven(pw_woven[h][:]), walk_rows(minus_pw[h][:]), ACT.Copy, scale=-1.0)
-        dom_woven = [weave_half("dom%d" % h, dom_rows, h, nc.vector.tensor_copy) for h in range(2)]
-        dom_mx = [quantise("dom%d" % h, dom_woven[h], E5M2) for h in range(2)]
-        dv = []
         for h in range(2):
-            pw_mx = quantise("pw%d" % h, pw_woven[h], E4M3)
-            banks = [psum.tile([P, HALF_BLOCKS, N // 2], F32, name="dv%d%d" % (h, g), tag="back") for g in range(2)]
-            for m in range(BLOCKS):
-                g, within = divmod(m, HALF_BLOCKS)
-                multiply(banks[g][:, within, :], dom_mx[g], within, pw_mx, slice(0, N // 2))
-            dv.append(banks)
-        for m in range(BLOCKS):
+            for g, pair in enumerate((FIRST_PAIR, SECOND_PAIR)):
+                score = paired_product("score%d%d" % (h, g), "front", q_mx[g], k_mx[h])
+                nc.scalar.activation(prob[h][:, pair, :], score[:], ACT.Sigmoid)
+            for j in range(PACK):
+                nc.scalar.activation(minus_pw[h][:, j, :], prob[h][:, j, :], ACT.Copy, scale=minus_gate[:, j : j + 1])
+
+        dom_mx = [quantise("dom0", weave_half("dom0", dom_rows, 0, nc.vector.tensor_copy), E5M2)]
+        late_dom = weave_half("dom1", dom_rows, 1, nc.scalar.copy)
+        slopes = [new_tile("slope%d" % h, [P, PACK, N // 2], F32) for h in range(2)]
+        pw_mx = []
+        dv = [[], []]
+        for h in range(2):
+            pw_woven = new_woven("pw%d" % h, N // 2)
+            nc.vector.tensor_scalar(walk_woven(pw_woven[:]), walk_rows(minus_pw[h][:]), -1.0, None, MULT)
+            pw_mx.append(quantise("pw%d" % h, pw_woven, E4M3))
+            dv[0].append(paired_product("dv0%d" % h, "back", dom_mx[0], pw_mx[h]))
+            for pair in (FIRST_PAIR, SECOND_PAIR):
+                nc.vector.scalar_tensor_tensor(
+                    slopes[h][:, pair, :], prob[h][:, pair, :], 1.0, minus_pw[h][:, pair, :], SUBTRACT, MULT
+                )
+        dom_mx.append(quantise("dom1", late_dom, E5M2))
+        dv[1].extend(paired_product("dv1%d" % h, "back", dom_mx[1], pw_mx[h]) for h in range(2))
+
+        def put_dv(m):
             halves = [new_tile("dv%d_staged%d" % (m, h), [P, N // 2], F32) for h in range(2)]
             for h in range(2):
-                nc.scalar.copy(halves[h][:], dv[h][m // HALF_BLOCKS][:, m % HALF_BLOCKS, :])
+                nc.scalar.copy(halves[h][:], dv[m // HALF_BLOCKS][h][:, m % HALF_BLOCKS, :])
             for h, slots in enumerate(SLOT_HALVES):
                 nc.scalar.activation(windows[m][:].indirect(listed(slots)), halves[h][:], ACT.Copy)
             nc.sync.dma_start(out_1[m * P : (m + 1) * P, :], windows[m][:])
 
+        put_dv(0)
+        do_woven = [weave_dealt("do%d" % h, do_rows, h, nc.scalar.copy) for h in range(2)]
+        for m in range(1, BLOCKS):
+            put_dv(m)
+
         v_rows = held.tile([P, PACK, N], F32, name="v_rows", tag="gathered")
         v_woven = [table_woven("v", h) for h in range(2)]
-        do_woven = [weave_dealt("do%d" % h, do_rows, h, nc.vector.tensor_copy) for h in range(2)]
-        do_mx = [quantise("do%d" % h, do_woven[h], E5M2) for h in range(2)]
         gather(v_rows, v_planes, 0)
         gather(v_rows, v_planes, 1)
         weave_pair(v_woven, v_rows, FIRST_PAIR)
         gather(v_rows, v_planes, 2)
-        slopes = [new_tile("slope%d" % h, [P, PACK, N // 2], F32) for h in range(2)]
-        for h, slots in enumerate(SLOT_HALVES):
-            for pair in (FIRST_PAIR, SECOND_PAIR):
-                nc.vector.scalar_tensor_tensor(
-                    slopes[h][:, pair, :], prob[:, pair, slots], 1.0, minus_pw[h][:, pair, :], SUBTRACT, MULT
-                )
+        do_mx = [quantise("do%d" % h, do_woven[h], E5M2) for h in range(2)]
         gather_last(v_rows, v_planes)
         weave_pair(v_woven, v_rows, SECOND_PAIR)
         v_mx = [quantise("v%d" % h, v_woven[h], E4M3) for h in range(2)]
+
 
         def weave_qm(m, copy):
             woven = new_woven("qm%d" % m, P)
@@ -253,7 +257,7 @@ def tile_attend_gat_sig_kv_kernel(tc, qT, kT, vT, doT, rw, qm, dom, offs, out_0,
             nc.scalar.copy(staged[h][:, start : start + part.stop - part.start], bank[:])
 
         def put_dk(m, staged):
-            window = windows[(BLOCKS + m) % WINDOWS]
+            window = windows[m]
             nc.vector.tensor_copy(window[:].indirect(offsets[:]), staged[:])
             nc.sync.dma_start(out_0[m * P : (m + 1) * P, :], window[:])
 
@@ -267,7 +271,7 @@ def tile_attend_gat_sig_kv_kernel(tc, qT, kT, vT, doT, rw, qm, dom, offs, out_0,
         form_ds(LAST)
         finish_part(1, qm_mx)
         finish_part(2, qm_mx)
-        window = windows[BLOCKS]
+        window = windows[0]
         nc.vector.tensor_copy(window[:].indirect(listed(SLOT_HALVES[0])), staged[0][:])
         qm_mx = quantise("qm1", qm_woven, E4M3, AT_DK_FIRST)
         nc.vector.tensor_copy(window[:].indirect(listed(SLOT_HALVES[1])), staged[1][:])

@@ -115,10 +115,20 @@ def tile_attend_gat_sig_kv_kernel(tc, qT, kT, vT, doT, rw, qm, dom, offs, out_0,
         def walk_rows(rows):
             return rows.rearrange("p t (c i) -> p c t i", i=RUN)
 
+        def weave_block(woven, rows, m, copy):
+            copy(
+                woven.rearrange("p (a i b) t -> p a b t i", i=RUN, b=PACK),
+                rows[:, :, m * P : (m + 1) * P].rearrange("p t (b a i) -> p a b t i", i=RUN, b=PACK),
+            )
+
         def weave_half(name, rows, h, copy, at=None):
             woven = new_woven(name, HALF, at)
-            copy(walk_woven(woven[:]), walk_rows(rows[:, :, h * HALF : (h + 1) * HALF]))
+            for within in range(HALF_BLOCKS):
+                weave_block(woven[:, within * P : (within + 1) * P, :], rows, h * HALF_BLOCKS + within, copy)
             return woven
+
+        def store(out, m, window):
+            nc.sync.dma_start(out[m * P : (m + 1) * P, :].rearrange("(b a) c -> a b c", b=PACK), window[:])
 
         def multiply(out, stationary, m, moving, slots):
             cols = slice(m * P, (m + 1) * P)
@@ -206,7 +216,7 @@ def tile_attend_gat_sig_kv_kernel(tc, qT, kT, vT, doT, rw, qm, dom, offs, out_0,
                 nc.scalar.copy(halves[h][:], dv[m // HALF_BLOCKS][h][:, m % HALF_BLOCKS, :])
             for h, slots in enumerate(SLOT_HALVES):
                 nc.scalar.activation(windows[m][:].indirect(listed(slots)), halves[h][:], ACT.Copy)
-            nc.sync.dma_start(out_1[m * P : (m + 1) * P, :], windows[m][:])
+            store(out_1, m, windows[m])
 
         put_dv(0)
         do_woven = [weave_dealt("do%d" % h, do_rows, h, nc.scalar.copy) for h in range(2)]
@@ -227,7 +237,7 @@ def tile_attend_gat_sig_kv_kernel(tc, qT, kT, vT, doT, rw, qm, dom, offs, out_0,
 
         def weave_qm(m, copy):
             woven = new_woven("qm%d" % m, P)
-            copy(walk_woven(woven[:]), walk_rows(qm_rows[:, :, m * P : (m + 1) * P]))
+            weave_block(woven[:], qm_rows, m, copy)
             return woven
 
         ds_parts = [slice(0, 2 * P), slice(2 * P, 3 * P), slice(3 * P, N)]
@@ -259,7 +269,7 @@ def tile_attend_gat_sig_kv_kernel(tc, qT, kT, vT, doT, rw, qm, dom, offs, out_0,
         def put_dk(m, staged):
             window = windows[m]
             nc.vector.tensor_copy(window[:].indirect(offsets[:]), staged[:])
-            nc.sync.dma_start(out_0[m * P : (m + 1) * P, :], window[:])
+            store(out_0, m, window)
 
         qm_woven = weave_qm(0, nc.vector.tensor_copy)
         form_ds(0)
@@ -275,7 +285,7 @@ def tile_attend_gat_sig_kv_kernel(tc, qT, kT, vT, doT, rw, qm, dom, offs, out_0,
         nc.vector.tensor_copy(window[:].indirect(listed(SLOT_HALVES[0])), staged[0][:])
         qm_mx = quantise("qm1", qm_woven, E4M3, AT_DK_FIRST)
         nc.vector.tensor_copy(window[:].indirect(listed(SLOT_HALVES[1])), staged[1][:])
-        nc.sync.dma_start(out_0[:P, :], window[:])
+        store(out_0, 0, window)
         qm_late = weave_half("qm_late", qm_rows, 1, nc.vector.tensor_copy, AT_DK_SECOND)
         dk1 = stage("dk1", product("dk1", "front", [qm_mx], 0, ds_mx))
         qm_late_mx = quantise("qm_late", qm_late, E4M3)

@@ -32,6 +32,7 @@ SLOT_HALVES = [slice(0, N // 2), slice(N // 2, N)]
 FIRST_PAIR, SECOND_PAIR = slice(0, 2), slice(2, PACK)
 TABLE_LOADS = (FIRST_PAIR, slice(2, LAST), slice(LAST, PACK))
 RUN = 2
+QUADRANT = 32
 AT_DK_FIRST = 0
 AT_DK_SECOND = N * 2
 
@@ -69,8 +70,9 @@ def tile_attend_gat_sig_kv_kernel(tc, qT, kT, vT, doT, rw, qm, dom, offs, out_0,
         q_rows = load_rows("q", qT[0], Q_CELL)
         offsets = held.tile([P, N // BAND], U16, name="offsets")
         nc.sync.dma_start(offsets[:], offs)
-        gate = held.tile([P, PACK], F32, name="gate")
-        nc.sync.dma_start(gate[:], rw[0].rearrange("(p j) o -> p (j o)", j=PACK))
+        gate_rows = new_tile("gate_rows", [P, P], F32)
+        nc.vector.memset(gate_rows[:], 0.0)
+        nc.sync.dma_start(gate_rows[0:P:QUADRANT, :], rw[0].rearrange("(g c) o -> g (c o)", c=P))
         k_planes = load_table("k", kT, K_CELL)
         dom_rows = load_rows("dom", dom[0], DOM_CELL)
         do_rows = load_rows("do", doT[0], DO_CELL)
@@ -82,8 +84,6 @@ def tile_attend_gat_sig_kv_kernel(tc, qT, kT, vT, doT, rw, qm, dom, offs, out_0,
             window = moved_tile("window%d" % w, [P, T], WINDOW_CELL + w)
             nc.vector.memset(window[:].bitcast(I32), 0)
             windows.append(window)
-        minus_gate = held.tile([P, PACK], F32, name="minus_gate")
-        nc.vector.tensor_scalar(minus_gate[:], gate[:], -1.0, None, MULT)
 
         def new_woven(name, width=N, at=None):
             return new_tile(name + "_woven", [P, width, PACK], BF16, at)
@@ -168,6 +168,13 @@ def tile_attend_gat_sig_kv_kernel(tc, qT, kT, vT, doT, rw, qm, dom, offs, out_0,
 
         q_woven = [weave_dealt("q%d" % h, q_rows, h, nc.vector.tensor_copy) for h in range(2)]
         q_mx = [quantise("q%d" % h, q_woven[h], E4M3) for h in range(2)]
+        gate_dealt = new_tile("gate_dealt", [P, PACK, QUADRANT], F32)
+        nc.vector.tensor_copy(gate_dealt[:], gate_rows[:].rearrange("p (i j) -> p j i", j=PACK))
+        gate_turned = new_tile("gate_turned", [P, PACK, QUADRANT], F32)
+        flat = "p j i -> p (j i)"
+        nc.vector.transpose(gate_turned[:].rearrange(flat), gate_dealt[:].rearrange(flat))
+        minus_gate = held.tile([P, PACK], F32, name="minus_gate")
+        nc.vector.tensor_scalar(minus_gate[:], gate_turned[:, :, 0], -1.0, None, MULT)
         k_rows = held.tile([P, PACK, N], F32, name="k_rows", tag="gathered")
         k_woven = [table_woven("k", h) for h in range(2)]
         gather(k_rows, k_planes, 0)

@@ -30,7 +30,8 @@ HALF = DV // 2
 HALF_BLOCKS = HALF // P
 SLOT_HALVES = [slice(0, N // 2), slice(N // 2, N)]
 FIRST_PAIR, SECOND_PAIR = slice(0, 2), slice(2, PACK)
-TABLE_LOADS = (FIRST_PAIR, slice(2, LAST), slice(LAST, PACK))
+KEY_LOADS = [slice(t, t + 1) for t in range(PACK)]
+VALUE_LOADS = [FIRST_PAIR, slice(2, LAST), slice(LAST, PACK)]
 RUN = 2
 QUADRANT = 32
 AT_DK_FIRST = 0
@@ -64,8 +65,8 @@ def tile_attend_gat_sig_kv_kernel(tc, qT, kT, vT, doT, rw, qm, dom, offs, out_0,
             nc.sync.dma_start(planes[:], table.rearrange("(p t) c -> p t c", t=PACK)[:, places, :])
             return [planes[:, t, :] for t in range(count)]
 
-        def load_table(name, table, cell):
-            return [plane for places in TABLE_LOADS for plane in load_planes(name, table, places, cell)]
+        def load_table(name, table, cell, loads):
+            return [plane for places in loads for plane in load_planes(name, table, places, cell)]
 
         q_rows = load_rows("q", qT[0], Q_CELL)
         offsets = held.tile([P, N // BAND], U16, name="offsets")
@@ -73,10 +74,10 @@ def tile_attend_gat_sig_kv_kernel(tc, qT, kT, vT, doT, rw, qm, dom, offs, out_0,
         gate_rows = new_tile("gate_rows", [P, P], F32)
         nc.vector.memset(gate_rows[:], 0.0)
         nc.sync.dma_start(gate_rows[0:P:QUADRANT, :], rw[0].rearrange("(g c) o -> g (c o)", c=P))
-        k_planes = load_table("k", kT, K_CELL)
+        k_planes = load_table("k", kT, K_CELL, KEY_LOADS)
         dom_rows = load_rows("dom", dom[0], DOM_CELL)
         do_rows = load_rows("do", doT[0], DO_CELL)
-        v_planes = load_table("v", vT, V_CELL)
+        v_planes = load_table("v", vT, V_CELL, VALUE_LOADS)
         qm_rows = load_rows("qm", qm[0], QM_CELL)
 
         windows = []

from contextlib import ExitStack

import concourse.mybir as mybir

N, T, D, DV, R = 512, 2048, 512, 512, 512
FLOPS = 2 * R * N * (2 * D + 2 * DV)

F32 = mybir.dt.float32
BF16 = mybir.dt.bfloat16
I32 = mybir.dt.int32
U32 = mybir.dt.uint32
U16 = mybir.dt.uint16
U8 = mybir.dt.uint8
E4M3 = mybir.dt.float8_e4m3fn_x4
E5M2 = mybir.dt.float8_e5m2_x4
ACT = mybir.ActivationFunctionType
MULT = mybir.AluOpType.mult
SUBTRACT = mybir.AluOpType.subtract

P = 128
PACK = 4
LAST = PACK - 1
BAND = 16
ALIGN = 64
DMA_ALIGN = 4096
CELL = T * 4
K_CELL, V_CELL, Q_CELL, DOM_CELL, DO_CELL, QM_CELL, WINDOW_CELL = 0, 4, 8, 9, 10, 11, 12
BLOCKS = DV // P
HALF = DV // 2
HALF_BLOCKS = HALF // P
SLOT_HALVES = [slice(0, N // 2), slice(N // 2, N)]
FIRST_PAIR, SECOND_PAIR = slice(0, 2), slice(2, PACK)
KEY_LOADS = [slice(t, t + 1) for t in range(PACK)]
VALUE_LOADS = [FIRST_PAIR, slice(2, LAST), slice(LAST, PACK)]
RUN = 2
QUADRANT = 32
AT_DK_FIRST = 0
AT_DK_SECOND = N * 2


def tile_attend_gat_sig_kv_kernel(tc, qT, kT, vT, doT, rw, qm, dom, offs, out_0, out_1):
    nc = tc.nc
    with ExitStack() as ctx:
        moved = ctx.enter_context(tc.tile_pool(name="moved", bufs=1))
        held = ctx.enter_context(tc.tile_pool(name="held", bufs=1))
        shared = ctx.enter_context(tc.tile_pool(name="shared", bufs=1))
        psum = ctx.enter_context(tc.psum_pool(name="psum", bufs=PACK))

        def new_tile(name, shape, dtype, at=None):
            if at is None:
                return held.tile(shape, dtype, name=name, align_bytes=ALIGN)
            return shared.tile(shape, dtype, name=name, offset=at, align_bytes=ALIGN)

        def moved_tile(name, shape, cell):
            return moved.tile(shape, F32, name=name, offset=cell * CELL, align_bytes=DMA_ALIGN)

        def load_rows(name, src, cell):
            rows = moved_tile(name + "_rows", [P, PACK, src.shape[1]], cell)
            nc.sync.dma_start(rows[:], src.rearrange("(p t) c -> p t c", t=PACK))
            return rows

        def load_planes(name, table, places, cell):
            count = places.stop - places.start
            planes = moved_tile("%s_planes%d" % (name, places.start), [P, count, T], cell + places.start)
            nc.sync.dma_start(planes[:], table.rearrange("(p t) c -> p t c", t=PACK)[:, places, :])
            return [planes[:, t, :] for t in range(count)]

        def load_table(name, table, cell, loads):
            return [plane for places in loads for plane in load_planes(name, table, places, cell)]

        q_rows = load_rows("q", qT[0], Q_CELL)
        offsets = held.tile([P, N // BAND], U16, name="offsets")
        nc.sync.dma_start(offsets[:], offs)
        gate_rows = new_tile("gate_rows", [P, P], F32)
        nc.vector.memset(gate_rows[:], 0.0)
        nc.sync.dma_start(gate_rows[0:P:QUADRANT, :], rw[0].rearrange("(g c) o -> g (c o)", c=P))
        k_planes = load_table("k", kT, K_CELL, KEY_LOADS)
        dom_rows = load_rows("dom", dom[0], DOM_CELL)
        do_rows = load_rows("do", doT[0], DO_CELL)
        v_planes = load_table("v", vT, V_CELL, VALUE_LOADS)
        qm_rows = load_rows("qm", qm[0], QM_CELL)

        windows = []
        for w in range(BLOCKS):
            window = moved_tile("window%d" % w, [P, T], WINDOW_CELL + w)
            nc.vector.memset(window[:].bitcast(I32), 0)
            windows.append(window)

        def new_woven(name, width=N, at=None):
            return new_tile(name + "_woven", [P, width, PACK], BF16, at)

        def table_woven(name, h):
            shape = [P, N // 2, PACK]
            return held.tile(shape, BF16, name="%s%d_woven" % (name, h), tag="table%d" % h, align_bytes=ALIGN)

        def quantise(name, woven, fmt, at=None):
            width = woven.shape[1]
            words = new_tile(name + "_words", [P, width], U32, at)
            scales = new_tile(name + "_scales", [P, width], U8, None if at is None else at + PACK * width)
            flat = woven[:].rearrange("p c t -> p (c t)")
            nc.vector.quantize_mx(out=words[:].bitcast(fmt), scales=scales[:], in_=flat)
            return words, scales, fmt

        def weave_dealt(name, rows, h, copy):
            woven = new_woven(name, HALF)
            first = h * HALF_BLOCKS
            copy(
                woven[:].rearrange("p (j s) t -> p s t j", j=HALF_BLOCKS),
                rows[:].rearrange("p t (s j) -> p s t j", j=PACK)[:, :, :, first : first + HALF_BLOCKS],
            )
            return woven

        def walk_woven(woven):
            return woven.rearrange("p (c i) t -> p c t i", i=RUN)

        def walk_rows(rows):
            return rows.rearrange("p t (c i) -> p c t i", i=RUN)

        def weave_block(woven, rows, m, copy):
            copy(
                woven.rearrange("p (a i b) t -> p a b t i", i=RUN, b=PACK),
                rows[:, :, m * P : (m + 1) * P].rearrange("p t (b a i) -> p a b t i", i=RUN, b=PACK),
            )

        def weave_half(name, rows, h, copy, at=None):
            woven = new_woven(name, HALF, at)
            for within in range(HALF_BLOCKS):
                weave_block(woven[:, within * P : (within + 1) * P, :], rows, h * HALF_BLOCKS + within, copy)
            return woven

        def store(out, m, window):
            nc.sync.dma_start(out[m * P : (m + 1) * P, :].rearrange("(b a) c -> a b c", b=PACK), window[:])

        def multiply(out, stationary, m, moving, slots):
            cols = slice(m * P, (m + 1) * P)
            nc.tensor.matmul_mx(
                out=out,
                lhsT=stationary[0][:, cols].bitcast(stationary[2]),
                lhsT_scale=stationary[1][:, cols],
                rhs=moving[0][:, slots].bitcast(moving[2]),
                rhs_scale=moving[1][:, slots],
                start=True,
                stop=True,
            )

        def product(name, tag, halves, m, moving):
            bank = psum.tile([P, N], F32, name=name, tag=tag)
            multiply(bank[:], halves[m // HALF_BLOCKS], m % HALF_BLOCKS, moving, slice(0, N))
            return bank

        def listed(slots):
            return offsets[:, slots.start // BAND : slots.stop // BAND]

        def stage(name, bank):
            staged = new_tile(name + "_staged", [P, N], F32)
            nc.scalar.copy(staged[:], bank[:])
            return staged

        def gather(rows, planes, t):
            nc.vector.tensor_copy(rows[:, t, :], planes[t].indirect(offsets[:]))

        def gather_last(rows, planes):
            for slots in SLOT_HALVES:
                nc.vector.tensor_copy(rows[:, LAST, slots], planes[LAST].indirect(listed(slots)))

        def weave_pair(woven, rows, pair):
            for h, slots in enumerate(SLOT_HALVES):
                nc.vector.tensor_copy(walk_woven(woven[h][:, :, pair]), walk_rows(rows[:, pair, slots]))

        q_woven = [weave_dealt("q%d" % h, q_rows, h, nc.vector.tensor_copy) for h in range(2)]
        q_mx = [quantise("q%d" % h, q_woven[h], E4M3) for h in range(2)]
        gate_dealt = new_tile("gate_dealt", [P, PACK, QUADRANT], F32)
        nc.vector.tensor_copy(gate_dealt[:], gate_rows[:].rearrange("p (i j) -> p j i", j=PACK))
        gate_turned = new_tile("gate_turned", [P, PACK, QUADRANT], F32)
        flat = "p j i -> p (j i)"
        nc.vector.transpose(gate_turned[:].rearrange(flat), gate_dealt[:].rearrange(flat))
        minus_gate = held.tile([P, PACK], F32, name="minus_gate")
        nc.vector.tensor_scalar(minus_gate[:], gate_turned[:, :, 0], -1.0, None, MULT)
        k_rows = held.tile([P, PACK, N], F32, name="k_rows", tag="gathered")
        k_woven = [table_woven("k", h) for h in range(2)]
        gather(k_rows, k_planes, 0)
        gather(k_rows, k_planes, 1)
        weave_pair(k_woven, k_rows, FIRST_PAIR)
        gather(k_rows, k_planes, 2)
        gather_last(k_rows, k_planes)
        weave_pair(k_woven, k_rows, SECOND_PAIR)
        k_mx = [quantise("k%d" % h, k_woven[h], E4M3) for h in range(2)]

        def paired_product(name, tag, stationary, moving):
            bank = psum.tile([P, HALF_BLOCKS, N // 2], F32, name=name, tag=tag)
            for within in range(HALF_BLOCKS):
                multiply(bank[:, within, :], stationary, within, moving, slice(0, N // 2))
            return bank

        prob = [new_tile("prob%d" % h, [P, PACK, N // 2], F32) for h in range(2)]
        minus_pw = [new_tile("minus_pw%d" % h, [P, PACK, N // 2], F32) for h in range(2)]
        for h in range(2):
            for g, pair in enumerate((FIRST_PAIR, SECOND_PAIR)):
                score = paired_product("score%d%d" % (h, g), "front", q_mx[g], k_mx[h])
                nc.scalar.activation(prob[h][:, pair, :], score[:], ACT.Sigmoid)
            for j in range(PACK):
                nc.scalar.activation(minus_pw[h][:, j, :], prob[h][:, j, :], ACT.Copy, scale=minus_gate[:, j : j + 1])

        dom_mx = [quantise("dom0", weave_half("dom0", dom_rows, 0, nc.vector.tensor_copy), E5M2)]
        late_dom = weave_half("dom1", dom_rows, 1, nc.scalar.copy)
        slopes = [new_tile("slope%d" % h, [P, PACK, N // 2], F32) for h in range(2)]
        pw_mx = []
        dv = [[], []]
        for h in range(2):
            pw_woven = new_woven("pw%d" % h, N // 2)
            nc.vector.tensor_scalar(walk_woven(pw_woven[:]), walk_rows(minus_pw[h][:]), -1.0, None, MULT)
            pw_mx.append(quantise("pw%d" % h, pw_woven, E4M3))
            dv[0].append(paired_product("dv0%d" % h, "back", dom_mx[0], pw_mx[h]))
            for pair in (FIRST_PAIR, SECOND_PAIR):
                nc.vector.scalar_tensor_tensor(
                    slopes[h][:, pair, :], prob[h][:, pair, :], 1.0, minus_pw[h][:, pair, :], SUBTRACT, MULT
                )
        dom_mx.append(quantise("dom1", late_dom, E5M2))
        dv[1].extend(paired_product("dv1%d" % h, "back", dom_mx[1], pw_mx[h]) for h in range(2))

        def put_dv(m):
            halves = [new_tile("dv%d_staged%d" % (m, h), [P, N // 2], F32) for h in range(2)]
            for h in range(2):
                nc.scalar.copy(halves[h][:], dv[m // HALF_BLOCKS][h][:, m % HALF_BLOCKS, :])
            for h, slots in enumerate(SLOT_HALVES):
                nc.scalar.activation(windows[m][:].indirect(listed(slots)), halves[h][:], ACT.Copy)
            store(out_1, m, windows[m])

        put_dv(0)
        do_woven = [weave_dealt("do%d" % h, do_rows, h, nc.scalar.copy) for h in range(2)]
        for m in range(1, BLOCKS):
            put_dv(m)

        v_rows = held.tile([P, PACK, N], F32, name="v_rows", tag="gathered")
        v_woven = [table_woven("v", h) for h in range(2)]
        gather(v_rows, v_planes, 0)
        gather(v_rows, v_planes, 1)
        weave_pair(v_woven, v_rows, FIRST_PAIR)
        gather(v_rows, v_planes, 2)
        do_mx = [quantise("do%d" % h, do_woven[h], E5M2) for h in range(2)]
        gather_last(v_rows, v_planes)
        weave_pair(v_woven, v_rows, SECOND_PAIR)
        v_mx = [quantise("v%d" % h, v_woven[h], E4M3) for h in range(2)]


        def weave_qm(m, copy):
            woven = new_woven("qm%d" % m, P)
            weave_block(woven[:], qm_rows, m, copy)
            return woven

        ds_parts = [slice(0, 2 * P), slice(2 * P, 3 * P), slice(3 * P, N)]
        ds_woven = [new_woven("ds%d" % g, part.stop - part.start) for g, part in enumerate(ds_parts)]
        ds_mx = (new_tile("ds_words", [P, N], U32), new_tile("ds_scales", [P, N], U8), E5M2)

        def form_ds(b):
            h, within = b // 2, slice((b % 2) * P, (b % 2 + 1) * P)
            woven = ds_woven[0][:, within, :] if h == 0 else ds_woven[b - 1][:]
            dp = psum.tile([P, PACK, P], F32, name="dp%d" % b, tag="front")
            for j in range(PACK):
                multiply(dp[:, j, :], do_mx[j // HALF_BLOCKS], j % HALF_BLOCKS, v_mx[h], within)
            nc.vector.tensor_tensor(walk_woven(woven), walk_rows(dp[:]), walk_rows(slopes[h][:, :, within]), MULT)

        staged = [new_tile("dk0_staged%d" % h, [P, N // 2], F32, at) for h, at in enumerate((AT_DK_FIRST, AT_DK_SECOND))]

        def finish_part(g, stationary):
            part = ds_parts[g]
            nc.vector.quantize_mx(
                out=ds_mx[0][:, part].bitcast(E5M2),
                scales=ds_mx[1][:, part],
                in_=ds_woven[g][:].rearrange("p c t -> p (c t)"),
            )
            bank = psum.tile([P, part.stop - part.start], F32, name="dk0_%d" % g, tag="back")
            multiply(bank[:], stationary, 0, ds_mx, part)
            h, start = divmod(part.start, N // 2)
            nc.scalar.copy(staged[h][:, start : start + part.stop - part.start], bank[:])

        def put_dk(m, staged):
            window = windows[m]
            nc.vector.tensor_copy(window[:].indirect(offsets[:]), staged[:])
            store(out_0, m, window)

        qm_woven = weave_qm(0, nc.vector.tensor_copy)
        form_ds(0)
        qm_mx = quantise("qm0", qm_woven, E4M3)
        qm_woven = weave_qm(1, nc.scalar.copy)
        form_ds(1)
        form_ds(2)
        finish_part(0, qm_mx)
        form_ds(LAST)
        finish_part(1, qm_mx)
        finish_part(2, qm_mx)
        window = windows[0]
        nc.vector.tensor_copy(window[:].indirect(listed(SLOT_HALVES[0])), staged[0][:])
        qm_mx = quantise("qm1", qm_woven, E4M3, AT_DK_FIRST)
        nc.vector.tensor_copy(window[:].indirect(listed(SLOT_HALVES[1])), staged[1][:])
        store(out_0, 0, window)
        qm_late = weave_half("qm_late", qm_rows, 1, nc.vector.tensor_copy, AT_DK_SECOND)
        dk1 = stage("dk1", product("dk1", "front", [qm_mx], 0, ds_mx))
        qm_late_mx = quantise("qm_late", qm_late, E4M3)
        put_dk(1, dk1)
        for m in range(HALF_BLOCKS, BLOCKS):
            put_dk(m, stage("dk%d" % m, product("dk%d" % m, "front", [None, qm_late_mx], m, ds_mx)))
